import numpy as np
import ml_dtypes


def mxq(x, axis, fmt="e4m3"):
    dtype, down = {"e4m3": (ml_dtypes.float8_e4m3fn, 7), "e5m2": (ml_dtypes.float8_e5m2, 14)}[fmt]
    v = np.moveaxis(np.asarray(x, np.float32).astype(ml_dtypes.bfloat16).astype(np.float64), axis, -1)
    blocks = v.reshape(v.shape[:-1] + (-1, 32))
    amax = np.abs(blocks).max(-1, keepdims=True)
    byte = np.maximum(np.where(amax > 0, np.frexp(amax)[1] - 1 + 127, 0) - down, 1)
    scale = np.exp2(byte - 127.0)
    codes = (blocks / scale).astype(np.float32).astype(dtype).astype(np.float64)
    return np.moveaxis((codes * scale).reshape(v.shape), -1, axis)


WIDE = False


def mx_kscale(k):
    if not WIDE:
        return np.ones(k)
    levels = np.array([10, -10, 5, -5, 0])
    if k % 512:
        return np.exp2(np.random.permutation(np.resize(levels, k // 32))).repeat(32)
    a = np.empty((k // 512, 16))
    for p in range(k // 512):
        a[p, :8] = np.random.permutation(np.resize(levels, 8))
        for g in range(8):
            far = levels[np.abs(levels - a[p, g]) >= 10]
            a[p, g + 8] = far[np.random.randint(len(far))]
    return np.exp2(a.ravel()).repeat(32)


def f64(x):
    return np.asarray(x).astype(np.float64)


def striped(idx):
    return np.tile(idx.reshape(-1, 16).T, (8, 1)).astype(np.uint16)


def unstriped(offs):
    return offs[:16].T.reshape(-1).astype(np.int64)


E2M1 = np.array([0.0, 0.5, 1.0, 1.5, 2.0, 3.0, 4.0, 6.0, -0.0, -0.5, -1.0, -1.5, -2.0, -3.0, -4.0, -6.0])


def pack_weight(w, fmt):
    k, n = w.shape
    w = f64(np.asarray(w, np.float32).astype(ml_dtypes.bfloat16)).reshape(k // 32, 32, n)
    amax = np.abs(w).max(1)
    if fmt == "e4m3":
        byte = np.frexp(amax)[1] - 1 + 127 - 7
    else:
        mant, ex = np.frexp(amax / 6.0)
        byte = np.where(mant > 0.5, ex, ex - 1) + 127
    byte = np.clip(np.where(amax > 0, byte, 1), 1, 254)
    scaled = (w * np.exp2(127.0 - byte)[:, None, :]).reshape(k, n).astype(np.float32)
    by_word = np.ascontiguousarray(scaled.reshape(k // 512, 128, 4, n).transpose(0, 1, 3, 2))
    if fmt == "e4m3":
        words = by_word.astype(ml_dtypes.float8_e4m3fn).view(np.uint8)
    else:
        c = by_word.astype(ml_dtypes.float4_e2m1fn).view(np.uint8) & 0xF
        words = (c[..., 0::2] | (c[..., 1::2] << 4)).reshape(k // 512, 128, 2 * n)
    return np.ascontiguousarray(words), np.ascontiguousarray(byte.astype(np.uint8).reshape(k // 512, 16, n))


def unpack_weight(words, scales, fmt):
    g, _, n = scales.shape
    words = np.ascontiguousarray(words).reshape(g, 128, n, -1)
    if fmt == "e4m3":
        vals = words.view(ml_dtypes.float8_e4m3fn).astype(np.float64)
    else:
        nib = np.empty((g, 128, n, 4), np.uint8)
        nib[..., 0::2] = words & 0xF
        nib[..., 1::2] = words >> 4
        vals = E2M1[nib]
    vals = vals * np.repeat(np.exp2(scales.astype(np.float64) - 127.0), 8, axis=1)[..., None]
    return vals.transpose(0, 1, 3, 2).reshape(g * 512, n)


def planes(y):
    n, m = y.shape
    v = y.astype(np.float32).astype(ml_dtypes.bfloat16).astype(np.float64).reshape(n // 32, 32, m)
    top = np.abs(v).max(1)
    byte = np.clip(np.where(top > 0, np.frexp(top)[1] - 1 + 127 - 7, 1), 1, 254)
    codes = (v * np.exp2(127.0 - byte)[:, None, :]).reshape(n, m).astype(np.float32).astype(ml_dtypes.float8_e4m3fn).view(np.uint8)
    words = codes.reshape(n // 512, 128, 4, m).transpose(0, 1, 3, 2)
    return np.ascontiguousarray(words), np.ascontiguousarray(byte.astype(np.uint8).reshape(n // 512, 16, m))


def gelu(v):
    return 0.5 * v * (1.0 + np.tanh(np.sqrt(2.0 / np.pi) * (v + 0.044715 * v**3)))


K, T, E, C, H, N = 1024, 512, 4, 256, 512, 512


def by_expert(wq, xq):
    return np.concatenate([wq[e].T @ xq[:, e * C:(e + 1) * C] for e in range(E)], axis=1)


def setup_inputs():
    n = np.random.standard_normal
    s = mx_kscale(K)
    u = mx_kscale(H)
    first = np.random.permutation(np.repeat(np.arange(E), T // E))
    second = (first + 1 + np.random.permutation(np.repeat(np.arange(E - 1), -(-T // (E - 1)))[:T])) % E
    while np.bincount(second, minlength=E).max() != T // E:
        load = np.bincount(second, minlength=E); hi, lo = int(load.argmax()), int(load.argmin())
        t = np.flatnonzero((second == hi) & (first != lo))[0]; second[t] = lo
    slot_token = np.empty(E * C, np.int64); pos = np.empty((2, T), np.int64); fill = np.zeros(E, np.int64)
    place = np.stack([np.random.permutation(C) for _ in range(E)])
    for r, deal in enumerate((first, second)):
        for t in np.random.permutation(T):
            e = deal[t]; j = e * C + place[e, fill[e]]; fill[e] += 1; slot_token[j] = t; pos[r, t] = j
    g = np.random.uniform(0.2, 0.8, T)
    partner = np.concatenate([np.random.permutation(T) for _ in range(-(-E * C // T))])[:E * C]
    x = pack_weight(n((K, T)) * s[:, None], "e4m3")
    w1 = [pack_weight(m, "e2m1") for m in n((E, K, H)) / np.sqrt(K) / s[None, :, None] * u]
    wp = [pack_weight(m, "e2m1") for m in n((E, K, H)) / np.sqrt(K) / s[None, :, None] * u]
    w2 = [pack_weight(m, "e2m1") for m in n((E, H, N)) / np.sqrt(H) / u[None, :, None]]
    return {
        "x_words": x[0],
        "x_scales": x[1],
        "w1_words": np.stack([m[0] for m in w1]),
        "w1_scales": np.stack([m[1] for m in w1]),
        "wp_words": np.stack([m[0] for m in wp]),
        "wp_scales": np.stack([m[1] for m in wp]),
        "w2_words": np.stack([m[0] for m in w2]),
        "w2_scales": np.stack([m[1] for m in w2]),
        "gate": np.stack([np.tile(g, (128, 1)), np.tile(1.0 - g, (128, 1))]).astype(np.float32),
        "offs": striped(slot_token),
        "pos1": striped(pos[0]),
        "pos2": striped(pos[1]),
        "offs2": striped(partner),
    }


def reference(x_words, x_scales, w1_words, w1_scales, wp_words, wp_scales, w2_words, w2_scales, gate, offs, pos1, pos2, offs2):
    w1 = np.stack([unpack_weight(w1_words[e], w1_scales[e], "e2m1") for e in range(E)])
    wp = np.stack([unpack_weight(wp_words[e], wp_scales[e], "e2m1") for e in range(E)])
    w2 = np.stack([unpack_weight(w2_words[e], w2_scales[e], "e2m1") for e in range(E)])
    idx, idx2 = unstriped(offs), unstriped(offs2)
    x = unpack_weight(x_words, x_scales, "e4m3")
    h = gelu(by_expert(w1, x[:, idx]) + by_expert(wp, x[:, idx2]))
    y = by_expert(w2, mxq(h, 0, "e4m3"))
    out = sum(f64(gate[r, :1]) * y[:, unstriped(p)] for r, p in enumerate((pos1, pos2)))
    out_0 = out
    return (out_0,) + planes(out_0)

@@ -1,0 +1,262 @@
+from contextlib import ExitStack
+
+import concourse.mybir as mybir
+from concourse.masks import make_identity
+
+K, T, E, C, H, N = 1024, 512, 4, 256, 512, 512
+S = E * C
+FLOPS = 2 * S * (2 * K * H + H * N)
+
+F32 = mybir.dt.float32
+BF16 = mybir.dt.bfloat16
+I32 = mybir.dt.int32
+U32 = mybir.dt.uint32
+U16 = mybir.dt.uint16
+U8 = mybir.dt.uint8
+FP8X4 = mybir.dt.float8_e4m3fn_x4
+FP4X4 = mybir.dt.float4_e2m1fn_x4
+GELU = mybir.ActivationFunctionType.Gelu_apprx_tanh
+MULT = mybir.AluOpType.mult
+ADD = mybir.AluOpType.add
+
+P = 128
+PASSES = K // 512
+STRIPE = 16
+TOKEN_CHUNKS = ((0, 384), (384, 128))
+
+
+def tile_moe_duo_gelu_kernel(
+    tc, x_words, x_scales, w1_words, w1_scales, wp_words, wp_scales, w2_words, w2_scales,
+    gate, offs, pos1, pos2, offs2, out_0, out_1, out_2,
+):
+    nc = tc.nc
+    with ExitStack() as ctx:
+        keep = ctx.enter_context(tc.tile_pool(name="keep", bufs=1))
+        psum = ctx.enter_context(tc.psum_pool(name="psum", bufs=1))
+
+        def sb(shape, dtype, name, tag=None):
+            return keep.tile(shape, dtype, name=name, tag=tag or name, align_bytes=64)
+
+        def load_list(src, name):
+            tile = keep.tile(list(src.shape), U16, name=name)
+            nc.sync.dma_start(tile[:], src)
+            return tile
+
+        def load_planes(plane, scales):
+            rows = scales.rearrange("e s b c -> b (e s) c").bitcast(I32)
+            for q in range(4):
+                nc.sync.dma_start(plane[32 * q : 32 * q + 4].bitcast(I32), rows[4 * q : 4 * q + 4])
+
+        def load_words(words, e, name):
+            tile = sb([P, words.shape[1], 1024], U8, f"{name}{e}")
+            nc.sync.dma_start(tile[:].bitcast(I32), words[e].rearrange("s p c -> p s c").bitcast(I32))
+            return tile
+
+        xs = sb([P, T], U8, "xs")
+        w1s = sb([P, E * PASSES, H], U8, "w1s")
+        wps = sb([P, E * PASSES, H], U8, "wps")
+        w2s = sb([P, E, N], U8, "w2s")
+        for plane in (xs, w1s, wps, w2s):
+            nc.vector.memset(plane[:].bitcast(I32), 0)
+
+        slot_lists = [load_list(offs, "offs_sb"), load_list(offs2, "offs2_sb")]
+        groups = x_scales.rearrange("s (q r) c -> (s q) r c", r=4).bitcast(I32)
+        xs_i = xs[:].bitcast(I32)
+        nc.sync.dma_start(xs_i[0:16], groups[0:8:2])
+        nc.sync.dma_start(xs_i[32:48], groups[1:8:2])
+        nc.sync.dma_start(xs_i[64:68], groups[2])
+        nc.sync.dma_start(xs_i[96:100], groups[3])
+        xw = []
+        for s in range(PASSES):
+            tile = sb([P, T], I32, f"xw{s}")
+            nc.sync.dma_start(tile[:], x_words[s].rearrange("p t d -> p (t d)").bitcast(I32))
+            xw.append(tile)
+
+        first = [{}, {}]
+        load_planes(w1s, w1_scales)
+        first[0][0] = load_words(w1_words, 0, "w1_")
+        load_planes(wps, wp_scales)
+        first[1][0] = load_words(wp_words, 0, "wp_")
+        first[0][1] = load_words(w1_words, 1, "w1_")
+        first[1][1] = load_words(wp_words, 1, "wp_")
+        w2_raw = sb([P, E, 1024], U8, "w2_raw")
+        nc.sync.dma_start(w2_raw[:].bitcast(I32), w2_words.rearrange("e s p c -> p (e s) c").bitcast(I32))
+        load_planes(w2s, w2_scales)
+        for e in (2, 3):
+            first[0][e] = load_words(w1_words, e, "w1_")
+            first[1][e] = load_words(wp_words, e, "wp_")
+        first_scales = (w1s, wps)
+        token_lists = [load_list(pos1, "pos1_sb"), load_list(pos2, "pos2_sb")]
+        gates = []
+        for r in range(2):
+            tile = sb([P, T], F32, f"gate{r}")
+            nc.sync.dma_start(tile[:], gate[r])
+            gates.append(tile)
+
+        ident = sb([P, P], F32, "ident")
+        make_identity(nc, ident[:])
+
+        y = [sb([P, S], F32, f"y{t}") for t in range(4)]
+
+        def entries(lst, start, count):
+            return lst[:, start // STRIPE : (start + count) // STRIPE]
+
+        slot_scales = {}
+
+        def gather_scales(experts, queue):
+            n = len(experts)
+            direct = sb([P, n, 2, C], U8, f"sg{experts[0]}")
+            moved = sb([P, n, 2, C], U8, f"sm{experts[0]}")
+            for a, e in enumerate(experts):
+                for l in range(2):
+                    nc.vector.tensor_copy(direct[:, a, l, :], xs[:].indirect(entries(slot_lists[l], e * C, C)))
+                    slot_scales[e, l, 0] = direct[:, a, l, :]
+                    slot_scales[e, l, 1] = moved[:, a, l, :]
+            src = direct[:].rearrange("p a l c -> p (a l c)").bitcast(I32)
+            dst = moved[:].rearrange("p a l c -> p (a l c)").bitcast(I32)
+            queue.dma_start(dst[0:64], src[8:72])
+            queue.dma_start(dst[64:128], src[12:76])
+
+        def first_layer(start, width, tag):
+            e = start // C
+            sums = [psum.tile([P, H], F32, name=f"hp{start}_{b}", tag="hp", bufs=4) for b in range(width // P)]
+            order = [(l, s) for s in range(PASSES) for l in range(2)]
+            for j, (l, s) in enumerate(order):
+                words = sb([P, width], U32, f"gw{start}_{j}", tag if j == 0 else None)
+                nc.vector.tensor_copy(words[:], xw[s][:].bitcast(U32).indirect(entries(slot_lists[l], start, width)))
+                for b, acc in enumerate(sums):
+                    c0 = start % C + b * P
+                    nc.tensor.matmul_mx(
+                        acc[:],
+                        lhsT=words[:, b * P : (b + 1) * P].bitcast(FP8X4),
+                        lhsT_scale=slot_scales[e, l, s][:, c0 : c0 + P],
+                        rhs=first[l][e][:, s, :].bitcast(FP4X4),
+                        rhs_scale=first_scales[l][:, e * PASSES + s, :],
+                        start=(j == 0),
+                        stop=(j == len(order) - 1),
+                    )
+            return sums
+
+        def activate(start, sums, tag):
+            blocks = len(sums)
+            turned = psum.tile([P, blocks, 2, P], F32, name=f"xt{start}", tag="xt", bufs=2)
+            for b, acc in enumerate(sums):
+                hb = sb([P, H], BF16, f"hb{start}_{b}")
+                nc.scalar.activation(
+                    hb[:].rearrange("s (u p d) -> s u p d", u=2, d=2),
+                    acc[:].rearrange("s (p u d) -> s u p d", u=2, d=2),
+                    GELU,
+                )
+                pairs = hb[:].bitcast(F32)
+                for u in range(2):
+                    nc.tensor.transpose(turned[:, b, u, :], pairs[:, u * P : (u + 1) * P], ident[:])
+            hq = sb([P, blocks * H], BF16, f"hq{start}", tag)
+            nc.scalar.copy(
+                hq[:].bitcast(F32).rearrange("p (b s u) -> p b s u", b=blocks, u=2),
+                turned[:].rearrange("p b u s -> p b s u"),
+            )
+            return hq
+
+        second = {}
+
+        def deal_second(e):
+            words = sb([P, 1024], U8, f"w2w{e}")
+            scales = sb([P, N], U8, f"w2p{e}")
+            nc.vector.tensor_copy(
+                words[:].bitcast(U16).rearrange("p (t c i) -> p c t i", t=4, i=8),
+                w2_raw[:, e, :].bitcast(U16).rearrange("p (c i t) -> p c t i", t=4, i=8),
+            )
+            nc.vector.tensor_copy(
+                scales[:].rearrange("p (t c i) -> p c t i", t=4, i=16),
+                w2s[:, e, :].rearrange("p (c i t) -> p c t i", t=4, i=16),
+            )
+            second[e] = (words, scales)
+
+        def second_layer(start, hq, copiers):
+            width = hq.shape[1] // 4
+            words, scales = second[start // C]
+            codes = sb([P, width], U32, f"hc{start}")
+            plane = sb([P, width], U8, f"hs{start}")
+            nc.vector.quantize_mx(codes[:].bitcast(FP8X4), plane[:], hq[:])
+            for half in range(2):
+                bank = psum.tile([P, 2, width], F32, name=f"yp{start}_{half}", tag="yp", bufs=2)
+                for k in range(2):
+                    t = 2 * half + k
+                    nc.tensor.matmul_mx(
+                        bank[:, k, :],
+                        lhsT=words[:, 2 * P * t : 2 * P * (t + 1)].bitcast(FP4X4),
+                        lhsT_scale=scales[:, P * t : P * (t + 1)],
+                        rhs=codes[:].bitcast(FP8X4),
+                        rhs_scale=plane[:],
+                        start=True,
+                        stop=True,
+                    )
+                for k in range(2):
+                    copiers[half](y[2 * half + k][:, start : start + width], bank[:, k, :])
+
+        on_scalar = (nc.scalar.copy, nc.scalar.copy)
+        on_vector = (nc.vector.tensor_copy, nc.vector.tensor_copy)
+        shared = (nc.vector.tensor_copy, nc.scalar.copy)
+
+        gather_scales((0, 1), nc.scalar)
+        sums0 = first_layer(0, C, None)
+        sums1 = first_layer(C, C, None)
+        hq0 = activate(0, sums0, "hold0")
+        gather_scales((2,), nc.sync)
+        for e in range(E - 1):
+            deal_second(e)
+        hq1 = activate(C, sums1, "hold1")
+        second_layer(0, hq0, on_scalar)
+        sums2 = first_layer(2 * C, C, "hold0")
+        gather_scales((3,), nc.sync)
+        second_layer(C, hq1, on_scalar)
+        hq2 = activate(2 * C, sums2, None)
+        sums3a = first_layer(3 * C, P, "hold1")
+        sums3b = first_layer(3 * C + P, P, None)
+        hq3a = activate(3 * C, sums3a, None)
+        hq3b = activate(3 * C + P, sums3b, None)
+        deal_second(E - 1)
+        second_layer(2 * C, hq2, on_vector)
+        second_layer(3 * C, hq3a, on_scalar)
+        second_layer(3 * C + P, hq3b, shared)
+
+        out_rows = out_0.rearrange("(p t) c -> p t c", t=4)
+        out_codes = sb([P, T], U32, "out_codes")
+        out_plane = sb([P, T], U8, "out_plane")
+        code_rows = out_1[0].rearrange("p t d -> p (t d)").bitcast(I32)
+
+        def gather_products(start, width):
+            parts = [sb([P, 4, width], F32, f"part{start}_{r}") for r in range(2)]
+            for t in range(4):
+                for r in range(2):
+                    nc.vector.tensor_tensor(
+                        parts[r][:, t, :],
+                        y[t][:].indirect(entries(token_lists[r], start, width)),
+                        gates[r][:, start : start + width],
+                        MULT,
+                    )
+            return parts
+
+        def finish(start, width, parts, rounder, queue):
+            total = sb([P, 4, width], F32, f"total{start}")
+            nc.vector.tensor_tensor(total[:], parts[0][:], parts[1][:], ADD)
+            queue.dma_start(out_rows[:, :, start : start + width], total[:])
+            rounded = sb([P, width * 4], BF16, f"rounded{start}")
+            rounder(
+                rounded[:].rearrange("p (c i t) -> p c t i", t=4, i=4),
+                total[:].rearrange("p t (c i) -> p c t i", i=4),
+            )
+            done = 0
+            for piece in (256, 128):
+                if width - done >= piece:
+                    cols = slice(start + done, start + done + piece)
+                    nc.vector.quantize_mx(out_codes[:, cols].bitcast(FP8X4), out_plane[:, cols], rounded[:, 4 * done : 4 * (done + piece)])
+                    done = done + piece
+            nc.sync.dma_start(code_rows[:, start : start + width], out_codes[:, start : start + width].bitcast(I32))
+
+        for (start, width), rounder, queue in zip(TOKEN_CHUNKS, (nc.scalar.copy, nc.vector.tensor_copy), (nc.sync, nc.scalar)):
+            finish(start, width, gather_products(start, width), rounder, queue)
+        scale_rows = out_2[0].bitcast(I32)
+        for q in range(4):
+            queue = nc.sync if q % 2 else nc.scalar
+            queue.dma_start(scale_rows[4 * q : 4 * q + 4], out_plane[32 * q : 32 * q + 4].bitcast(I32))

@@ -34,64 +34,55 @@ def tile_moe_duo_gelu_kernel(
         keep = ctx.enter_context(tc.tile_pool(name="keep", bufs=1))
         psum = ctx.enter_context(tc.psum_pool(name="psum", bufs=1))
 
-        def sb(shape, dtype, name, tag=None):
-            return keep.tile(shape, dtype, name=name, tag=tag or name, align_bytes=64)
+        reuse = ctx.enter_context(tc.tile_pool(name="reuse", bufs=1))
+
+        def sb(shape, dtype, name, place=None):
+            if isinstance(place, int):
+                return reuse.tile(shape, dtype, name=name, tag=name, align_bytes=64, offset=place)
+            return keep.tile(shape, dtype, name=name, tag=place or name, align_bytes=64)
 
         def load_list(src, name):
             tile = keep.tile(list(src.shape), U16, name=name)
             nc.sync.dma_start(tile[:], src)
             return tile
 
-        def load_planes(plane, scales):
+        def load_planes(plane, scales, queue):
             rows = scales.rearrange("e s b c -> b (e s) c").bitcast(I32)
-            for q in range(4):
-                nc.sync.dma_start(plane[32 * q : 32 * q + 4].bitcast(I32), rows[4 * q : 4 * q + 4])
+            for r in range(4):
+                queue.dma_start(plane[r:P:32].bitcast(I32), rows[r:16:4])
 
-        def load_words(words, e, name):
-            tile = sb([P, words.shape[1], 1024], U8, f"{name}{e}")
-            nc.sync.dma_start(tile[:].bitcast(I32), words[e].rearrange("s p c -> p s c").bitcast(I32))
-            return tile
+        def load_words(words, e0, count, name, offset):
+            tile = sb([P, count, words.shape[1], 1024], U8, f"{name}{e0}", offset)
+            nc.sync.dma_start(
+                tile[:].rearrange("p e s c -> p (e s) c").bitcast(I32),
+                words[e0 : e0 + count].rearrange("e s p c -> p (e s) c").bitcast(I32),
+            )
+            return [tile[:, a] for a in range(count)]
 
         xs = sb([P, T], U8, "xs")
-        w1s = sb([P, E * PASSES, H], U8, "w1s")
-        wps = sb([P, E * PASSES, H], U8, "wps")
-        w2s = sb([P, E, N], U8, "w2s")
-        for plane in (xs, w1s, wps, w2s):
-            nc.vector.memset(plane[:].bitcast(I32), 0)
+        planes = sb([P, E * PASSES, 2, H], U8, "planes")
+        w1s, wps = planes[:, :, 0, :], planes[:, :, 1, :]
+        w2s = planes[:, 0:PASSES].rearrange("p s l c -> p (s l) c")
+        nc.gpsimd.memset(xs[:].bitcast(I32), 0)
+        nc.vector.memset(planes[:, 0:E].bitcast(I32), 0)
+        nc.gpsimd.memset(planes[:, E : 2 * E].bitcast(I32), 0)
 
-        slot_lists = [load_list(offs, "offs_sb"), load_list(offs2, "offs2_sb")]
+        slot_lists = [load_list(offs, "offs_sb")]
         groups = x_scales.rearrange("s (q r) c -> (s q) r c", r=4).bitcast(I32)
         xs_i = xs[:].bitcast(I32)
         nc.sync.dma_start(xs_i[0:16], groups[0:8:2])
         nc.sync.dma_start(xs_i[32:48], groups[1:8:2])
         nc.sync.dma_start(xs_i[64:68], groups[2])
         nc.sync.dma_start(xs_i[96:100], groups[3])
-        xw = []
-        for s in range(PASSES):
-            tile = sb([P, T], I32, f"xw{s}")
-            nc.sync.dma_start(tile[:], x_words[s].rearrange("p t d -> p (t d)").bitcast(I32))
-            xw.append(tile)
+        slot_lists.append(load_list(offs2, "offs2_sb"))
+        xw = sb([P, PASSES, T], I32, "xw")
+        nc.sync.dma_start(xw[:], x_words.rearrange("s p t d -> p s (t d)").bitcast(I32))
 
-        first = [{}, {}]
-        load_planes(w1s, w1_scales)
-        first[0][0] = load_words(w1_words, 0, "w1_")
-        load_planes(wps, wp_scales)
-        first[1][0] = load_words(wp_words, 0, "wp_")
-        first[0][1] = load_words(w1_words, 1, "w1_")
-        first[1][1] = load_words(wp_words, 1, "wp_")
-        w2_raw = sb([P, E, 1024], U8, "w2_raw")
-        nc.sync.dma_start(w2_raw[:].bitcast(I32), w2_words.rearrange("e s p c -> p (e s) c").bitcast(I32))
-        load_planes(w2s, w2_scales)
-        for e in (2, 3):
-            first[0][e] = load_words(w1_words, e, "w1_")
-            first[1][e] = load_words(wp_words, e, "wp_")
+        first = [load_words(w1_words, 0, 1, "w1_", None)]
+        load_planes(w1s, w1_scales, nc.sync)
+        first.append(load_words(wp_words, 0, 1, "wp_", None))
+        load_planes(wps, wp_scales, nc.sync)
         first_scales = (w1s, wps)
-        token_lists = [load_list(pos1, "pos1_sb"), load_list(pos2, "pos2_sb")]
-        gates = []
-        for r in range(2):
-            tile = sb([P, T], F32, f"gate{r}")
-            nc.sync.dma_start(tile[:], gate[r])
-            gates.append(tile)
 
         ident = sb([P, P], F32, "ident")
         make_identity(nc, ident[:])
@@ -103,41 +94,42 @@ def tile_moe_duo_gelu_kernel(
 
         slot_scales = {}
 
-        def gather_scales(experts, queue):
-            n = len(experts)
-            direct = sb([P, n, 2, C], U8, f"sg{experts[0]}")
-            moved = sb([P, n, 2, C], U8, f"sm{experts[0]}")
-            for a, e in enumerate(experts):
-                for l in range(2):
-                    nc.vector.tensor_copy(direct[:, a, l, :], xs[:].indirect(entries(slot_lists[l], e * C, C)))
-                    slot_scales[e, l, 0] = direct[:, a, l, :]
-                    slot_scales[e, l, 1] = moved[:, a, l, :]
-            src = direct[:].rearrange("p a l c -> p (a l c)").bitcast(I32)
-            dst = moved[:].rearrange("p a l c -> p (a l c)").bitcast(I32)
-            queue.dma_start(dst[0:64], src[8:72])
-            queue.dma_start(dst[64:128], src[12:76])
+        def gather_scales(e, direct_at, moved_at):
+            direct = sb([P, 2, C], U8, f"sg{e}", direct_at)
+            moved = sb([P, 2, C], U8, f"sm{e}", moved_at)
+            for l in range(2):
+                nc.vector.tensor_copy(direct[:, l, :], xs[:].indirect(entries(slot_lists[l], e * C, C)))
+                slot_scales[e, l, 0] = direct[:, l, :]
+                slot_scales[e, l, 1] = moved[:, l, :]
+            src = direct[:].rearrange("p l c -> p (l c)").bitcast(I32)
+            dst = moved[:].rearrange("p l c -> p (l c)").bitcast(I32)
+            nc.sync.dma_start(dst[0:64], src[8:72])
+            nc.sync.dma_start(dst[64:128], src[12:76])
 
-        def first_layer(start, width, tag):
+        def open_sums(start, width):
+            return [psum.tile([P, H], F32, name=f"hp{start}_{b}", tag="hp", bufs=4) for b in range(width // P)]
+
+        def first_layer(start, sums, passes, first_pass, place):
             e = start // C
-            sums = [psum.tile([P, H], F32, name=f"hp{start}_{b}", tag="hp", bufs=4) for b in range(width // P)]
-            order = [(l, s) for s in range(PASSES) for l in range(2)]
-            for j, (l, s) in enumerate(order):
-                words = sb([P, width], U32, f"gw{start}_{j}", tag if j == 0 else None)
-                nc.vector.tensor_copy(words[:], xw[s][:].bitcast(U32).indirect(entries(slot_lists[l], start, width)))
-                for b, acc in enumerate(sums):
-                    c0 = start % C + b * P
-                    nc.tensor.matmul_mx(
-                        acc[:],
-                        lhsT=words[:, b * P : (b + 1) * P].bitcast(FP8X4),
-                        lhsT_scale=slot_scales[e, l, s][:, c0 : c0 + P],
-                        rhs=first[l][e][:, s, :].bitcast(FP4X4),
-                        rhs_scale=first_scales[l][:, e * PASSES + s, :],
-                        start=(j == 0),
-                        stop=(j == len(order) - 1),
-                    )
-            return sums
+            width = len(sums) * P
+            gathered = sb([P, len(passes), 2, width], U32, f"gw{start}_{passes[0]}", place)
+            for a, s in enumerate(passes):
+                for l in range(2):
+                    words = gathered[:, a, l, :]
+                    nc.vector.tensor_copy(words, xw[:, s, :].bitcast(U32).indirect(entries(slot_lists[l], start, width)))
+                    for b, acc in enumerate(sums):
+                        c0 = start % C + b * P
+                        nc.tensor.matmul_mx(
+                            acc[:],
+                            lhsT=words[:, b * P : (b + 1) * P].bitcast(FP8X4),
+                            lhsT_scale=slot_scales[e, l, s][:, c0 : c0 + P],
+                            rhs=first[l][e][:, s, :].bitcast(FP4X4),
+                            rhs_scale=first_scales[l][:, e * PASSES + s, :],
+                            start=(s == first_pass and l == 0),
+                            stop=(s != first_pass and l == 1),
+                        )
 
-        def activate(start, sums, tag):
+        def activate(start, sums, offset):
             blocks = len(sums)
             turned = psum.tile([P, blocks, 2, P], F32, name=f"xt{start}", tag="xt", bufs=2)
             for b, acc in enumerate(sums):
@@ -150,7 +142,7 @@ def tile_moe_duo_gelu_kernel(
                 pairs = hb[:].bitcast(F32)
                 for u in range(2):
                     nc.tensor.transpose(turned[:, b, u, :], pairs[:, u * P : (u + 1) * P], ident[:])
-            hq = sb([P, blocks * H], BF16, f"hq{start}", tag)
+            hq = sb([P, blocks * H], BF16, f"hq{start}", offset)
             nc.scalar.copy(
                 hq[:].bitcast(F32).rearrange("p (b s u) -> p b s u", b=blocks, u=2),
                 turned[:].rearrange("p b u s -> p b s u"),
@@ -159,29 +151,31 @@ def tile_moe_duo_gelu_kernel(
 
         second = {}
 
-        def deal_second(e):
-            words = sb([P, 1024], U8, f"w2w{e}")
-            scales = sb([P, N], U8, f"w2p{e}")
+        def deal_second(e0, words_at, scales_at):
+            words = sb([P, 2, 1024], U8, f"w2w{e0}", words_at)
+            scales = sb([P, 2, N], U8, f"w2p{e0}", scales_at)
             nc.vector.tensor_copy(
-                words[:].bitcast(U16).rearrange("p (t c i) -> p c t i", t=4, i=8),
-                w2_raw[:, e, :].bitcast(U16).rearrange("p (c i t) -> p c t i", t=4, i=8),
+                words[:].bitcast(U16).rearrange("p e (t c i) -> p e c t i", t=4, i=8),
+                w2w[:, e0 : e0 + 2, :].bitcast(U16).rearrange("p e (c i t) -> p e c t i", t=4, i=8),
             )
             nc.vector.tensor_copy(
-                scales[:].rearrange("p (t c i) -> p c t i", t=4, i=16),
-                w2s[:, e, :].rearrange("p (c i t) -> p c t i", t=4, i=16),
+                scales[:].rearrange("p e (t c i) -> p e c t i", t=4, i=16),
+                w2s[:, e0 : e0 + 2, :].rearrange("p e (c i t) -> p e c t i", t=4, i=16),
             )
-            second[e] = (words, scales)
+            for a in range(2):
+                second[e0 + a] = (words[:, a, :], scales[:, a, :])
 
-        def second_layer(start, hq, copiers):
+        def second_layer(start, hq, copiers, tag, bufs):
             width = hq.shape[1] // 4
             words, scales = second[start // C]
             codes = sb([P, width], U32, f"hc{start}")
             plane = sb([P, width], U8, f"hs{start}")
             nc.vector.quantize_mx(codes[:].bitcast(FP8X4), plane[:], hq[:])
-            for half in range(2):
-                bank = psum.tile([P, 2, width], F32, name=f"yp{start}_{half}", tag="yp", bufs=2)
-                for k in range(2):
-                    t = 2 * half + k
+            per_bank = 4 // len(copiers)
+            for part, copier in enumerate(copiers):
+                bank = psum.tile([P, per_bank, width], F32, name=f"yp{start}_{part}", tag=tag, bufs=bufs)
+                for k in range(per_bank):
+                    t = per_bank * part + k
                     nc.tensor.matmul_mx(
                         bank[:, k, :],
                         lhsT=words[:, 2 * P * t : 2 * P * (t + 1)].bitcast(FP4X4),
@@ -191,55 +185,76 @@ def tile_moe_duo_gelu_kernel(
                         start=True,
                         stop=True,
                     )
-                for k in range(2):
-                    copiers[half](y[2 * half + k][:, start : start + width], bank[:, k, :])
+                for k in range(per_bank):
+                    copier(y[per_bank * part + k][:, start : start + width], bank[:, k, :])
 
         on_scalar = (nc.scalar.copy, nc.scalar.copy)
         on_vector = (nc.vector.tensor_copy, nc.vector.tensor_copy)
         shared = (nc.vector.tensor_copy, nc.scalar.copy)
 
-        gather_scales((0, 1), nc.scalar)
-        sums0 = first_layer(0, C, None)
-        sums1 = first_layer(C, C, None)
-        hq0 = activate(0, sums0, "hold0")
-        gather_scales((2,), nc.sync)
-        for e in range(E - 1):
-            deal_second(e)
-        hq1 = activate(C, sums1, "hold1")
-        second_layer(0, hq0, on_scalar)
-        sums2 = first_layer(2 * C, C, "hold0")
-        gather_scales((3,), nc.sync)
-        second_layer(C, hq1, on_scalar)
+        gather_scales(0, 10240, 16384)
+        gather_scales(1, None, None)
+        first[0].extend(load_words(w1_words, 1, 1, "w1_", 0))
+        first[1].extend(load_words(wp_words, 1, 1, "wp_", 4096))
+        sums0 = open_sums(0, C)
+        first_layer(0, sums0, (0, 1), 0, 24576)
+        gather_scales(2, None, None)
+        first[0].extend(load_words(w1_words, 2, 1, "w1_", 8256))
+        first[1].extend(load_words(wp_words, 2, 1, "wp_", 10688))
+        load_planes(w2s, w2_scales, nc.sync)
+        w2w = sb([P, E, 1024], U8, "w2w", 16832)
+        nc.sync.dma_start(w2w[:].bitcast(I32), w2_words.rearrange("e s p c -> p (e s) c").bitcast(I32))
+        first[0].extend(load_words(w1_words, 3, 1, "w1_", 24576))
+        first[1].extend(load_words(wp_words, 3, 1, "wp_", 24576 + 2048))
+        hq0 = activate(0, sums0, "grouped0")
+        sums1 = open_sums(C, C)
+        first_layer(C, sums1, (1, 0), 1, None)
+        token_lists = [load_list(pos1, "pos1_sb"), load_list(pos2, "pos2_sb")]
+        gates = []
+        for r in range(2):
+            tile = sb([P, T], F32, f"gate{r}", 4096 * r)
+            nc.sync.dma_start(tile[:], gate[r])
+            gates.append(tile)
+        hq1 = activate(C, sums1, 30720)
+        sums2 = open_sums(2 * C, C)
+        first_layer(2 * C, sums2, (0,), 0, None)
+        gather_scales(3, 15936, None)
+        deal_second(0, None, None)
+        second_layer(0, hq0, on_scalar, "yp", 2)
+        first_layer(2 * C, sums2, (1,), 0, "grouped0")
         hq2 = activate(2 * C, sums2, None)
-        sums3a = first_layer(3 * C, P, "hold1")
-        sums3b = first_layer(3 * C + P, P, None)
+        second_layer(C, hq1, on_scalar, "yp", 2)
+        sums3a = open_sums(3 * C, P)
+        first_layer(3 * C, sums3a, (0, 1), 0, 30720 - 1024)
+        sums3b = open_sums(3 * C + P, P)
+        first_layer(3 * C + P, sums3b, (0, 1), 0, 30720 + 1024)
         hq3a = activate(3 * C, sums3a, None)
         hq3b = activate(3 * C + P, sums3b, None)
-        deal_second(E - 1)
-        second_layer(2 * C, hq2, on_vector)
-        second_layer(3 * C, hq3a, on_scalar)
-        second_layer(3 * C + P, hq3b, shared)
+        deal_second(2, 28672, 30720)
+        second_layer(2 * C, hq2, on_vector, "yp", 2)
+        second_layer(3 * C, hq3a, on_scalar[:1], "hp", 4)
+        second_layer(3 * C + P, hq3b, shared, "hp", 4)
 
         out_rows = out_0.rearrange("(p t) c -> p t c", t=4)
         out_codes = sb([P, T], U32, "out_codes")
         out_plane = sb([P, T], U8, "out_plane")
         code_rows = out_1[0].rearrange("p t d -> p (t d)").bitcast(I32)
 
-        def gather_products(start, width):
-            parts = [sb([P, 4, width], F32, f"part{start}_{r}") for r in range(2)]
-            for t in range(4):
-                for r in range(2):
-                    nc.vector.tensor_tensor(
-                        parts[r][:, t, :],
-                        y[t][:].indirect(entries(token_lists[r], start, width)),
-                        gates[r][:, start : start + width],
-                        MULT,
-                    )
-            return parts
+        def gather_product(chunk, t, r):
+            start, width, parts, total = chunk
+            nc.vector.tensor_tensor(
+                parts[r][:, t, :],
+                y[t][:].indirect(entries(token_lists[r], start, width)),
+                gates[r][:, start : start + width],
+                MULT,
+            )
 
-        def finish(start, width, parts, rounder, queue):
-            total = sb([P, 4, width], F32, f"total{start}")
-            nc.vector.tensor_tensor(total[:], parts[0][:], parts[1][:], ADD)
+        def add_up(chunk, t0, t1):
+            start, width, parts, total = chunk
+            nc.vector.tensor_tensor(total[:, t0:t1], parts[0][:, t0:t1], parts[1][:, t0:t1], ADD)
+
+        def finish(chunk, rounder, queue):
+            start, width, parts, total = chunk
             queue.dma_start(out_rows[:, :, start : start + width], total[:])
             rounded = sb([P, width * 4], BF16, f"rounded{start}")
             rounder(
@@ -254,9 +269,23 @@ def tile_moe_duo_gelu_kernel(
                     done = done + piece
             nc.sync.dma_start(code_rows[:, start : start + width], out_codes[:, start : start + width].bitcast(I32))
 
-        for (start, width), rounder, queue in zip(TOKEN_CHUNKS, (nc.scalar.copy, nc.vector.tensor_copy), (nc.sync, nc.scalar)):
-            finish(start, width, gather_products(start, width), rounder, queue)
+        head, tail = [
+            (start, width, [sb([P, 4, width], F32, f"part{start}_{r}") for r in range(2)], sb([P, 4, width], F32, f"total{start}"))
+            for start, width in TOKEN_CHUNKS
+        ]
+        steps = [(t, r) for t in range(4) for r in range(2)]
+        for t, r in steps:
+            gather_product(head, t, r)
+        gather_product(tail, *steps[0])
+        add_up(head, 0, 4)
+        for t, r in steps[1:-1]:
+            gather_product(tail, t, r)
+        add_up(tail, 0, 3)
+        gather_product(tail, *steps[-1])
+        finish(head, nc.scalar.copy, nc.sync)
+        add_up(tail, 3, 4)
+        finish(tail, nc.vector.tensor_copy, nc.scalar)
         scale_rows = out_2[0].bitcast(I32)
-        for q in range(4):
-            queue = nc.sync if q % 2 else nc.scalar
-            queue.dma_start(scale_rows[4 * q : 4 * q + 4], out_plane[32 * q : 32 * q + 4].bitcast(I32))
+        for r in range(4):
+            queue = nc.sync if r % 2 else nc.scalar
+            queue.dma_start(scale_rows[r:16:4], out_plane[r:P:32].bitcast(I32))

@@ -16,6 +16,7 @@ U8 = mybir.dt.uint8
 FP8X4 = mybir.dt.float8_e4m3fn_x4
 FP4X4 = mybir.dt.float4_e2m1fn_x4
 GELU = mybir.ActivationFunctionType.Gelu_apprx_tanh
+COPY = mybir.ActivationFunctionType.Copy
 MULT = mybir.AluOpType.mult
 ADD = mybir.AluOpType.add
 
@@ -34,129 +35,119 @@ def tile_moe_duo_gelu_kernel(
         keep = ctx.enter_context(tc.tile_pool(name="keep", bufs=1))
         psum = ctx.enter_context(tc.psum_pool(name="psum", bufs=1))
 
-        reuse = ctx.enter_context(tc.tile_pool(name="reuse", bufs=1))
-
-        def sb(shape, dtype, name, place=None):
-            if isinstance(place, int):
-                return reuse.tile(shape, dtype, name=name, tag=name, align_bytes=64, offset=place)
-            return keep.tile(shape, dtype, name=name, tag=place or name, align_bytes=64)
+        def sb(shape, dtype, name, tag=None, bufs=1):
+            return keep.tile(shape, dtype, name=name, tag=tag or name, bufs=bufs, align_bytes=64)
 
         def load_list(src, name):
             tile = keep.tile(list(src.shape), U16, name=name)
             nc.sync.dma_start(tile[:], src)
             return tile
 
-        def load_planes(plane, scales, queue):
+        def load_planes(plane, scales):
             rows = scales.rearrange("e s b c -> b (e s) c").bitcast(I32)
             for r in range(4):
-                queue.dma_start(plane[r:P:32].bitcast(I32), rows[r:16:4])
+                nc.sync.dma_start(plane[r:P:32].bitcast(I32), rows[r:16:4])
 
-        def load_words(words, e0, count, name, offset):
-            tile = sb([P, count, words.shape[1], 1024], U8, f"{name}{e0}", offset)
-            nc.sync.dma_start(
-                tile[:].rearrange("p e s c -> p (e s) c").bitcast(I32),
-                words[e0 : e0 + count].rearrange("e s p c -> p (e s) c").bitcast(I32),
-            )
-            return [tile[:, a] for a in range(count)]
+        def load_words(words, e, name, tag=None):
+            tile = sb([P, PASSES, 1024], U8, f"{name}{e}", tag)
+            nc.sync.dma_start(tile[:].bitcast(I32), words[e].rearrange("s p c -> p s c").bitcast(I32))
+            return [tile]
+
+        def entries(lst, start, count):
+            return lst[:, start // STRIPE : (start + count) // STRIPE]
 
         xs = sb([P, T], U8, "xs")
-        planes = sb([P, E * PASSES, 2, H], U8, "planes")
-        w1s, wps = planes[:, :, 0, :], planes[:, :, 1, :]
-        w2s = planes[:, 0:PASSES].rearrange("p s l c -> p (s l) c")
+        first_scales = [sb([P, E * PASSES, H], U8, f"first_scales{l}") for l in range(2)]
+        w2s = first_scales[0][:, 0:E]
+        moved = [sb([P, 2, C], U8, f"moved{a}") for a in range(2)]
         nc.gpsimd.memset(xs[:].bitcast(I32), 0)
-        nc.vector.memset(planes[:, 0:E].bitcast(I32), 0)
-        nc.gpsimd.memset(planes[:, E : 2 * E].bitcast(I32), 0)
+        nc.vector.memset(first_scales[0][:].bitcast(I32), 0)
+        nc.gpsimd.memset(first_scales[1][:].bitcast(I32), 0)
+        for tile in moved:
+            nc.vector.memset(tile[:].bitcast(I32), 0)
 
         slot_lists = [load_list(offs, "offs_sb")]
-        groups = x_scales.rearrange("s (q r) c -> (s q) r c", r=4).bitcast(I32)
-        xs_i = xs[:].bitcast(I32)
-        nc.sync.dma_start(xs_i[0:16], groups[0:8:2])
-        nc.sync.dma_start(xs_i[32:48], groups[1:8:2])
-        nc.sync.dma_start(xs_i[64:68], groups[2])
-        nc.sync.dma_start(xs_i[96:100], groups[3])
+        for q in range(4):
+            nc.sync.dma_start(xs[:].bitcast(I32)[32 * q : 32 * q + 8], x_scales[:, 4 * q : 4 * q + 4, :].bitcast(I32))
+        xw = [sb([P, T], I32, f"xw{s}") for s in range(PASSES)]
+        x_rows = x_words.rearrange("s p t d -> s p (t d)").bitcast(I32)
+        nc.sync.dma_start(xw[0][:], x_rows[0])
         slot_lists.append(load_list(offs2, "offs2_sb"))
-        xw = sb([P, PASSES, T], I32, "xw")
-        nc.sync.dma_start(xw[:], x_words.rearrange("s p t d -> p s (t d)").bitcast(I32))
-
-        first = [load_words(w1_words, 0, 1, "w1_", None)]
-        load_planes(w1s, w1_scales, nc.sync)
-        first.append(load_words(wp_words, 0, 1, "wp_", None))
-        load_planes(wps, wp_scales, nc.sync)
-        first_scales = (w1s, wps)
+        nc.sync.dma_start(xw[1][:], x_rows[1])
+        first = [load_words(w1_words, 0, "w1_")]
+        load_planes(first_scales[0], w1_scales)
+        first.append(load_words(wp_words, 0, "wp_"))
+        load_planes(first_scales[1], wp_scales)
 
         ident = sb([P, P], F32, "ident")
         make_identity(nc, ident[:])
 
         y = [sb([P, S], F32, f"y{t}") for t in range(4)]
+        direct = {}
 
-        def entries(lst, start, count):
-            return lst[:, start // STRIPE : (start + count) // STRIPE]
+        def gather_scales(e, l):
+            if l == 0:
+                direct[e] = sb([P, 2, C], U8, f"direct{e}")
+            nc.vector.tensor_copy(direct[e][:, l, :], xs[:].indirect(entries(slot_lists[l], e * C, C)))
 
-        slot_scales = {}
+        def move_scales(e):
+            src = direct[e][:].rearrange("p l c -> p (l c)").bitcast(I32)
+            dst = moved[e % 2][:].rearrange("p l c -> p (l c)").bitcast(I32)
+            for p0, count in ((0, 64), (64, 4), (96, 4)):
+                nc.sync.dma_start(dst[p0 : p0 + count], src[p0 + 4 : p0 + 4 + count])
 
-        def gather_scales(e, direct_at, moved_at):
-            direct = sb([P, 2, C], U8, f"sg{e}", direct_at)
-            moved = sb([P, 2, C], U8, f"sm{e}", moved_at)
-            for l in range(2):
-                nc.vector.tensor_copy(direct[:, l, :], xs[:].indirect(entries(slot_lists[l], e * C, C)))
-                slot_scales[e, l, 0] = direct[:, l, :]
-                slot_scales[e, l, 1] = moved[:, l, :]
-            src = direct[:].rearrange("p l c -> p (l c)").bitcast(I32)
-            dst = moved[:].rearrange("p l c -> p (l c)").bitcast(I32)
-            nc.sync.dma_start(dst[0:64], src[8:72])
-            nc.sync.dma_start(dst[64:128], src[12:76])
+        sums = {}
+        gathered = {}
 
-        def open_sums(start, width):
-            return [psum.tile([P, H], F32, name=f"hp{start}_{b}", tag="hp", bufs=4) for b in range(width // P)]
+        def first_layer(e, s, l, blocks=(0, 1)):
+            if (e, s, l) not in gathered:
+                gathered[e, s, l] = sb([P, C], U32, f"gw{e}_{s}_{l}")
+            cols = slice(blocks[0] * P, (blocks[-1] + 1) * P)
+            nc.vector.tensor_copy(
+                gathered[e, s, l][:, cols],
+                xw[s][:].bitcast(U32).indirect(entries(slot_lists[l], e * C + cols.start, cols.stop - cols.start)),
+            )
+            scales = moved[e % 2] if s else direct[e]
+            for b in blocks:
+                if (e, b) not in sums:
+                    sums[e, b] = psum.tile([P, H], F32, name=f"sum{e}_{b}", tag="sum", bufs=4)
+                nc.tensor.matmul_mx(
+                    sums[e, b][:],
+                    lhsT=gathered[e, s, l][:, b * P : (b + 1) * P].bitcast(FP8X4),
+                    lhsT_scale=scales[:, l, b * P : (b + 1) * P],
+                    rhs=first[l][e][:, s, :].bitcast(FP4X4),
+                    rhs_scale=first_scales[l][:, e * PASSES + s, :],
+                    start=(s == 0 and l == 0),
+                    stop=(s == 1 and l == 1),
+                )
 
-        def first_layer(start, sums, passes, first_pass, place):
-            e = start // C
-            width = len(sums) * P
-            gathered = sb([P, len(passes), 2, width], U32, f"gw{start}_{passes[0]}", place)
-            for a, s in enumerate(passes):
-                for l in range(2):
-                    words = gathered[:, a, l, :]
-                    nc.vector.tensor_copy(words, xw[:, s, :].bitcast(U32).indirect(entries(slot_lists[l], start, width)))
-                    for b, acc in enumerate(sums):
-                        c0 = start % C + b * P
-                        nc.tensor.matmul_mx(
-                            acc[:],
-                            lhsT=words[:, b * P : (b + 1) * P].bitcast(FP8X4),
-                            lhsT_scale=slot_scales[e, l, s][:, c0 : c0 + P],
-                            rhs=first[l][e][:, s, :].bitcast(FP4X4),
-                            rhs_scale=first_scales[l][:, e * PASSES + s, :],
-                            start=(s == first_pass and l == 0),
-                            stop=(s != first_pass and l == 1),
-                        )
-
-        def activate(start, sums, offset):
-            blocks = len(sums)
-            turned = psum.tile([P, blocks, 2, P], F32, name=f"xt{start}", tag="xt", bufs=2)
-            for b, acc in enumerate(sums):
-                hb = sb([P, H], BF16, f"hb{start}_{b}")
+        def activate(e, blocks):
+            turned = psum.tile([P, len(blocks), 2, P], F32, name=f"turned{e}_{blocks[0]}", tag="turned", bufs=2)
+            for a, b in enumerate(blocks):
+                hb = sb([P, H], BF16, f"hb{e}_{b}")
                 nc.scalar.activation(
                     hb[:].rearrange("s (u p d) -> s u p d", u=2, d=2),
-                    acc[:].rearrange("s (p u d) -> s u p d", u=2, d=2),
+                    sums[e, b][:].rearrange("s (p u d) -> s u p d", u=2, d=2),
                     GELU,
                 )
                 pairs = hb[:].bitcast(F32)
                 for u in range(2):
-                    nc.tensor.transpose(turned[:, b, u, :], pairs[:, u * P : (u + 1) * P], ident[:])
-            hq = sb([P, blocks * H], BF16, f"hq{start}", offset)
+                    nc.tensor.transpose(turned[:, a, u, :], pairs[:, u * P : (u + 1) * P], ident[:])
+            hq = sb([P, len(blocks) * H], BF16, f"hq{e}_{blocks[0]}")
             nc.scalar.copy(
-                hq[:].bitcast(F32).rearrange("p (b s u) -> p b s u", b=blocks, u=2),
+                hq[:].bitcast(F32).rearrange("p (b s u) -> p b s u", b=len(blocks), u=2),
                 turned[:].rearrange("p b u s -> p b s u"),
             )
             return hq
 
         second = {}
 
-        def deal_second(e0, words_at, scales_at):
-            words = sb([P, 2, 1024], U8, f"w2w{e0}", words_at)
-            scales = sb([P, 2, N], U8, f"w2p{e0}", scales_at)
+        def deal_second(e0):
+            words = sb([P, 2, 1024], U8, f"w2w{e0}")
+            scales = sb([P, 2, N], U8, f"w2p{e0}")
             nc.vector.tensor_copy(
                 words[:].bitcast(U16).rearrange("p e (t c i) -> p e c t i", t=4, i=8),
-                w2w[:, e0 : e0 + 2, :].bitcast(U16).rearrange("p e (c i t) -> p e c t i", t=4, i=8),
+                w2w[e0 // 2][:].bitcast(U16).rearrange("p e (c i t) -> p e c t i", t=4, i=8),
             )
             nc.vector.tensor_copy(
                 scales[:].rearrange("p e (t c i) -> p e c t i", t=4, i=16),
@@ -165,126 +156,116 @@ def tile_moe_duo_gelu_kernel(
             for a in range(2):
                 second[e0 + a] = (words[:, a, :], scales[:, a, :])
 
-        def second_layer(start, hq, copiers, tag, bufs):
+        def quantise(hq, name):
             width = hq.shape[1] // 4
-            words, scales = second[start // C]
-            codes = sb([P, width], U32, f"hc{start}")
-            plane = sb([P, width], U8, f"hs{start}")
+            codes = sb([P, width], U32, f"hc{name}")
+            plane = sb([P, width], U8, f"hs{name}")
             nc.vector.quantize_mx(codes[:].bitcast(FP8X4), plane[:], hq[:])
-            per_bank = 4 // len(copiers)
-            for part, copier in enumerate(copiers):
-                bank = psum.tile([P, per_bank, width], F32, name=f"yp{start}_{part}", tag=tag, bufs=bufs)
-                for k in range(per_bank):
-                    t = per_bank * part + k
-                    nc.tensor.matmul_mx(
-                        bank[:, k, :],
-                        lhsT=words[:, 2 * P * t : 2 * P * (t + 1)].bitcast(FP4X4),
-                        lhsT_scale=scales[:, P * t : P * (t + 1)],
-                        rhs=codes[:].bitcast(FP8X4),
-                        rhs_scale=plane[:],
-                        start=True,
-                        stop=True,
-                    )
-                for k in range(per_bank):
-                    copier(y[per_bank * part + k][:, start : start + width], bank[:, k, :])
+            return codes, plane
 
-        on_scalar = (nc.scalar.copy, nc.scalar.copy)
-        on_vector = (nc.vector.tensor_copy, nc.vector.tensor_copy)
-        shared = (nc.vector.tensor_copy, nc.scalar.copy)
+        def second_product(bank_cols, e, t, operand):
+            words, scales = second[e]
+            nc.tensor.matmul_mx(
+                bank_cols,
+                lhsT=words[:, 2 * P * t : 2 * P * (t + 1)].bitcast(FP4X4),
+                lhsT_scale=scales[:, P * t : P * (t + 1)],
+                rhs=operand[0][:].bitcast(FP8X4),
+                rhs_scale=operand[1][:],
+                start=True,
+                stop=True,
+            )
 
-        gather_scales(0, 10240, 16384)
-        gather_scales(1, None, None)
-        first[0].extend(load_words(w1_words, 1, 1, "w1_", 0))
-        first[1].extend(load_words(wp_words, 1, 1, "wp_", 4096))
-        sums0 = open_sums(0, C)
-        first_layer(0, sums0, (0, 1), 0, 24576)
-        gather_scales(2, None, None)
-        first[0].extend(load_words(w1_words, 2, 1, "w1_", 8256))
-        first[1].extend(load_words(wp_words, 2, 1, "wp_", 10688))
-        load_planes(w2s, w2_scales, nc.sync)
-        w2w = sb([P, E, 1024], U8, "w2w", 16832)
-        nc.sync.dma_start(w2w[:].bitcast(I32), w2_words.rearrange("e s p c -> p (e s) c").bitcast(I32))
-        first[0].extend(load_words(w1_words, 3, 1, "w1_", 24576))
-        first[1].extend(load_words(wp_words, 3, 1, "wp_", 24576 + 2048))
-        hq0 = activate(0, sums0, "grouped0")
-        sums1 = open_sums(C, C)
-        first_layer(C, sums1, (1, 0), 1, None)
+        def second_layer(start, operands, tag, bufs, copiers):
+            width = sum(op[0].shape[1] for op in operands)
+            for t in range(4):
+                bank = psum.tile([P, width], F32, name=f"yp{start}_{t}", tag=tag, bufs=bufs)
+                done = 0
+                for op in operands:
+                    w = op[0].shape[1]
+                    second_product(bank[:, done : done + w], (start + done) // C, t, op)
+                    done = done + w
+                copiers[t](y[t][:, start : start + width], bank[:])
+
+        for e in range(2):
+            for l in range(2):
+                gather_scales(e, l)
+                first_layer(e, 0, l)
+            move_scales(e)
+            if e == 0:
+                first[0].extend(load_words(w1_words, 1, "w1_"))
+                first[1].extend(load_words(wp_words, 1, "wp_"))
         token_lists = [load_list(pos1, "pos1_sb"), load_list(pos2, "pos2_sb")]
+        first_layer(0, 1, 0)
+        first[0].extend(load_words(w1_words, 2, "w1_", "gw0_0_0"))
+        first_layer(0, 1, 1)
+        first[1].extend(load_words(wp_words, 2, "wp_", "gw0_0_1"))
+        hq0 = activate(0, (0, 1))
+        w2w = []
+        for a in range(2):
+            tile = sb([P, 2, 1024], U8, f"w2raw{a}", f"hb0_{a}")
+            nc.sync.dma_start(tile[:].bitcast(I32), w2_words[2 * a : 2 * a + 2].rearrange("e s p c -> p (e s) c").bitcast(I32))
+            w2w.append(tile)
+        first_layer(1, 1, 0)
+        first[0].extend(load_words(w1_words, 3, "w1_", "gw1_0_0"))
+        first_layer(1, 1, 1)
+        first[1].extend(load_words(wp_words, 3, "wp_", "gw1_0_1"))
+        load_planes(w2s, w2_scales)
+        hq1 = activate(1, (0, 1))
+        gather_scales(2, 0)
+        gather_scales(2, 1)
+        move_scales(2)
+        first_layer(2, 0, 0)
+        first_layer(2, 0, 1)
+        gather_scales(3, 0)
+        gather_scales(3, 1)
+        move_scales(3)
         gates = []
         for r in range(2):
-            tile = sb([P, T], F32, f"gate{r}", 4096 * r)
+            tile = sb([P, T], F32, f"gate{r}", f"hb1_{r}")
             nc.sync.dma_start(tile[:], gate[r])
             gates.append(tile)
-        hq1 = activate(C, sums1, 30720)
-        sums2 = open_sums(2 * C, C)
-        first_layer(2 * C, sums2, (0,), 0, None)
-        gather_scales(3, 15936, None)
-        deal_second(0, None, None)
-        second_layer(0, hq0, on_scalar, "yp", 2)
-        first_layer(2 * C, sums2, (1,), 0, "grouped0")
-        hq2 = activate(2 * C, sums2, None)
-        second_layer(C, hq1, on_scalar, "yp", 2)
-        sums3a = open_sums(3 * C, P)
-        first_layer(3 * C, sums3a, (0, 1), 0, 30720 - 1024)
-        sums3b = open_sums(3 * C + P, P)
-        first_layer(3 * C + P, sums3b, (0, 1), 0, 30720 + 1024)
-        hq3a = activate(3 * C, sums3a, None)
-        hq3b = activate(3 * C + P, sums3b, None)
-        deal_second(2, 28672, 30720)
-        second_layer(2 * C, hq2, on_vector, "yp", 2)
-        second_layer(3 * C, hq3a, on_scalar[:1], "hp", 4)
-        second_layer(3 * C + P, hq3b, shared, "hp", 4)
+        first_layer(2, 1, 0)
+        first_layer(2, 1, 1)
+        hq2 = activate(2, (0, 1))
+        first_layer(3, 0, 0)
+        first_layer(3, 0, 1)
+        first_layer(3, 1, 0, (0,))
+        first_layer(3, 1, 1, (0,))
+        hq3a = activate(3, (0,))
+        first_layer(3, 1, 0, (1,))
+        first_layer(3, 1, 1, (1,))
+        hq3b = activate(3, (1,))
+        deal_second(0)
+        early = [quantise(hq0, "0"), quantise(hq1, "1")]
+        second_layer(0, early, "yp", 2, [nc.scalar.copy] * 4)
+        deal_second(2)
+        late = [quantise(hq2, "2"), quantise(hq3a, "3a"), quantise(hq3b, "3b")]
+        second_layer(2 * C, late, "sum", 4, [nc.vector.tensor_copy, nc.scalar.copy, nc.scalar.copy, nc.scalar.copy])
 
         out_rows = out_0.rearrange("(p t) c -> p t c", t=4)
         out_codes = sb([P, T], U32, "out_codes")
         out_plane = sb([P, T], U8, "out_plane")
         code_rows = out_1[0].rearrange("p t d -> p (t d)").bitcast(I32)
 
-        def gather_product(chunk, t, r):
-            start, width, parts, total = chunk
-            nc.vector.tensor_tensor(
-                parts[r][:, t, :],
-                y[t][:].indirect(entries(token_lists[r], start, width)),
-                gates[r][:, start : start + width],
-                MULT,
-            )
-
-        def add_up(chunk, t0, t1):
-            start, width, parts, total = chunk
-            nc.vector.tensor_tensor(total[:, t0:t1], parts[0][:, t0:t1], parts[1][:, t0:t1], ADD)
-
-        def finish(chunk, rounder, queue):
-            start, width, parts, total = chunk
-            queue.dma_start(out_rows[:, :, start : start + width], total[:])
+        for start, width in TOKEN_CHUNKS:
+            cols = slice(start, start + width)
+            total = sb([P, 4, width], F32, f"total{start}")
+            for t in range(4):
+                picked = sb([P, width], F32, f"picked{start}_{t}")
+                parts = [sb([P, width], F32, f"part{start}_{t}_{r}") for r in range(2)]
+                nc.scalar.activation(picked[:], y[t][:].indirect(entries(token_lists[1], start, width)), COPY)
+                nc.vector.tensor_tensor(parts[0][:], y[t][:].indirect(entries(token_lists[0], start, width)), gates[0][:, cols], MULT)
+                nc.vector.tensor_tensor(parts[1][:], picked[:], gates[1][:, cols], MULT)
+                nc.vector.tensor_tensor(total[:, t, :], parts[0][:], parts[1][:], ADD)
+            nc.sync.dma_start(out_rows[:, :, cols], total[:])
             rounded = sb([P, width * 4], BF16, f"rounded{start}")
+            rounder = nc.scalar.copy if start == 0 else nc.vector.tensor_copy
             rounder(
                 rounded[:].rearrange("p (c i t) -> p c t i", t=4, i=4),
                 total[:].rearrange("p t (c i) -> p c t i", i=4),
             )
-            done = 0
-            for piece in (256, 128):
-                if width - done >= piece:
-                    cols = slice(start + done, start + done + piece)
-                    nc.vector.quantize_mx(out_codes[:, cols].bitcast(FP8X4), out_plane[:, cols], rounded[:, 4 * done : 4 * (done + piece)])
-                    done = done + piece
-            nc.sync.dma_start(code_rows[:, start : start + width], out_codes[:, start : start + width].bitcast(I32))
-
-        head, tail = [
-            (start, width, [sb([P, 4, width], F32, f"part{start}_{r}") for r in range(2)], sb([P, 4, width], F32, f"total{start}"))
-            for start, width in TOKEN_CHUNKS
-        ]
-        steps = [(t, r) for t in range(4) for r in range(2)]
-        for t, r in steps:
-            gather_product(head, t, r)
-        gather_product(tail, *steps[0])
-        add_up(head, 0, 4)
-        for t, r in steps[1:-1]:
-            gather_product(tail, t, r)
-        add_up(tail, 0, 3)
-        gather_product(tail, *steps[-1])
-        finish(head, nc.scalar.copy, nc.sync)
-        add_up(tail, 3, 4)
-        finish(tail, nc.vector.tensor_copy, nc.scalar)
+            nc.vector.quantize_mx(out_codes[:, cols].bitcast(FP8X4), out_plane[:, cols], rounded[:])
+            nc.sync.dma_start(code_rows[:, cols], out_codes[:, cols].bitcast(I32))
         scale_rows = out_2[0].bitcast(I32)
         for r in range(4):
             queue = nc.sync if r % 2 else nc.scalar

@@ -48,66 +48,66 @@ def tile_moe_duo_gelu_kernel(
             for r in range(4):
                 nc.sync.dma_start(plane[r:P:32].bitcast(I32), rows[r:16:4])
 
-        def load_words(words, e, name, tag=None):
-            tile = sb([P, PASSES, 1024], U8, f"{name}{e}", tag)
-            nc.sync.dma_start(tile[:].bitcast(I32), words[e].rearrange("s p c -> p s c").bitcast(I32))
-            return [tile]
+        def load_words(words, e0, name):
+            tile = sb([P, 2, words.shape[1], 1024], U8, f"{name}{e0}")
+            nc.sync.dma_start(
+                tile[:].rearrange("p e s c -> p (e s) c").bitcast(I32),
+                words[e0 : e0 + 2].rearrange("e s p c -> p (e s) c").bitcast(I32),
+            )
+            return [tile[:, a] for a in range(2)]
 
         def entries(lst, start, count):
             return lst[:, start // STRIPE : (start + count) // STRIPE]
 
         xs = sb([P, T], U8, "xs")
         first_scales = [sb([P, E * PASSES, H], U8, f"first_scales{l}") for l in range(2)]
-        w2s = first_scales[0][:, 0:E]
-        moved = [sb([P, 2, C], U8, f"moved{a}") for a in range(2)]
+        w2s = sb([P, E, N], U8, "w2s")
+        moved = [sb([P, 2, 2, C], U8, f"moved{a}") for a in range(2)]
         nc.gpsimd.memset(xs[:].bitcast(I32), 0)
         nc.vector.memset(first_scales[0][:].bitcast(I32), 0)
         nc.gpsimd.memset(first_scales[1][:].bitcast(I32), 0)
         for tile in moved:
             nc.vector.memset(tile[:].bitcast(I32), 0)
+        nc.vector.memset(w2s[:].bitcast(I32), 0)
 
         slot_lists = [load_list(offs, "offs_sb")]
         for q in range(4):
             nc.sync.dma_start(xs[:].bitcast(I32)[32 * q : 32 * q + 8], x_scales[:, 4 * q : 4 * q + 4, :].bitcast(I32))
-        xw = [sb([P, T], I32, f"xw{s}") for s in range(PASSES)]
-        x_rows = x_words.rearrange("s p t d -> s p (t d)").bitcast(I32)
-        nc.sync.dma_start(xw[0][:], x_rows[0])
+        xw = sb([P, PASSES, T], I32, "xw")
+        nc.sync.dma_start(xw[:], x_words.rearrange("s p t d -> p s (t d)").bitcast(I32))
         slot_lists.append(load_list(offs2, "offs2_sb"))
-        nc.sync.dma_start(xw[1][:], x_rows[1])
         first = [load_words(w1_words, 0, "w1_")]
         load_planes(first_scales[0], w1_scales)
-        first.append(load_words(wp_words, 0, "wp_"))
         load_planes(first_scales[1], wp_scales)
+        first.append(load_words(wp_words, 0, "wp_"))
 
         ident = sb([P, P], F32, "ident")
         make_identity(nc, ident[:])
 
         y = [sb([P, S], F32, f"y{t}") for t in range(4)]
-        direct = {}
+        direct = [sb([P, 2, 2, C], U8, f"direct{a}") for a in range(2)]
 
         def gather_scales(e, l):
-            if l == 0:
-                direct[e] = sb([P, 2, C], U8, f"direct{e}")
-            nc.vector.tensor_copy(direct[e][:, l, :], xs[:].indirect(entries(slot_lists[l], e * C, C)))
+            nc.vector.tensor_copy(direct[e // 2][:, e % 2, l, :], xs[:].indirect(entries(slot_lists[l], e * C, C)))
 
-        def move_scales(e):
-            src = direct[e][:].rearrange("p l c -> p (l c)").bitcast(I32)
-            dst = moved[e % 2][:].rearrange("p l c -> p (l c)").bitcast(I32)
+        def move_scales(a):
+            src = direct[a][:].rearrange("p e l c -> p (e l c)").bitcast(I32)
+            dst = moved[a][:].rearrange("p e l c -> p (e l c)").bitcast(I32)
             for p0, count in ((0, 64), (64, 4), (96, 4)):
                 nc.sync.dma_start(dst[p0 : p0 + count], src[p0 + 4 : p0 + 4 + count])
 
         sums = {}
         gathered = {}
 
-        def first_layer(e, s, l, blocks=(0, 1)):
+        def first_layer(e, s, l, blocks=(0, 1), tag=None):
             if (e, s, l) not in gathered:
-                gathered[e, s, l] = sb([P, C], U32, f"gw{e}_{s}_{l}")
+                gathered[e, s, l] = sb([P, C], U32, f"gw{e}_{s}_{l}", tag)
             cols = slice(blocks[0] * P, (blocks[-1] + 1) * P)
             nc.vector.tensor_copy(
                 gathered[e, s, l][:, cols],
-                xw[s][:].bitcast(U32).indirect(entries(slot_lists[l], e * C + cols.start, cols.stop - cols.start)),
+                xw[:, s, :].bitcast(U32).indirect(entries(slot_lists[l], e * C + cols.start, cols.stop - cols.start)),
             )
-            scales = moved[e % 2] if s else direct[e]
+            scales = (direct, moved)[s][e // 2][:, e % 2]
             for b in blocks:
                 if (e, b) not in sums:
                     sums[e, b] = psum.tile([P, H], F32, name=f"sum{e}_{b}", tag="sum", bufs=4)
@@ -142,9 +142,9 @@ def tile_moe_duo_gelu_kernel(
 
         second = {}
 
-        def deal_second(e0):
-            words = sb([P, 2, 1024], U8, f"w2w{e0}")
-            scales = sb([P, 2, N], U8, f"w2p{e0}")
+        def deal_second(e0, words_tag=None, scales_tag=None):
+            words = sb([P, 2, 1024], U8, f"w2w{e0}", words_tag)
+            scales = sb([P, 2, N], U8, f"w2p{e0}", scales_tag)
             nc.vector.tensor_copy(
                 words[:].bitcast(U16).rearrange("p e (t c i) -> p e c t i", t=4, i=8),
                 w2w[e0 // 2][:].bitcast(U16).rearrange("p e (c i t) -> p e c t i", t=4, i=8),
@@ -156,9 +156,9 @@ def tile_moe_duo_gelu_kernel(
             for a in range(2):
                 second[e0 + a] = (words[:, a, :], scales[:, a, :])
 
-        def quantise(hq, name):
+        def quantise(hq, name, tag=None):
             width = hq.shape[1] // 4
-            codes = sb([P, width], U32, f"hc{name}")
+            codes = sb([P, width], U32, f"hc{name}", tag)
             plane = sb([P, width], U8, f"hs{name}")
             nc.vector.quantize_mx(codes[:].bitcast(FP8X4), plane[:], hq[:])
             return codes, plane
@@ -189,56 +189,45 @@ def tile_moe_duo_gelu_kernel(
         for e in range(2):
             for l in range(2):
                 gather_scales(e, l)
+                if e == 1 and l == 1:
+                    move_scales(0)
                 first_layer(e, 0, l)
-            move_scales(e)
-            if e == 0:
-                first[0].extend(load_words(w1_words, 1, "w1_"))
-                first[1].extend(load_words(wp_words, 1, "wp_"))
+        first[0].extend(load_words(w1_words, 2, "w1_"))
+        first[1].extend(load_words(wp_words, 2, "wp_"))
+        w2w = [sb([P, 2, 1024], U8, f"w2raw{a}") for a in range(2)]
+        for a in range(2):
+            nc.sync.dma_start(w2w[a][:].bitcast(I32), w2_words[2 * a : 2 * a + 2].rearrange("e s p c -> p (e s) c").bitcast(I32))
+        load_planes(w2s, w2_scales)
+        gates = sb([P, 2, T], F32, "gates")
+        nc.sync.dma_start(gates[:], gate.rearrange("r p t -> p r t"))
         token_lists = [load_list(pos1, "pos1_sb"), load_list(pos2, "pos2_sb")]
         first_layer(0, 1, 0)
-        first[0].extend(load_words(w1_words, 2, "w1_", "gw0_0_0"))
         first_layer(0, 1, 1)
-        first[1].extend(load_words(wp_words, 2, "wp_", "gw0_0_1"))
         hq0 = activate(0, (0, 1))
-        w2w = []
-        for a in range(2):
-            tile = sb([P, 2, 1024], U8, f"w2raw{a}", f"hb0_{a}")
-            nc.sync.dma_start(tile[:].bitcast(I32), w2_words[2 * a : 2 * a + 2].rearrange("e s p c -> p (e s) c").bitcast(I32))
-            w2w.append(tile)
-        first_layer(1, 1, 0)
-        first[0].extend(load_words(w1_words, 3, "w1_", "gw1_0_0"))
-        first_layer(1, 1, 1)
-        first[1].extend(load_words(wp_words, 3, "wp_", "gw1_0_1"))
-        load_planes(w2s, w2_scales)
-        hq1 = activate(1, (0, 1))
         gather_scales(2, 0)
         gather_scales(2, 1)
-        move_scales(2)
-        first_layer(2, 0, 0)
-        first_layer(2, 0, 1)
+        first_layer(1, 1, 0)
         gather_scales(3, 0)
+        first_layer(1, 1, 1)
         gather_scales(3, 1)
-        move_scales(3)
-        gates = []
-        for r in range(2):
-            tile = sb([P, T], F32, f"gate{r}", f"hb1_{r}")
-            nc.sync.dma_start(tile[:], gate[r])
-            gates.append(tile)
+        move_scales(1)
+        hq1 = activate(1, (0, 1))
+        for e in (2, 3):
+            first_layer(e, 0, 0)
+            first_layer(e, 0, 1)
         first_layer(2, 1, 0)
         first_layer(2, 1, 1)
         hq2 = activate(2, (0, 1))
-        first_layer(3, 0, 0)
-        first_layer(3, 0, 1)
-        first_layer(3, 1, 0, (0,))
+        deal_second(0)
+        first_layer(3, 1, 0, (0,), "w2raw0")
         first_layer(3, 1, 1, (0,))
         hq3a = activate(3, (0,))
         first_layer(3, 1, 0, (1,))
         first_layer(3, 1, 1, (1,))
         hq3b = activate(3, (1,))
-        deal_second(0)
-        early = [quantise(hq0, "0"), quantise(hq1, "1")]
+        early = [quantise(hq0, "0", "gw3_1_1"), quantise(hq1, "1")]
         second_layer(0, early, "yp", 2, [nc.scalar.copy] * 4)
-        deal_second(2)
+        deal_second(2, "hq0_0", "gw3_0_1")
         late = [quantise(hq2, "2"), quantise(hq3a, "3a"), quantise(hq3b, "3b")]
         second_layer(2 * C, late, "sum", 4, [nc.vector.tensor_copy, nc.scalar.copy, nc.scalar.copy, nc.scalar.copy])
 
@@ -254,8 +243,8 @@ def tile_moe_duo_gelu_kernel(
                 picked = sb([P, width], F32, f"picked{start}_{t}")
                 parts = [sb([P, width], F32, f"part{start}_{t}_{r}") for r in range(2)]
                 nc.scalar.activation(picked[:], y[t][:].indirect(entries(token_lists[1], start, width)), COPY)
-                nc.vector.tensor_tensor(parts[0][:], y[t][:].indirect(entries(token_lists[0], start, width)), gates[0][:, cols], MULT)
-                nc.vector.tensor_tensor(parts[1][:], picked[:], gates[1][:, cols], MULT)
+                nc.vector.tensor_tensor(parts[0][:], y[t][:].indirect(entries(token_lists[0], start, width)), gates[:, 0, cols], MULT)
+                nc.vector.tensor_tensor(parts[1][:], picked[:], gates[:, 1, cols], MULT)
                 nc.vector.tensor_tensor(total[:, t, :], parts[0][:], parts[1][:], ADD)
             nc.sync.dma_start(out_rows[:, :, cols], total[:])
             rounded = sb([P, width * 4], BF16, f"rounded{start}")

@@ -33,10 +33,14 @@ def tile_moe_duo_gelu_kernel(
     nc = tc.nc
     with ExitStack() as ctx:
         keep = ctx.enter_context(tc.tile_pool(name="keep", bufs=1))
+        reuse = ctx.enter_context(tc.tile_pool(name="reuse", bufs=1))
         psum = ctx.enter_context(tc.psum_pool(name="psum", bufs=1))
 
         def sb(shape, dtype, name, tag=None, bufs=1):
             return keep.tile(shape, dtype, name=name, tag=tag or name, bufs=bufs, align_bytes=64)
+
+        def placed(shape, dtype, name, offset):
+            return reuse.tile(shape, dtype, name=name, tag=name, align_bytes=64, offset=offset)
 
         def load_list(src, name):
             tile = keep.tile(list(src.shape), U16, name=name)
@@ -70,12 +74,11 @@ def tile_moe_duo_gelu_kernel(
             nc.vector.memset(tile[:].bitcast(I32), 0)
         nc.vector.memset(w2s[:].bitcast(I32), 0)
 
-        slot_lists = [load_list(offs, "offs_sb")]
+        slot_lists = [load_list(offs, "offs_sb"), load_list(offs2, "offs2_sb")]
         for q in range(4):
             nc.sync.dma_start(xs[:].bitcast(I32)[32 * q : 32 * q + 8], x_scales[:, 4 * q : 4 * q + 4, :].bitcast(I32))
         xw = sb([P, PASSES, T], I32, "xw")
         nc.sync.dma_start(xw[:], x_words.rearrange("s p t d -> p s (t d)").bitcast(I32))
-        slot_lists.append(load_list(offs2, "offs2_sb"))
         first = [load_words(w1_words, 0, "w1_")]
         load_planes(first_scales[0], w1_scales)
         load_planes(first_scales[1], wp_scales)
@@ -85,7 +88,7 @@ def tile_moe_duo_gelu_kernel(
         make_identity(nc, ident[:])
 
         y = [sb([P, S], F32, f"y{t}") for t in range(4)]
-        direct = [sb([P, 2, 2, C], U8, f"direct{a}") for a in range(2)]
+        direct = [sb([P, 2, 2, C], U8, "direct0")]
 
         def gather_scales(e, l):
             nc.vector.tensor_copy(direct[e // 2][:, e % 2, l, :], xs[:].indirect(entries(slot_lists[l], e * C, C)))
@@ -99,14 +102,16 @@ def tile_moe_duo_gelu_kernel(
         sums = {}
         gathered = {}
 
-        def first_layer(e, s, l, blocks=(0, 1), tag=None):
+        def gather_words(e, s, l, blocks=(0, 1)):
             if (e, s, l) not in gathered:
-                gathered[e, s, l] = sb([P, C], U32, f"gw{e}_{s}_{l}", tag)
+                gathered[e, s, l] = sb([P, C], U32, f"gw{e}_{s}_{l}")[:]
             cols = slice(blocks[0] * P, (blocks[-1] + 1) * P)
             nc.vector.tensor_copy(
                 gathered[e, s, l][:, cols],
                 xw[:, s, :].bitcast(U32).indirect(entries(slot_lists[l], e * C + cols.start, cols.stop - cols.start)),
             )
+
+        def multiply(e, s, l, blocks=(0, 1)):
             scales = (direct, moved)[s][e // 2][:, e % 2]
             for b in blocks:
                 if (e, b) not in sums:
@@ -120,6 +125,10 @@ def tile_moe_duo_gelu_kernel(
                     start=(s == 0 and l == 0),
                     stop=(s == 1 and l == 1),
                 )
+
+        def first_layer(e, s, l, blocks=(0, 1)):
+            gather_words(e, s, l, blocks)
+            multiply(e, s, l, blocks)
 
         def activate(e, blocks):
             turned = psum.tile([P, len(blocks), 2, P], F32, name=f"turned{e}_{blocks[0]}", tag="turned", bufs=2)
@@ -142,9 +151,9 @@ def tile_moe_duo_gelu_kernel(
 
         second = {}
 
-        def deal_second(e0, words_tag=None, scales_tag=None):
+        def deal_second(e0, words_tag=None, scales_at=None):
             words = sb([P, 2, 1024], U8, f"w2w{e0}", words_tag)
-            scales = sb([P, 2, N], U8, f"w2p{e0}", scales_tag)
+            scales = sb([P, 2, N], U8, f"w2p{e0}") if scales_at is None else placed([P, 2, N], U8, f"w2p{e0}", scales_at)
             nc.vector.tensor_copy(
                 words[:].bitcast(U16).rearrange("p e (t c i) -> p e c t i", t=4, i=8),
                 w2w[e0 // 2][:].bitcast(U16).rearrange("p e (c i t) -> p e c t i", t=4, i=8),
@@ -156,9 +165,9 @@ def tile_moe_duo_gelu_kernel(
             for a in range(2):
                 second[e0 + a] = (words[:, a, :], scales[:, a, :])
 
-        def quantise(hq, name, tag=None):
+        def quantise(hq, name, offset=None):
             width = hq.shape[1] // 4
-            codes = sb([P, width], U32, f"hc{name}", tag)
+            codes = sb([P, width], U32, f"hc{name}") if offset is None else placed([P, width], U32, f"hc{name}", offset)
             plane = sb([P, width], U8, f"hs{name}")
             nc.vector.quantize_mx(codes[:].bitcast(FP8X4), plane[:], hq[:])
             return codes, plane
@@ -189,9 +198,10 @@ def tile_moe_duo_gelu_kernel(
         for e in range(2):
             for l in range(2):
                 gather_scales(e, l)
-                if e == 1 and l == 1:
-                    move_scales(0)
-                first_layer(e, 0, l)
+        move_scales(0)
+        gathered[0, 0, 0] = placed([P, C], U32, "gw_first", 960)[:]
+        first_layer(0, 0, 0)
+        first_layer(0, 0, 1)
         first[0].extend(load_words(w1_words, 2, "w1_"))
         first[1].extend(load_words(wp_words, 2, "wp_"))
         w2w = [sb([P, 2, 1024], U8, f"w2raw{a}") for a in range(2)]
@@ -201,33 +211,40 @@ def tile_moe_duo_gelu_kernel(
         gates = sb([P, 2, T], F32, "gates")
         nc.sync.dma_start(gates[:], gate.rearrange("r p t -> p r t"))
         token_lists = [load_list(pos1, "pos1_sb"), load_list(pos2, "pos2_sb")]
-        first_layer(0, 1, 0)
-        first_layer(0, 1, 1)
-        hq0 = activate(0, (0, 1))
+        first_layer(1, 0, 0)
+        direct.append(placed([P, 2, 2, C], U8, "direct1", 0))
+        later = [(e, s, l) for e in range(E) for s in range(PASSES) for l in range(2) if (e, s, l) not in gathered]
+        behind = placed([P, len(later), C], U32, "gw_behind", 1024)
+        for a, key in enumerate(later):
+            gathered[key] = behind[:, a, :]
         gather_scales(2, 0)
+        first_layer(1, 0, 1)
         gather_scales(2, 1)
-        first_layer(1, 1, 0)
+        first_layer(0, 1, 0)
         gather_scales(3, 0)
-        first_layer(1, 1, 1)
+        first_layer(0, 1, 1)
         gather_scales(3, 1)
         move_scales(1)
+        hq0 = activate(0, (0, 1))
+        first_layer(1, 1, 0)
+        first_layer(1, 1, 1)
         hq1 = activate(1, (0, 1))
-        for e in (2, 3):
-            first_layer(e, 0, 0)
-            first_layer(e, 0, 1)
-        first_layer(2, 1, 0)
-        first_layer(2, 1, 1)
+        for s in range(PASSES):
+            first_layer(2, s, 0)
+            first_layer(2, s, 1)
         hq2 = activate(2, (0, 1))
-        deal_second(0)
-        first_layer(3, 1, 0, (0,), "w2raw0")
+        first_layer(3, 0, 0)
+        first_layer(3, 0, 1)
+        first_layer(3, 1, 0, (0,))
         first_layer(3, 1, 1, (0,))
         hq3a = activate(3, (0,))
         first_layer(3, 1, 0, (1,))
         first_layer(3, 1, 1, (1,))
         hq3b = activate(3, (1,))
-        early = [quantise(hq0, "0", "gw3_1_1"), quantise(hq1, "1")]
+        deal_second(0)
+        early = [quantise(hq0, "0", 1024), quantise(hq1, "1")]
         second_layer(0, early, "yp", 2, [nc.scalar.copy] * 4)
-        deal_second(2, "hq0_0", "gw3_0_1")
+        deal_second(2, "hq0_0", 0)
         late = [quantise(hq2, "2"), quantise(hq3a, "3a"), quantise(hq3b, "3b")]
         second_layer(2 * C, late, "sum", 4, [nc.vector.tensor_copy, nc.scalar.copy, nc.scalar.copy, nc.scalar.copy])
 

@@ -23,7 +23,7 @@ ADD = mybir.AluOpType.add
 P = 128
 PASSES = K // 512
 STRIPE = 16
-TOKEN_CHUNKS = ((0, 384), (384, 128))
+HALF = T // 2
 
 
 def tile_moe_duo_gelu_kernel(
@@ -93,11 +93,11 @@ def tile_moe_duo_gelu_kernel(
         def gather_scales(e, l):
             nc.vector.tensor_copy(direct[e // 2][:, e % 2, l, :], xs[:].indirect(entries(slot_lists[l], e * C, C)))
 
-        def move_scales(a):
-            src = direct[a][:].rearrange("p e l c -> p (e l c)").bitcast(I32)
-            dst = moved[a][:].rearrange("p e l c -> p (e l c)").bitcast(I32)
-            for p0, count in ((0, 64), (64, 4), (96, 4)):
-                nc.sync.dma_start(dst[p0 : p0 + count], src[p0 + 4 : p0 + 4 + count])
+        def move_scales(e0, count):
+            src = direct[e0 // 2][:, e0 % 2 : e0 % 2 + count].rearrange("p e l c -> p (e l c)").bitcast(I32)
+            dst = moved[e0 // 2][:, e0 % 2 : e0 % 2 + count].rearrange("p e l c -> p (e l c)").bitcast(I32)
+            for p0, rows in ((0, 64), (64, 4), (96, 4)):
+                nc.sync.dma_start(dst[p0 : p0 + rows], src[p0 + 4 : p0 + 4 + rows])
 
         sums = {}
         gathered = {}
@@ -130,21 +130,24 @@ def tile_moe_duo_gelu_kernel(
             gather_words(e, s, l, blocks)
             multiply(e, s, l, blocks)
 
-        def activate(e, blocks):
-            turned = psum.tile([P, len(blocks), 2, P], F32, name=f"turned{e}_{blocks[0]}", tag="turned", bufs=2)
-            for a, b in enumerate(blocks):
-                hb = sb([P, H], BF16, f"hb{e}_{b}")
-                nc.scalar.activation(
-                    hb[:].rearrange("s (u p d) -> s u p d", u=2, d=2),
-                    sums[e, b][:].rearrange("s (p u d) -> s u p d", u=2, d=2),
-                    GELU,
-                )
+        def activate(e, b):
+            hb = sb([P, H], BF16, f"hb{e}_{b}")
+            nc.scalar.activation(
+                hb[:].rearrange("s (u p d) -> s u p d", u=2, d=2),
+                sums[e, b][:].rearrange("s (p u d) -> s u p d", u=2, d=2),
+                GELU,
+            )
+            return hb
+
+        def turn(tiles, name, copier):
+            turned = psum.tile([P, len(tiles), 2, P], F32, name=f"turned{name}", tag="turned", bufs=2)
+            for a, hb in reversed(list(enumerate(tiles))):
                 pairs = hb[:].bitcast(F32)
                 for u in range(2):
                     nc.tensor.transpose(turned[:, a, u, :], pairs[:, u * P : (u + 1) * P], ident[:])
-            hq = sb([P, len(blocks) * H], BF16, f"hq{e}_{blocks[0]}")
-            nc.scalar.copy(
-                hq[:].bitcast(F32).rearrange("p (b s u) -> p b s u", b=len(blocks), u=2),
+            hq = sb([P, len(tiles) * H], BF16, f"hq{name}")
+            copier(
+                hq[:].bitcast(F32).rearrange("p (b s u) -> p b s u", b=len(tiles), u=2),
                 turned[:].rearrange("p b u s -> p b s u"),
             )
             return hq
@@ -184,10 +187,10 @@ def tile_moe_duo_gelu_kernel(
                 stop=True,
             )
 
-        def second_layer(start, operands, tag, bufs, copiers):
+        def second_layer(start, operands, banks, copiers):
             width = sum(op[0].shape[1] for op in operands)
             for t in range(4):
-                bank = psum.tile([P, width], F32, name=f"yp{start}_{t}", tag=tag, bufs=bufs)
+                bank = psum.tile([P, width], F32, name=f"yp{start}_{t}", tag=banks[t][0], bufs=banks[t][1])
                 done = 0
                 for op in operands:
                     w = op[0].shape[1]
@@ -198,7 +201,7 @@ def tile_moe_duo_gelu_kernel(
         for e in range(2):
             for l in range(2):
                 gather_scales(e, l)
-        move_scales(0)
+        move_scales(0, 2)
         gathered[0, 0, 0] = placed([P, C], U32, "gw_first", 960)[:]
         first_layer(0, 0, 0)
         first_layer(0, 0, 1)
@@ -217,61 +220,103 @@ def tile_moe_duo_gelu_kernel(
         behind = placed([P, len(later), C], U32, "gw_behind", 1024)
         for a, key in enumerate(later):
             gathered[key] = behind[:, a, :]
-        gather_scales(2, 0)
         first_layer(1, 0, 1)
+        hq = []
+        for e in range(2):
+            first_layer(e, 1, 0)
+            first_layer(e, 1, 1)
+            hq.append(turn([activate(e, 0), activate(e, 1)], f"{e}", nc.scalar.copy))
+        gather_scales(2, 0)
         gather_scales(2, 1)
-        first_layer(0, 1, 0)
+        move_scales(2, 1)
+        first_layer(2, 0, 0)
+        first_layer(2, 0, 1)
         gather_scales(3, 0)
-        first_layer(0, 1, 1)
         gather_scales(3, 1)
-        move_scales(1)
-        hq0 = activate(0, (0, 1))
-        first_layer(1, 1, 0)
-        first_layer(1, 1, 1)
-        hq1 = activate(1, (0, 1))
-        for s in range(PASSES):
-            first_layer(2, s, 0)
-            first_layer(2, s, 1)
-        hq2 = activate(2, (0, 1))
+        move_scales(3, 1)
         first_layer(3, 0, 0)
         first_layer(3, 0, 1)
-        first_layer(3, 1, 0, (0,))
-        first_layer(3, 1, 1, (0,))
-        hq3a = activate(3, (0,))
-        first_layer(3, 1, 0, (1,))
-        first_layer(3, 1, 1, (1,))
-        hq3b = activate(3, (1,))
+        first_layer(2, 1, 0)
+        first_layer(2, 1, 1)
+        hq.append(turn([activate(2, 0), activate(2, 1)], "2", nc.vector.tensor_copy))
+        for b in range(2):
+            first_layer(3, 1, 0, (b,))
+            first_layer(3, 1, 1, (b,))
+            hq.append(turn([activate(3, b)], f"3_{b}", nc.scalar.copy))
         deal_second(0)
-        early = [quantise(hq0, "0", 1024), quantise(hq1, "1")]
-        second_layer(0, early, "yp", 2, [nc.scalar.copy] * 4)
-        deal_second(2, "hq0_0", 0)
-        late = [quantise(hq2, "2"), quantise(hq3a, "3a"), quantise(hq3b, "3b")]
-        second_layer(2 * C, late, "sum", 4, [nc.vector.tensor_copy, nc.scalar.copy, nc.scalar.copy, nc.scalar.copy])
+        early = [quantise(hq[0], "0", 1024), quantise(hq[1], "1")]
+        second_layer(0, early, [("yp", 2)] * 2 + [("sum", 4)] * 2, [nc.scalar.copy] * 4)
+        deal_second(2, "hq0", 0)
+        late = [quantise(hq[2], "2"), quantise(hq[3], "3a"), quantise(hq[4], "3b")]
+        second_layer(2 * C, late, [("sum", 4)] * 2 + [("turned", 2)] * 2, [nc.vector.tensor_copy, nc.scalar.copy, nc.scalar.copy, nc.scalar.copy])
 
         out_rows = out_0.rearrange("(p t) c -> p t c", t=4)
         out_codes = sb([P, T], U32, "out_codes")
         out_plane = sb([P, T], U8, "out_plane")
         code_rows = out_1[0].rearrange("p t d -> p (t d)").bitcast(I32)
 
-        for start, width in TOKEN_CHUNKS:
-            cols = slice(start, start + width)
-            total = sb([P, 4, width], F32, f"total{start}")
-            for t in range(4):
-                picked = sb([P, width], F32, f"picked{start}_{t}")
-                parts = [sb([P, width], F32, f"part{start}_{t}_{r}") for r in range(2)]
-                nc.scalar.activation(picked[:], y[t][:].indirect(entries(token_lists[1], start, width)), COPY)
-                nc.vector.tensor_tensor(parts[0][:], y[t][:].indirect(entries(token_lists[0], start, width)), gates[:, 0, cols], MULT)
-                nc.vector.tensor_tensor(parts[1][:], picked[:], gates[:, 1, cols], MULT)
-                nc.vector.tensor_tensor(total[:, t, :], parts[0][:], parts[1][:], ADD)
-            nc.sync.dma_start(out_rows[:, :, cols], total[:])
-            rounded = sb([P, width * 4], BF16, f"rounded{start}")
-            rounder = nc.scalar.copy if start == 0 else nc.vector.tensor_copy
+        picked = [sb([P, 2, 4, HALF], F32, f"picked{h}") for h in range(2)]
+        products = [sb([P, 2, 4, HALF], F32, f"products{h}") for h in range(2)]
+
+        def column(h, r, t):
+            return y[t][:].indirect(entries(token_lists[r], h * HALF, HALF))
+
+        def pick(h, r, t):
+            nc.scalar.activation(picked[h][:, r, t, :], column(h, r, t), COPY)
+
+        def pick_and_weigh(h, t):
+            nc.vector.tensor_tensor(products[h][:, 0, t, :], column(h, 0, t), gates[:, 0, h * HALF : (h + 1) * HALF], MULT)
+
+        def weigh(h, r, t0, t1):
+            weights = gates[:, r : r + 1, h * HALF : (h + 1) * HALF].to_broadcast([P, t1 - t0, HALF])
+            nc.vector.tensor_tensor(products[h][:, r, t0:t1, :], picked[h][:, r, t0:t1, :], weights, MULT)
+
+        def add_up(total, start, t0, t1):
+            h, cols = start // HALF, slice(start % HALF, start % HALF + total.shape[2])
+            nc.vector.tensor_tensor(total[:, t0:t1, :], products[h][:, 0, t0:t1, cols], products[h][:, 1, t0:t1, cols], ADD)
+
+        def store_and_round(total, start, rounder):
+            width = total.shape[2]
+            nc.sync.dma_start(out_rows[:, :, start : start + width], total[:])
             rounder(
-                rounded[:].rearrange("p (c i t) -> p c t i", t=4, i=4),
+                rounded[:, 4 * start : 4 * (start + width)].rearrange("p (c i t) -> p c t i", t=4, i=4),
                 total[:].rearrange("p t (c i) -> p c t i", i=4),
             )
-            nc.vector.quantize_mx(out_codes[:, cols].bitcast(FP8X4), out_plane[:, cols], rounded[:])
-            nc.sync.dma_start(code_rows[:, cols], out_codes[:, cols].bitcast(I32))
+
+        def hand_on(h, queue):
+            cols = slice(h * HALF, (h + 1) * HALF)
+            nc.vector.quantize_mx(out_codes[:, cols].bitcast(FP8X4), out_plane[:, cols], rounded[:, 4 * cols.start : 4 * cols.stop])
+            queue.dma_start(code_rows[:, cols], out_codes[:, cols].bitcast(I32))
+
+        rounded = sb([P, 4 * T], BF16, "rounded")
+        starts = (0, HALF, HALF + P)
+        totals = [sb([P, 4, width], F32, f"total{start}") for start, width in zip(starts, (HALF, P, P))]
+        for t in range(4):
+            pick(0, 1, t)
+        pick(0, 0, 3)
+        for t in range(4):
+            pick(1, 1, t)
+        pick_and_weigh(0, 0)
+        pick_and_weigh(0, 1)
+        weigh(0, 1, 0, 2)
+        pick_and_weigh(0, 2)
+        add_up(totals[0], 0, 0, 2)
+        pick_and_weigh(1, 0)
+        weigh(0, 1, 2, 4)
+        weigh(0, 0, 3, 4)
+        pick_and_weigh(1, 1)
+        add_up(totals[0], 0, 2, 4)
+        store_and_round(totals[0], 0, nc.scalar.copy)
+        pick_and_weigh(1, 2)
+        weigh(1, 1, 0, 2)
+        pick_and_weigh(1, 3)
+        weigh(1, 1, 2, 4)
+        hand_on(0, nc.sync)
+        add_up(totals[1], starts[1], 0, 4)
+        store_and_round(totals[1], starts[1], nc.scalar.copy)
+        add_up(totals[2], starts[2], 0, 4)
+        store_and_round(totals[2], starts[2], nc.vector.tensor_copy)
+        hand_on(1, nc.scalar)
         scale_rows = out_2[0].bitcast(I32)
         for r in range(4):
             queue = nc.sync if r % 2 else nc.scalar

@@ -33,14 +33,10 @@ def tile_moe_duo_gelu_kernel(
     nc = tc.nc
     with ExitStack() as ctx:
         keep = ctx.enter_context(tc.tile_pool(name="keep", bufs=1))
-        reuse = ctx.enter_context(tc.tile_pool(name="reuse", bufs=1))
         psum = ctx.enter_context(tc.psum_pool(name="psum", bufs=1))
 
         def sb(shape, dtype, name, tag=None, bufs=1):
             return keep.tile(shape, dtype, name=name, tag=tag or name, bufs=bufs, align_bytes=64)
-
-        def placed(shape, dtype, name, offset):
-            return reuse.tile(shape, dtype, name=name, tag=name, align_bytes=64, offset=offset)
 
         def load_list(src, name):
             tile = keep.tile(list(src.shape), U16, name=name)
@@ -63,20 +59,19 @@ def tile_moe_duo_gelu_kernel(
         def entries(lst, start, count):
             return lst[:, start // STRIPE : (start + count) // STRIPE]
 
-        xs = sb([P, T], U8, "xs")
+        xs = sb([P, 2 * T], U8, "xs")
         first_scales = [sb([P, E * PASSES, H], U8, f"first_scales{l}") for l in range(2)]
         w2s = sb([P, E, N], U8, "w2s")
-        moved = [sb([P, 2, 2, C], U8, f"moved{a}") for a in range(2)]
+        moved = sb([P, 2, S], U8, "moved")
         nc.gpsimd.memset(xs[:].bitcast(I32), 0)
         nc.vector.memset(first_scales[0][:].bitcast(I32), 0)
         nc.gpsimd.memset(first_scales[1][:].bitcast(I32), 0)
-        for tile in moved:
-            nc.vector.memset(tile[:].bitcast(I32), 0)
+        nc.vector.memset(moved[:].bitcast(I32), 0)
         nc.vector.memset(w2s[:].bitcast(I32), 0)
 
         slot_lists = [load_list(offs, "offs_sb"), load_list(offs2, "offs2_sb")]
         for q in range(4):
-            nc.sync.dma_start(xs[:].bitcast(I32)[32 * q : 32 * q + 8], x_scales[:, 4 * q : 4 * q + 4, :].bitcast(I32))
+            nc.sync.dma_start(xs[:, 0:T].bitcast(I32)[32 * q : 32 * q + 8], x_scales[:, 4 * q : 4 * q + 4, :].bitcast(I32))
         xw = sb([P, PASSES, T], I32, "xw")
         nc.sync.dma_start(xw[:], x_words.rearrange("s p t d -> p s (t d)").bitcast(I32))
         first = [load_words(w1_words, 0, "w1_")]
@@ -88,16 +83,14 @@ def tile_moe_duo_gelu_kernel(
         make_identity(nc, ident[:])
 
         y = [sb([P, S], F32, f"y{t}") for t in range(4)]
-        direct = [sb([P, 2, 2, C], U8, "direct0")]
-
-        def gather_scales(e, l):
-            nc.vector.tensor_copy(direct[e // 2][:, e % 2, l, :], xs[:].indirect(entries(slot_lists[l], e * C, C)))
-
-        def move_scales(e0, count):
-            src = direct[e0 // 2][:, e0 % 2 : e0 % 2 + count].rearrange("p e l c -> p (e l c)").bitcast(I32)
-            dst = moved[e0 // 2][:, e0 % 2 : e0 % 2 + count].rearrange("p e l c -> p (e l c)").bitcast(I32)
-            for p0, rows in ((0, 64), (64, 4), (96, 4)):
-                nc.sync.dma_start(dst[p0 : p0 + rows], src[p0 + 4 : p0 + 4 + rows])
+        direct = sb([P, 2, S], U8, "direct")
+        for l in range(2):
+            for start in range(0, S, T):
+                nc.vector.tensor_copy(direct[:, l, start : start + T], xs[:].indirect(entries(slot_lists[l], start, T)))
+        src = direct[:].rearrange("p l c -> p (l c)").bitcast(I32)
+        dst = moved[:].rearrange("p l c -> p (l c)").bitcast(I32)
+        for p0, rows in ((0, 64), (64, 4), (96, 4)):
+            nc.sync.dma_start(dst[p0 : p0 + rows], src[p0 + 4 : p0 + 4 + rows])
 
         sums = {}
         gathered = {}
@@ -112,7 +105,7 @@ def tile_moe_duo_gelu_kernel(
             )
 
         def multiply(e, s, l, blocks=(0, 1)):
-            scales = (direct, moved)[s][e // 2][:, e % 2]
+            scales = (direct, moved)[s][:, :, e * C : (e + 1) * C]
             for b in blocks:
                 if (e, b) not in sums:
                     sums[e, b] = psum.tile([P, H], F32, name=f"sum{e}_{b}", tag="sum", bufs=4)
@@ -154,12 +147,12 @@ def tile_moe_duo_gelu_kernel(
 
         second = {}
 
-        def deal_second(e0, words_tag=None, scales_at=None):
+        def deal_second(e0, words_tag=None, scales_tag=None):
             words = sb([P, 2, 1024], U8, f"w2w{e0}", words_tag)
-            scales = sb([P, 2, N], U8, f"w2p{e0}") if scales_at is None else placed([P, 2, N], U8, f"w2p{e0}", scales_at)
+            scales = sb([P, 2, N], U8, f"w2p{e0}", scales_tag)
             nc.vector.tensor_copy(
                 words[:].bitcast(U16).rearrange("p e (t c i) -> p e c t i", t=4, i=8),
-                w2w[e0 // 2][:].bitcast(U16).rearrange("p e (c i t) -> p e c t i", t=4, i=8),
+                w2w[:, e0 : e0 + 2, :].bitcast(U16).rearrange("p e (c i t) -> p e c t i", t=4, i=8),
             )
             nc.vector.tensor_copy(
                 scales[:].rearrange("p e (t c i) -> p e c t i", t=4, i=16),
@@ -168,9 +161,9 @@ def tile_moe_duo_gelu_kernel(
             for a in range(2):
                 second[e0 + a] = (words[:, a, :], scales[:, a, :])
 
-        def quantise(hq, name, offset=None):
+        def quantise(hq, name, tag=None):
             width = hq.shape[1] // 4
-            codes = sb([P, width], U32, f"hc{name}") if offset is None else placed([P, width], U32, f"hc{name}", offset)
+            codes = sb([P, width], U32, f"hc{name}", tag)
             plane = sb([P, width], U8, f"hs{name}")
             nc.vector.quantize_mx(codes[:].bitcast(FP8X4), plane[:], hq[:])
             return codes, plane
@@ -198,57 +191,37 @@ def tile_moe_duo_gelu_kernel(
                     done = done + w
                 copiers[t](y[t][:, start : start + width], bank[:])
 
-        for e in range(2):
-            for l in range(2):
-                gather_scales(e, l)
-        move_scales(0, 2)
-        gathered[0, 0, 0] = placed([P, C], U32, "gw_first", 960)[:]
-        first_layer(0, 0, 0)
-        first_layer(0, 0, 1)
         first[0].extend(load_words(w1_words, 2, "w1_"))
         first[1].extend(load_words(wp_words, 2, "wp_"))
-        w2w = [sb([P, 2, 1024], U8, f"w2raw{a}") for a in range(2)]
-        for a in range(2):
-            nc.sync.dma_start(w2w[a][:].bitcast(I32), w2_words[2 * a : 2 * a + 2].rearrange("e s p c -> p (e s) c").bitcast(I32))
+        w2w = sb([P, E, 1024], U8, "w2raw")
+        nc.sync.dma_start(w2w[:].bitcast(I32), w2_words.rearrange("e s p c -> p (e s) c").bitcast(I32))
         load_planes(w2s, w2_scales)
         gates = sb([P, 2, T], F32, "gates")
         nc.sync.dma_start(gates[:], gate.rearrange("r p t -> p r t"))
         token_lists = [load_list(pos1, "pos1_sb"), load_list(pos2, "pos2_sb")]
-        first_layer(1, 0, 0)
-        direct.append(placed([P, 2, 2, C], U8, "direct1", 0))
-        later = [(e, s, l) for e in range(E) for s in range(PASSES) for l in range(2) if (e, s, l) not in gathered]
-        behind = placed([P, len(later), C], U32, "gw_behind", 1024)
-        for a, key in enumerate(later):
-            gathered[key] = behind[:, a, :]
-        first_layer(1, 0, 1)
-        hq = []
         for e in range(2):
+            first_layer(e, 0, 0)
+            first_layer(e, 0, 1)
+        hq = []
+        for e in range(3):
+            if e == 2:
+                first_layer(e, 0, 0)
+                first_layer(e, 0, 1)
             first_layer(e, 1, 0)
             first_layer(e, 1, 1)
             hq.append(turn([activate(e, 0), activate(e, 1)], f"{e}", nc.scalar.copy))
-        gather_scales(2, 0)
-        gather_scales(2, 1)
-        move_scales(2, 1)
-        first_layer(2, 0, 0)
-        first_layer(2, 0, 1)
-        gather_scales(3, 0)
-        gather_scales(3, 1)
-        move_scales(3, 1)
         first_layer(3, 0, 0)
         first_layer(3, 0, 1)
-        first_layer(2, 1, 0)
-        first_layer(2, 1, 1)
-        hq.append(turn([activate(2, 0), activate(2, 1)], "2", nc.vector.tensor_copy))
         for b in range(2):
             first_layer(3, 1, 0, (b,))
             first_layer(3, 1, 1, (b,))
             hq.append(turn([activate(3, b)], f"3_{b}", nc.scalar.copy))
         deal_second(0)
-        early = [quantise(hq[0], "0", 1024), quantise(hq[1], "1")]
-        second_layer(0, early, [("yp", 2)] * 2 + [("sum", 4)] * 2, [nc.scalar.copy] * 4)
-        deal_second(2, "hq0", 0)
+        early = [quantise(hq[0], "0"), quantise(hq[1], "1")]
+        second_layer(0, early, [("sum", 4)] * 4, [nc.vector.tensor_copy] * 2 + [nc.scalar.copy] * 2)
+        deal_second(2)
         late = [quantise(hq[2], "2"), quantise(hq[3], "3a"), quantise(hq[4], "3b")]
-        second_layer(2 * C, late, [("sum", 4)] * 2 + [("turned", 2)] * 2, [nc.vector.tensor_copy, nc.scalar.copy, nc.scalar.copy, nc.scalar.copy])
+        second_layer(2 * C, late, [("yp", 2)] * 2 + [("turned", 2)] * 2, [nc.vector.tensor_copy, nc.scalar.copy, nc.scalar.copy, nc.scalar.copy])
 
         out_rows = out_0.rearrange("(p t) c -> p t c", t=4)
         out_codes = sb([P, T], U32, "out_codes")

@@ -48,13 +48,18 @@ def tile_moe_duo_gelu_kernel(
             for r in range(4):
                 nc.sync.dma_start(plane[r:P:32].bitcast(I32), rows[r:16:4])
 
-        def load_words(words, e0, name):
-            tile = sb([P, 2, words.shape[1], 1024], U8, f"{name}{e0}")
+        first = {}
+
+        def load_words(l, e0, passes):
+            tile = sb([P, 2, len(passes), 1024], U8, f"first{l}_{e0}_{passes[0]}")
+            rows = (w1_words, wp_words)[l][e0 : e0 + 2, passes[0] : passes[-1] + 1]
             nc.sync.dma_start(
                 tile[:].rearrange("p e s c -> p (e s) c").bitcast(I32),
-                words[e0 : e0 + 2].rearrange("e s p c -> p (e s) c").bitcast(I32),
+                rows.rearrange("e s p c -> p (e s) c").bitcast(I32),
             )
-            return [tile[:, a] for a in range(2)]
+            for a in range(2):
+                for s in passes:
+                    first[l, e0 + a, s] = tile[:, a, s - passes[0], :]
 
         def entries(lst, start, count):
             return lst[:, start // STRIPE : (start + count) // STRIPE]
@@ -74,10 +79,12 @@ def tile_moe_duo_gelu_kernel(
             nc.sync.dma_start(xs[:, 0:T].bitcast(I32)[32 * q : 32 * q + 8], x_scales[:, 4 * q : 4 * q + 4, :].bitcast(I32))
         xw = sb([P, PASSES, T], I32, "xw")
         nc.sync.dma_start(xw[:], x_words.rearrange("s p t d -> p s (t d)").bitcast(I32))
-        first = [load_words(w1_words, 0, "w1_")]
+        load_words(0, 0, (0,))
+        load_words(1, 0, (0,))
         load_planes(first_scales[0], w1_scales)
         load_planes(first_scales[1], wp_scales)
-        first.append(load_words(wp_words, 0, "wp_"))
+        load_words(0, 0, (1,))
+        load_words(1, 0, (1,))
 
         ident = sb([P, P], F32, "ident")
         make_identity(nc, ident[:])
@@ -113,7 +120,7 @@ def tile_moe_duo_gelu_kernel(
                     sums[e, b][:],
                     lhsT=gathered[e, s, l][:, b * P : (b + 1) * P].bitcast(FP8X4),
                     lhsT_scale=scales[:, l, b * P : (b + 1) * P],
-                    rhs=first[l][e][:, s, :].bitcast(FP4X4),
+                    rhs=first[l, e, s].bitcast(FP4X4),
                     rhs_scale=first_scales[l][:, e * PASSES + s, :],
                     start=(s == 0 and l == 0),
                     stop=(s == 1 and l == 1),
@@ -191,8 +198,8 @@ def tile_moe_duo_gelu_kernel(
                     done = done + w
                 copiers[t](y[t][:, start : start + width], bank[:])
 
-        first[0].extend(load_words(w1_words, 2, "w1_"))
-        first[1].extend(load_words(wp_words, 2, "wp_"))
+        load_words(0, 2, (0, 1))
+        load_words(1, 2, (0, 1))
         w2w = sb([P, E, 1024], U8, "w2raw")
         nc.sync.dma_start(w2w[:].bitcast(I32), w2_words.rearrange("e s p c -> p (e s) c").bitcast(I32))
         load_planes(w2s, w2_scales)
@@ -218,7 +225,7 @@ def tile_moe_duo_gelu_kernel(
             hq.append(turn([activate(3, b)], f"3_{b}", nc.scalar.copy))
         deal_second(0)
         early = [quantise(hq[0], "0"), quantise(hq[1], "1")]
-        second_layer(0, early, [("sum", 4)] * 4, [nc.vector.tensor_copy] * 2 + [nc.scalar.copy] * 2)
+        second_layer(0, early, [("sum", 4)] * 4, [nc.vector.tensor_copy] + [nc.scalar.copy] * 3)
         deal_second(2)
         late = [quantise(hq[2], "2"), quantise(hq[3], "3a"), quantise(hq[4], "3b")]
         second_layer(2 * C, late, [("yp", 2)] * 2 + [("turned", 2)] * 2, [nc.vector.tensor_copy, nc.scalar.copy, nc.scalar.copy, nc.scalar.copy])

@@ -35,7 +35,7 @@ def tile_moe_duo_gelu_kernel(
         keep = ctx.enter_context(tc.tile_pool(name="keep", bufs=1))
         psum = ctx.enter_context(tc.psum_pool(name="psum", bufs=1))
 
-        def sb(shape, dtype, name, tag=None, bufs=1):
+        def sb(shape, dtype, name, tag=None, bufs=1, at=None):
             return keep.tile(shape, dtype, name=name, tag=tag or name, bufs=bufs, align_bytes=64)
 
         def load_list(src, name):
@@ -67,11 +67,12 @@ def tile_moe_duo_gelu_kernel(
         xs = sb([P, 2 * T], U8, "xs")
         first_scales = [sb([P, E * PASSES, H], U8, f"first_scales{l}") for l in range(2)]
         w2s = sb([P, E, N], U8, "w2s")
-        moved = sb([P, 2, S], U8, "moved")
+        moved = [sb([P, 2 * T], U8, f"moved{g}") for g in range(2)]
         nc.gpsimd.memset(xs[:].bitcast(I32), 0)
         nc.vector.memset(first_scales[0][:].bitcast(I32), 0)
         nc.gpsimd.memset(first_scales[1][:].bitcast(I32), 0)
-        nc.vector.memset(moved[:].bitcast(I32), 0)
+        for g in range(2):
+            nc.vector.memset(moved[g][:].bitcast(I32), 0)
         nc.vector.memset(w2s[:].bitcast(I32), 0)
 
         slot_lists = [load_list(offs, "offs_sb"), load_list(offs2, "offs2_sb")]
@@ -90,45 +91,55 @@ def tile_moe_duo_gelu_kernel(
         make_identity(nc, ident[:])
 
         y = [sb([P, S], F32, f"y{t}") for t in range(4)]
-        direct = sb([P, 2, S], U8, "direct")
-        for l in range(2):
-            for start in range(0, S, T):
-                nc.vector.tensor_copy(direct[:, l, start : start + T], xs[:].indirect(entries(slot_lists[l], start, T)))
-        src = direct[:].rearrange("p l c -> p (l c)").bitcast(I32)
-        dst = moved[:].rearrange("p l c -> p (l c)").bitcast(I32)
-        for p0, rows in ((0, 64), (64, 4), (96, 4)):
-            nc.sync.dma_start(dst[p0 : p0 + rows], src[p0 + 4 : p0 + 4 + rows])
+        direct = {}
+
+        def gather_scales(g, lists, tag=None):
+            tile = sb([P, len(lists) * T], U8, f"direct{g}_{lists[0]}", tag)
+            for a, l in enumerate(lists):
+                direct[g, l] = tile[:, a * T : (a + 1) * T]
+                nc.vector.tensor_copy(direct[g, l], xs[:].indirect(entries(slot_lists[l], g * T, T)))
+            src = tile[:].bitcast(I32)
+            dst = moved[g][:, lists[0] * T : (lists[-1] + 1) * T].bitcast(I32)
+            for p0, rows in ((0, 64), (64, 4), (96, 4)):
+                nc.sync.dma_start(dst[p0 : p0 + rows], src[p0 + 4 : p0 + 4 + rows])
+
+        def bank(name, which, shape):
+            return psum.tile(shape, F32, name=name, tag=f"bank{which}", bufs=1)
 
         sums = {}
         gathered = {}
 
+        def room(units, tag=None, at=None):
+            tile = sb([P, len(units) * C], U32, f"gw{units[0][0]}_{units[0][1]}_{units[0][2]}", tag, at=at)
+            for a, unit in enumerate(units):
+                gathered[unit] = tile[:, a * C : (a + 1) * C]
+
         def gather_words(e, s, l, blocks=(0, 1)):
-            if (e, s, l) not in gathered:
-                gathered[e, s, l] = sb([P, C], U32, f"gw{e}_{s}_{l}")[:]
             cols = slice(blocks[0] * P, (blocks[-1] + 1) * P)
             nc.vector.tensor_copy(
                 gathered[e, s, l][:, cols],
                 xw[:, s, :].bitcast(U32).indirect(entries(slot_lists[l], e * C + cols.start, cols.stop - cols.start)),
             )
 
+        def first_layer(e, s, l, blocks=(0, 1)):
+            gather_words(e, s, l, blocks)
+            multiply(e, s, l, blocks)
+
         def multiply(e, s, l, blocks=(0, 1)):
-            scales = (direct, moved)[s][:, :, e * C : (e + 1) * C]
+            plane = direct[e // 2, l] if s == 0 else moved[e // 2][:, l * T : (l + 1) * T]
+            scales = plane[:, (e % 2) * C : (e % 2 + 1) * C]
             for b in blocks:
                 if (e, b) not in sums:
-                    sums[e, b] = psum.tile([P, H], F32, name=f"sum{e}_{b}", tag="sum", bufs=4)
+                    sums[e, b] = bank(f"sum{e}_{b}", (0, 2, 0, 4)[e] + b, [P, H])
                 nc.tensor.matmul_mx(
                     sums[e, b][:],
                     lhsT=gathered[e, s, l][:, b * P : (b + 1) * P].bitcast(FP8X4),
-                    lhsT_scale=scales[:, l, b * P : (b + 1) * P],
+                    lhsT_scale=scales[:, b * P : (b + 1) * P],
                     rhs=first[l, e, s].bitcast(FP4X4),
                     rhs_scale=first_scales[l][:, e * PASSES + s, :],
                     start=(s == 0 and l == 0),
                     stop=(s == 1 and l == 1),
                 )
-
-        def first_layer(e, s, l, blocks=(0, 1)):
-            gather_words(e, s, l, blocks)
-            multiply(e, s, l, blocks)
 
         def activate(e, b):
             hb = sb([P, H], BF16, f"hb{e}_{b}")
@@ -139,40 +150,39 @@ def tile_moe_duo_gelu_kernel(
             )
             return hb
 
-        def turn(tiles, name, copier):
-            turned = psum.tile([P, len(tiles), 2, P], F32, name=f"turned{name}", tag="turned", bufs=2)
+        def turn(tiles, hq, which, copier):
+            turned = bank(f"turned{len(turns)}", which, [P, len(tiles), 2, P])
+            turns.append(turned)
             for a, hb in reversed(list(enumerate(tiles))):
                 pairs = hb[:].bitcast(F32)
                 for u in range(2):
                     nc.tensor.transpose(turned[:, a, u, :], pairs[:, u * P : (u + 1) * P], ident[:])
-            hq = sb([P, len(tiles) * H], BF16, f"hq{name}")
             copier(
-                hq[:].bitcast(F32).rearrange("p (b s u) -> p b s u", b=len(tiles), u=2),
+                hq.bitcast(F32).rearrange("p (b s u) -> p b s u", b=len(tiles), u=2),
                 turned[:].rearrange("p b u s -> p b s u"),
             )
-            return hq
 
+        turns = []
         second = {}
 
-        def deal_second(e0, words_tag=None, scales_tag=None):
-            words = sb([P, 2, 1024], U8, f"w2w{e0}", words_tag)
-            scales = sb([P, 2, N], U8, f"w2p{e0}", scales_tag)
-            nc.vector.tensor_copy(
-                words[:].bitcast(U16).rearrange("p e (t c i) -> p e c t i", t=4, i=8),
-                w2w[:, e0 : e0 + 2, :].bitcast(U16).rearrange("p e (c i t) -> p e c t i", t=4, i=8),
+        def deal_second(e):
+            words = sb([P, 1024], U8, f"w2w{e}")
+            scales = sb([P, N], U8, f"w2p{e}")
+            nc.gpsimd.tensor_copy(
+                scales[:].rearrange("p (t m) -> p t m", t=4),
+                w2s[:, e, :].rearrange("p (m t) -> p t m", t=4),
             )
-            nc.vector.tensor_copy(
-                scales[:].rearrange("p e (t c i) -> p e c t i", t=4, i=16),
-                w2s[:, e0 : e0 + 2, :].rearrange("p e (c i t) -> p e c t i", t=4, i=16),
+            nc.gpsimd.tensor_copy(
+                words[:].rearrange("p (t m d) -> p t m d", t=4, d=2),
+                w2w[:, e, :].rearrange("p (m t d) -> p t m d", t=4, d=2),
             )
-            for a in range(2):
-                second[e0 + a] = (words[:, a, :], scales[:, a, :])
+            second[e] = (words[:], scales[:])
 
-        def quantise(hq, name, tag=None):
+        def quantise(hq, name):
             width = hq.shape[1] // 4
-            codes = sb([P, width], U32, f"hc{name}", tag)
+            codes = sb([P, width], U32, f"hc{name}")
             plane = sb([P, width], U8, f"hs{name}")
-            nc.vector.quantize_mx(codes[:].bitcast(FP8X4), plane[:], hq[:])
+            nc.vector.quantize_mx(codes[:].bitcast(FP8X4), plane[:], hq)
             return codes, plane
 
         def second_product(bank_cols, e, t, operand):
@@ -187,48 +197,70 @@ def tile_moe_duo_gelu_kernel(
                 stop=True,
             )
 
-        def second_layer(start, operands, banks, copiers):
-            width = sum(op[0].shape[1] for op in operands)
-            for t in range(4):
-                bank = psum.tile([P, width], F32, name=f"yp{start}_{t}", tag=banks[t][0], bufs=banks[t][1])
-                done = 0
-                for op in operands:
-                    w = op[0].shape[1]
-                    second_product(bank[:, done : done + w], (start + done) // C, t, op)
-                    done = done + w
-                copiers[t](y[t][:, start : start + width], bank[:])
+        def second_pair(e, pair, operand, which):
+            yp = bank(f"yp{e}_{pair}", which, [P, 2, C])
+            for a in range(2):
+                second_product(yp[:, a, :], e, 2 * pair + a, operand)
+            return yp
 
-        load_words(0, 2, (0, 1))
-        load_words(1, 2, (0, 1))
+        def empty_pair(e, pair, yp, copier):
+            for a in range(2):
+                copier(y[2 * pair + a][:, e * C : (e + 1) * C], yp[:, a, :])
+
+        on_scalar, on_vector = nc.scalar.copy, nc.vector.tensor_copy
+        gather_scales(0, (0, 1))
         w2w = sb([P, E, 1024], U8, "w2raw")
         nc.sync.dma_start(w2w[:].bitcast(I32), w2_words.rearrange("e s p c -> p (e s) c").bitcast(I32))
         load_planes(w2s, w2_scales)
+        load_words(0, 2, (0, 1))
+        load_words(1, 2, (0, 1))
+        for e in range(E):
+            deal_second(e)
+        hq = [sb([P, 2 * H], BF16, f"hq{e}")[:] for e in range(E)]
+        for s in range(PASSES):
+            for e in range(2):
+                for l in range(2):
+                    room([(e, s, l)])
+                    first_layer(e, s, l)
+                if s == 1:
+                    turn([activate(e, 0), activate(e, 1)], hq[e], 4 + e, on_scalar)
+        room([(2, 0, 0)], "gw0_0_0")
+        gather_words(2, 0, 0)
+        gather_scales(1, (0, 1), "gw0_0_1")
         gates = sb([P, 2, T], F32, "gates")
         nc.sync.dma_start(gates[:], gate.rearrange("r p t -> p r t"))
         token_lists = [load_list(pos1, "pos1_sb"), load_list(pos2, "pos2_sb")]
-        for e in range(2):
-            first_layer(e, 0, 0)
-            first_layer(e, 0, 1)
-        hq = []
-        for e in range(3):
-            if e == 2:
-                first_layer(e, 0, 0)
-                first_layer(e, 0, 1)
-            first_layer(e, 1, 0)
-            first_layer(e, 1, 1)
-            hq.append(turn([activate(e, 0), activate(e, 1)], f"{e}", nc.scalar.copy))
+        multiply(2, 0, 0)
+        coded = quantise(hq[0], "0")
+        for pair in range(2):
+            empty_pair(0, pair, second_pair(0, pair, coded, 6 + pair), on_scalar)
+        room([(2, 0, 1)], "hq0")
+        first_layer(2, 0, 1)
+        coded = quantise(hq[1], "1")
+        for pair in range(2):
+            empty_pair(1, pair, second_pair(1, pair, coded, 4 + pair), on_scalar)
+        room([(2, 1, 0), (2, 1, 1), (3, 0, 0), (3, 0, 1), (3, 1, 0), (3, 1, 1)], "hq1")
+        first_layer(2, 1, 0)
+        first_layer(2, 1, 1)
+        hb2 = [activate(2, 0), activate(2, 1)]
         first_layer(3, 0, 0)
         first_layer(3, 0, 1)
+        hb3 = []
         for b in range(2):
             first_layer(3, 1, 0, (b,))
             first_layer(3, 1, 1, (b,))
-            hq.append(turn([activate(3, b)], f"3_{b}", nc.scalar.copy))
-        deal_second(0)
-        early = [quantise(hq[0], "0"), quantise(hq[1], "1")]
-        second_layer(0, early, [("sum", 4)] * 4, [nc.vector.tensor_copy] + [nc.scalar.copy] * 3)
-        deal_second(2)
-        late = [quantise(hq[2], "2"), quantise(hq[3], "3a"), quantise(hq[4], "3b")]
-        second_layer(2 * C, late, [("yp", 2)] * 2 + [("turned", 2)] * 2, [nc.vector.tensor_copy, nc.scalar.copy, nc.scalar.copy, nc.scalar.copy])
+            hb3.append(activate(3, b))
+        turn(hb2, hq[2], 6, on_vector)
+        late = [quantise(hq[2], "2")]
+        for b in range(2):
+            turn([hb3[b]], hq[3][:, b * H : (b + 1) * H], (7, 4)[b], on_scalar)
+        late.append(quantise(hq[3], "3"))
+        banks = [bank(f"yp23_{t}", (2, 3, 0, 1)[t], [P, 2, C]) for t in range(4)]
+        for a in range(2):
+            for t in range(4):
+                second_product(banks[t][:, a, :], 2 + a, t, late[a])
+        for t in range(4):
+            (on_vector, on_scalar)[t % 2](y[t][:, 2 * C : 4 * C], banks[t][:].rearrange("p a c -> p (a c)"))
 
         out_rows = out_0.rearrange("(p t) c -> p t c", t=4)
         out_codes = sb([P, T], U32, "out_codes")

@@ -33,9 +33,12 @@ def tile_moe_duo_gelu_kernel(
     nc = tc.nc
     with ExitStack() as ctx:
         keep = ctx.enter_context(tc.tile_pool(name="keep", bufs=1))
+        lane = ctx.enter_context(tc.tile_pool(name="lane", bufs=1))
         psum = ctx.enter_context(tc.psum_pool(name="psum", bufs=1))
 
         def sb(shape, dtype, name, tag=None, bufs=1, at=None):
+            if at is not None:
+                return lane.tile(shape, dtype, name=name, align_bytes=64, offset=at)
             return keep.tile(shape, dtype, name=name, tag=tag or name, bufs=bufs, align_bytes=64)
 
         def load_list(src, name):
@@ -78,17 +81,17 @@ def tile_moe_duo_gelu_kernel(
         slot_lists = [load_list(offs, "offs_sb"), load_list(offs2, "offs2_sb")]
         for q in range(4):
             nc.sync.dma_start(xs[:, 0:T].bitcast(I32)[32 * q : 32 * q + 8], x_scales[:, 4 * q : 4 * q + 4, :].bitcast(I32))
-        xw = sb([P, PASSES, T], I32, "xw")
+        xw = sb([P, PASSES, T], I32, "xw", at=0)
         nc.sync.dma_start(xw[:], x_words.rearrange("s p t d -> p s (t d)").bitcast(I32))
         load_words(0, 0, (0,))
         load_words(1, 0, (0,))
         load_planes(first_scales[0], w1_scales)
         load_planes(first_scales[1], wp_scales)
-        load_words(0, 0, (1,))
-        load_words(1, 0, (1,))
 
         ident = sb([P, P], F32, "ident")
         make_identity(nc, ident[:])
+        table_first = sb([P, 1], BF16, "table_first")
+        nc.scalar.activation(table_first[:], ident[:, 0:1], GELU)
 
         y = [sb([P, S], F32, f"y{t}") for t in range(4)]
         direct = {}
@@ -130,7 +133,7 @@ def tile_moe_duo_gelu_kernel(
             scales = plane[:, (e % 2) * C : (e % 2 + 1) * C]
             for b in blocks:
                 if (e, b) not in sums:
-                    sums[e, b] = bank(f"sum{e}_{b}", (0, 2, 0, 4)[e] + b, [P, H])
+                    sums[e, b] = bank(f"sum{e}_{b}", (2 * e + b) % 4, [P, H])
                 nc.tensor.matmul_mx(
                     sums[e, b][:],
                     lhsT=gathered[e, s, l][:, b * P : (b + 1) * P].bitcast(FP8X4),
@@ -164,19 +167,30 @@ def tile_moe_duo_gelu_kernel(
 
         turns = []
         second = {}
+        second_scales = {}
 
-        def deal_second(e):
-            words = sb([P, 1024], U8, f"w2w{e}")
-            scales = sb([P, N], U8, f"w2p{e}")
-            nc.gpsimd.tensor_copy(
-                scales[:].rearrange("p (t m) -> p t m", t=4),
-                w2s[:, e, :].rearrange("p (m t) -> p t m", t=4),
+        def deal_words(e0, count, copier, at=None):
+            words = sb([P, count, 1024], U8, f"w2w{e0}", at=at)
+            copier(
+                words[:].bitcast(U16).rearrange("p e (t c i) -> p e c t i", t=4, i=8),
+                w2w[e0 // 2][:, e0 % 2 : e0 % 2 + count, :].bitcast(U16).rearrange("p e (c i t) -> p e c t i", t=4, i=8),
             )
-            nc.gpsimd.tensor_copy(
-                words[:].rearrange("p (t m d) -> p t m d", t=4, d=2),
-                w2w[:, e, :].rearrange("p (m t d) -> p t m d", t=4, d=2),
+            for a in range(count):
+                second[e0 + a] = words[:, a, :]
+
+        def deal_scales(e0, count, copier, at=None):
+            scales = sb([P, count, N], U8, f"w2p{e0}", at=at)
+            copier(
+                scales[:].rearrange("p e (t c i) -> p e c t i", t=4, i=16),
+                w2s[:, e0 : e0 + count, :].rearrange("p e (c i t) -> p e c t i", t=4, i=16),
             )
-            second[e] = (words[:], scales[:])
+            for a in range(count):
+                second_scales[e0 + a] = scales[:, a, :]
+
+        def load_second(e0):
+            tile = sb([P, 2, 1024], U8, f"w2raw{e0}")
+            nc.sync.dma_start(tile[:].bitcast(I32), w2_words[e0 : e0 + 2].rearrange("e s p c -> p (e s) c").bitcast(I32))
+            w2w.append(tile)
 
         def quantise(hq, name):
             width = hq.shape[1] // 4
@@ -186,7 +200,7 @@ def tile_moe_duo_gelu_kernel(
             return codes, plane
 
         def second_product(bank_cols, e, t, operand):
-            words, scales = second[e]
+            words, scales = second[e], second_scales[e]
             nc.tensor.matmul_mx(
                 bank_cols,
                 lhsT=words[:, 2 * P * t : 2 * P * (t + 1)].bitcast(FP4X4),
@@ -208,14 +222,18 @@ def tile_moe_duo_gelu_kernel(
                 copier(y[2 * pair + a][:, e * C : (e + 1) * C], yp[:, a, :])
 
         on_scalar, on_vector = nc.scalar.copy, nc.vector.tensor_copy
+        w2w = []
+        load_words(0, 0, (1,))
+        load_words(1, 0, (1,))
         gather_scales(0, (0, 1))
-        w2w = sb([P, E, 1024], U8, "w2raw")
-        nc.sync.dma_start(w2w[:].bitcast(I32), w2_words.rearrange("e s p c -> p (e s) c").bitcast(I32))
+        load_second(0)
         load_planes(w2s, w2_scales)
         load_words(0, 2, (0, 1))
         load_words(1, 2, (0, 1))
-        for e in range(E):
-            deal_second(e)
+        load_second(2)
+        for e in range(2):
+            deal_words(e, 1, on_scalar)
+            deal_scales(e, 1, nc.gpsimd.tensor_copy)
         hq = [sb([P, 2 * H], BF16, f"hq{e}")[:] for e in range(E)]
         for s in range(PASSES):
             for e in range(2):
@@ -240,22 +258,24 @@ def tile_moe_duo_gelu_kernel(
         for pair in range(2):
             empty_pair(1, pair, second_pair(1, pair, coded, 4 + pair), on_scalar)
         room([(2, 1, 0), (2, 1, 1), (3, 0, 0), (3, 0, 1), (3, 1, 0), (3, 1, 1)], "hq1")
+        first_layer(3, 0, 0)
+        first_layer(3, 0, 1)
         first_layer(2, 1, 0)
         first_layer(2, 1, 1)
         hb2 = [activate(2, 0), activate(2, 1)]
-        first_layer(3, 0, 0)
-        first_layer(3, 0, 1)
         hb3 = []
         for b in range(2):
             first_layer(3, 1, 0, (b,))
             first_layer(3, 1, 1, (b,))
             hb3.append(activate(3, b))
+        deal_scales(2, 2, on_vector, at=0)
+        deal_words(2, 2, on_vector, at=2 * N)
         turn(hb2, hq[2], 6, on_vector)
         late = [quantise(hq[2], "2")]
         for b in range(2):
-            turn([hb3[b]], hq[3][:, b * H : (b + 1) * H], (7, 4)[b], on_scalar)
+            turn([hb3[b]], hq[3][:, b * H : (b + 1) * H], (7, 0)[b], on_scalar)
         late.append(quantise(hq[3], "3"))
-        banks = [bank(f"yp23_{t}", (2, 3, 0, 1)[t], [P, 2, C]) for t in range(4)]
+        banks = [bank(f"yp23_{t}", (4, 5, 1, 2)[t], [P, 2, C]) for t in range(4)]
         for a in range(2):
             for t in range(4):
                 second_product(banks[t][:, a, :], 2 + a, t, late[a])

@@ -53,14 +53,14 @@ def tile_moe_duo_gelu_kernel(
 
         first = {}
 
-        def load_words(l, e0, passes):
-            tile = sb([P, 2, len(passes), 1024], U8, f"first{l}_{e0}_{passes[0]}")
-            rows = (w1_words, wp_words)[l][e0 : e0 + 2, passes[0] : passes[-1] + 1]
+        def load_words(l, e0, count, passes):
+            tile = sb([P, count, len(passes), 1024], U8, f"first{l}_{e0}_{passes[0]}")
+            rows = (w1_words, wp_words)[l][e0 : e0 + count, passes[0] : passes[-1] + 1]
             nc.sync.dma_start(
                 tile[:].rearrange("p e s c -> p (e s) c").bitcast(I32),
                 rows.rearrange("e s p c -> p (e s) c").bitcast(I32),
             )
-            for a in range(2):
+            for a in range(count):
                 for s in passes:
                     first[l, e0 + a, s] = tile[:, a, s - passes[0], :]
 
@@ -70,7 +70,7 @@ def tile_moe_duo_gelu_kernel(
         xs = sb([P, 2 * T], U8, "xs")
         first_scales = [sb([P, E * PASSES, H], U8, f"first_scales{l}") for l in range(2)]
         w2s = sb([P, E, N], U8, "w2s")
-        moved = [sb([P, 2 * T], U8, f"moved{g}") for g in range(2)]
+        moved = [sb([P, width], U8, f"moved{width}") for width in (3 * T, T)]
         nc.gpsimd.memset(xs[:].bitcast(I32), 0)
         nc.vector.memset(first_scales[0][:].bitcast(I32), 0)
         nc.gpsimd.memset(first_scales[1][:].bitcast(I32), 0)
@@ -78,31 +78,37 @@ def tile_moe_duo_gelu_kernel(
             nc.vector.memset(moved[g][:].bitcast(I32), 0)
         nc.vector.memset(w2s[:].bitcast(I32), 0)
 
-        slot_lists = [load_list(offs, "offs_sb"), load_list(offs2, "offs2_sb")]
+        slot_lists = [load_list(offs, "offs_sb")]
         for q in range(4):
             nc.sync.dma_start(xs[:, 0:T].bitcast(I32)[32 * q : 32 * q + 8], x_scales[:, 4 * q : 4 * q + 4, :].bitcast(I32))
-        xw = sb([P, PASSES, T], I32, "xw", at=0)
-        nc.sync.dma_start(xw[:], x_words.rearrange("s p t d -> p s (t d)").bitcast(I32))
-        load_words(0, 0, (0,))
-        load_words(1, 0, (0,))
+        xw = [sb([P, T], I32, f"xw{s}") for s in range(PASSES)]
+
+        def load_tokens(s):
+            nc.sync.dma_start(xw[s][:], x_words[s].rearrange("p t d -> p (t d)").bitcast(I32))
+
+        load_tokens(0)
+        slot_lists.append(load_list(offs2, "offs2_sb"))
+        load_words(0, 0, 2, (0,))
+        load_words(1, 0, 2, (0,))
         load_planes(first_scales[0], w1_scales)
         load_planes(first_scales[1], wp_scales)
 
         ident = sb([P, P], F32, "ident")
         make_identity(nc, ident[:])
-        table_first = sb([P, 1], BF16, "table_first")
-        nc.scalar.activation(table_first[:], ident[:, 0:1], GELU)
 
         y = [sb([P, S], F32, f"y{t}") for t in range(4)]
-        direct = {}
+        direct = [sb([P, 3 * T], U8, "direct_first")]
 
-        def gather_scales(g, lists, tag=None):
-            tile = sb([P, len(lists) * T], U8, f"direct{g}_{lists[0]}", tag)
-            for a, l in enumerate(lists):
-                direct[g, l] = tile[:, a * T : (a + 1) * T]
-                nc.vector.tensor_copy(direct[g, l], xs[:].indirect(entries(slot_lists[l], g * T, T)))
-            src = tile[:].bitcast(I32)
-            dst = moved[g][:, lists[0] * T : (lists[-1] + 1) * T].bitcast(I32)
+        def plane(tiles, l, g):
+            if (l, g) == (1, 1):
+                return tiles[1][:]
+            return tiles[0][:, (2 * l + g) * T : (2 * l + g + 1) * T]
+
+        def gather_scales(l, g):
+            nc.vector.tensor_copy(plane(direct, l, g), xs[:].indirect(entries(slot_lists[l], g * T, T)))
+
+        def move_scales(batch):
+            src, dst = direct[batch][:].bitcast(I32), moved[batch][:].bitcast(I32)
             for p0, rows in ((0, 64), (64, 4), (96, 4)):
                 nc.sync.dma_start(dst[p0 : p0 + rows], src[p0 + 4 : p0 + 4 + rows])
 
@@ -121,16 +127,17 @@ def tile_moe_duo_gelu_kernel(
             cols = slice(blocks[0] * P, (blocks[-1] + 1) * P)
             nc.vector.tensor_copy(
                 gathered[e, s, l][:, cols],
-                xw[:, s, :].bitcast(U32).indirect(entries(slot_lists[l], e * C + cols.start, cols.stop - cols.start)),
+                xw[s][:].bitcast(U32).indirect(entries(slot_lists[l], e * C + cols.start, cols.stop - cols.start)),
             )
 
         def first_layer(e, s, l, blocks=(0, 1)):
+            if (e, s, l) not in gathered:
+                room([(e, s, l)])
             gather_words(e, s, l, blocks)
             multiply(e, s, l, blocks)
 
         def multiply(e, s, l, blocks=(0, 1)):
-            plane = direct[e // 2, l] if s == 0 else moved[e // 2][:, l * T : (l + 1) * T]
-            scales = plane[:, (e % 2) * C : (e % 2 + 1) * C]
+            scales = plane((direct, moved)[s], l, e // 2)[:, (e % 2) * C : (e % 2 + 1) * C]
             for b in blocks:
                 if (e, b) not in sums:
                     sums[e, b] = bank(f"sum{e}_{b}", (2 * e + b) % 4, [P, H])
@@ -169,11 +176,11 @@ def tile_moe_duo_gelu_kernel(
         second = {}
         second_scales = {}
 
-        def deal_words(e0, count, copier, at=None):
-            words = sb([P, count, 1024], U8, f"w2w{e0}", at=at)
+        def deal_words(e0, count, copier, tag=None):
+            words = sb([P, count, 1024], U8, f"w2w{e0}", tag)
             copier(
                 words[:].bitcast(U16).rearrange("p e (t c i) -> p e c t i", t=4, i=8),
-                w2w[e0 // 2][:, e0 % 2 : e0 % 2 + count, :].bitcast(U16).rearrange("p e (c i t) -> p e c t i", t=4, i=8),
+                w2w[:, e0 : e0 + count, :].bitcast(U16).rearrange("p e (c i t) -> p e c t i", t=4, i=8),
             )
             for a in range(count):
                 second[e0 + a] = words[:, a, :]
@@ -187,17 +194,12 @@ def tile_moe_duo_gelu_kernel(
             for a in range(count):
                 second_scales[e0 + a] = scales[:, a, :]
 
-        def load_second(e0):
-            tile = sb([P, 2, 1024], U8, f"w2raw{e0}")
-            nc.sync.dma_start(tile[:].bitcast(I32), w2_words[e0 : e0 + 2].rearrange("e s p c -> p (e s) c").bitcast(I32))
-            w2w.append(tile)
-
-        def quantise(hq, name):
+        def quantise(hq, name, tag=None):
             width = hq.shape[1] // 4
-            codes = sb([P, width], U32, f"hc{name}")
+            codes = sb([P, width], U32, f"hc{name}", tag)
             plane = sb([P, width], U8, f"hs{name}")
             nc.vector.quantize_mx(codes[:].bitcast(FP8X4), plane[:], hq)
-            return codes, plane
+            return codes[:], plane[:]
 
         def second_product(bank_cols, e, t, operand):
             words, scales = second[e], second_scales[e]
@@ -205,8 +207,8 @@ def tile_moe_duo_gelu_kernel(
                 bank_cols,
                 lhsT=words[:, 2 * P * t : 2 * P * (t + 1)].bitcast(FP4X4),
                 lhsT_scale=scales[:, P * t : P * (t + 1)],
-                rhs=operand[0][:].bitcast(FP8X4),
-                rhs_scale=operand[1][:],
+                rhs=operand[0].bitcast(FP8X4),
+                rhs_scale=operand[1],
                 start=True,
                 stop=True,
             )
@@ -222,65 +224,73 @@ def tile_moe_duo_gelu_kernel(
                 copier(y[2 * pair + a][:, e * C : (e + 1) * C], yp[:, a, :])
 
         on_scalar, on_vector = nc.scalar.copy, nc.vector.tensor_copy
-        w2w = []
-        load_words(0, 0, (1,))
-        load_words(1, 0, (1,))
-        gather_scales(0, (0, 1))
-        load_second(0)
-        load_planes(w2s, w2_scales)
-        load_words(0, 2, (0, 1))
-        load_words(1, 2, (0, 1))
-        load_second(2)
+        load_tokens(1)
+        load_words(0, 0, 2, (1,))
+        load_words(1, 0, 2, (1,))
+        gather_scales(0, 0)
+        gather_scales(0, 1)
         for e in range(2):
-            deal_words(e, 1, on_scalar)
+            first_layer(e, 0, 0)
+        gather_scales(1, 0)
+        move_scales(0)
+        load_words(0, 2, 2, (0, 1))
+        load_words(1, 2, 2, (0, 1))
+        w2w = sb([P, E, 1024], U8, "w2raw")
+        nc.sync.dma_start(w2w[:].bitcast(I32), w2_words.rearrange("e s p c -> p (e s) c").bitcast(I32))
+        hq01 = sb([P, 4 * H], BF16, "hq01")
+        hq = [hq01[:, 0 : 2 * H], hq01[:, 2 * H : 4 * H], sb([P, 2 * H], BF16, "hq2")[:]]
+        for e in range(2):
+            first_layer(e, 0, 1)
+        hb = []
+        for e in range(2):
+            first_layer(e, 1, 0)
+            first_layer(e, 1, 1)
+            hb.extend([activate(e, 0), activate(e, 1)])
+        for e in range(2):
+            turn(hb[2 * e : 2 * e + 2], hq[e], 4 + e, on_scalar)
+        room([(2, 0, 0)], "gw0_0_1")
+        first_layer(2, 0, 0)
+        direct.append(sb([P, T], U8, "direct_last", "gw1_0_1"))
+        gather_scales(1, 1)
+        move_scales(1)
+        load_planes(w2s, w2_scales)
+        for e in range(E):
             deal_scales(e, 1, nc.gpsimd.tensor_copy)
-        hq = [sb([P, 2 * H], BF16, f"hq{e}")[:] for e in range(E)]
-        for s in range(PASSES):
-            for e in range(2):
-                for l in range(2):
-                    room([(e, s, l)])
-                    first_layer(e, s, l)
-                if s == 1:
-                    turn([activate(e, 0), activate(e, 1)], hq[e], 4 + e, on_scalar)
-        room([(2, 0, 0)], "gw0_0_0")
-        gather_words(2, 0, 0)
-        gather_scales(1, (0, 1), "gw0_0_1")
+        deal_words(0, 2, on_scalar)
         gates = sb([P, 2, T], F32, "gates")
         nc.sync.dma_start(gates[:], gate.rearrange("r p t -> p r t"))
         token_lists = [load_list(pos1, "pos1_sb"), load_list(pos2, "pos2_sb")]
-        multiply(2, 0, 0)
-        coded = quantise(hq[0], "0")
-        for pair in range(2):
-            empty_pair(0, pair, second_pair(0, pair, coded, 6 + pair), on_scalar)
-        room([(2, 0, 1)], "hq0")
-        first_layer(2, 0, 1)
-        coded = quantise(hq[1], "1")
-        for pair in range(2):
-            empty_pair(1, pair, second_pair(1, pair, coded, 4 + pair), on_scalar)
-        room([(2, 1, 0), (2, 1, 1), (3, 0, 0), (3, 0, 1), (3, 1, 0), (3, 1, 1)], "hq1")
-        first_layer(3, 0, 0)
-        first_layer(3, 0, 1)
-        first_layer(2, 1, 0)
-        first_layer(2, 1, 1)
-        hb2 = [activate(2, 0), activate(2, 1)]
-        hb3 = []
+        order = [(2, 1, 0), (2, 0, 1), (3, 0, 0), (2, 1, 1), (3, 0, 1), (3, 1, 0), (3, 1, 1)]
+        room(order, "gw0_1_0")
+        for unit in order[0:4]:
+            first_layer(*unit)
+        hb = [activate(2, 0), activate(2, 1)]
+        for unit in order[4:6]:
+            first_layer(*unit)
         for b in range(2):
-            first_layer(3, 1, 0, (b,))
             first_layer(3, 1, 1, (b,))
-            hb3.append(activate(3, b))
-        deal_scales(2, 2, on_vector, at=0)
-        deal_words(2, 2, on_vector, at=2 * N)
-        turn(hb2, hq[2], 6, on_vector)
-        late = [quantise(hq[2], "2")]
+            hb.append(activate(3, b))
+        both = quantise(hq01[:], "01")
+        early = [(e, (both[0][:, e * C : (e + 1) * C], both[1][:, e * C : (e + 1) * C])) for e in range(2)]
+        deal_words(2, 2, on_vector, "xw1")
+        turn(hb[0:2], hq[2], 6, on_vector)
+        hq3 = [sb([P, H], BF16, f"hq3_{b}")[:] for b in range(2)]
         for b in range(2):
-            turn([hb3[b]], hq[3][:, b * H : (b + 1) * H], (7, 0)[b], on_scalar)
-        late.append(quantise(hq[3], "3"))
-        banks = [bank(f"yp23_{t}", (4, 5, 1, 2)[t], [P, 2, C]) for t in range(4)]
-        for a in range(2):
+            turn([hb[2 + b]], hq3[b], (7, 4)[b], on_scalar)
+        late = [(2, quantise(hq[2], "2")), (3, quantise(hq3[0], "3a")), (3, quantise(hq3[1], "3b"))]
+
+        def second_layer(start, parts, banks, copiers):
             for t in range(4):
-                second_product(banks[t][:, a, :], 2 + a, t, late[a])
-        for t in range(4):
-            (on_vector, on_scalar)[t % 2](y[t][:, 2 * C : 4 * C], banks[t][:].rearrange("p a c -> p (a c)"))
+                yp = bank(f"yp{start}_{t}", banks[t], [P, T])
+                done = 0
+                for e, operand in parts:
+                    width = operand[0].shape[1]
+                    second_product(yp[:, done : done + width], e, t, operand)
+                    done = done + width
+                copiers[t](y[t][:, start : start + T], yp[:])
+
+        second_layer(0, early, (0, 1, 5, 6), (on_vector, on_scalar, on_vector, on_scalar))
+        second_layer(T, late, (2, 3, 7, 4), (on_vector, on_scalar, on_vector, on_scalar))
 
         out_rows = out_0.rearrange("(p t) c -> p t c", t=4)
         out_codes = sb([P, T], U32, "out_codes")

@@ -24,6 +24,7 @@ P = 128
 PASSES = K // 512
 STRIPE = 16
 HALF = T // 2
+PAIR = 2 * C
 
 
 def tile_moe_duo_gelu_kernel(
@@ -33,18 +34,22 @@ def tile_moe_duo_gelu_kernel(
     nc = tc.nc
     with ExitStack() as ctx:
         keep = ctx.enter_context(tc.tile_pool(name="keep", bufs=1))
-        lane = ctx.enter_context(tc.tile_pool(name="lane", bufs=1))
         psum = ctx.enter_context(tc.psum_pool(name="psum", bufs=1))
+        on_scalar, on_vector = nc.scalar.copy, nc.vector.tensor_copy
 
-        def sb(shape, dtype, name, tag=None, bufs=1, at=None):
-            if at is not None:
-                return lane.tile(shape, dtype, name=name, align_bytes=64, offset=at)
-            return keep.tile(shape, dtype, name=name, tag=tag or name, bufs=bufs, align_bytes=64)
+        def sb(shape, dtype, name, tag=None):
+            return keep.tile(shape, dtype, name=name, tag=tag or name, bufs=1, align_bytes=64)
+
+        def bank(name, which, shape):
+            return psum.tile(shape, F32, name=name, tag=f"bank{which}", bufs=1)
 
         def load_list(src, name):
             tile = keep.tile(list(src.shape), U16, name=name)
             nc.sync.dma_start(tile[:], src)
             return tile
+
+        def entries(lst, start, count):
+            return lst[:, start // STRIPE : (start + count) // STRIPE]
 
         def load_planes(plane, scales):
             rows = scales.rearrange("e s b c -> b (e s) c").bitcast(I32)
@@ -53,94 +58,86 @@ def tile_moe_duo_gelu_kernel(
 
         first = {}
 
-        def load_words(l, e0, count, passes):
-            tile = sb([P, count, len(passes), 1024], U8, f"first{l}_{e0}_{passes[0]}")
-            rows = (w1_words, wp_words)[l][e0 : e0 + count, passes[0] : passes[-1] + 1]
+        def load_words(l, pair, passes):
+            tile = sb([P, 2, len(passes), 1024], U8, f"first{l}_{pair}_{passes[0]}")
+            rows = (w1_words, wp_words)[l][2 * pair : 2 * pair + 2, passes[0] : passes[-1] + 1]
             nc.sync.dma_start(
                 tile[:].rearrange("p e s c -> p (e s) c").bitcast(I32),
                 rows.rearrange("e s p c -> p (e s) c").bitcast(I32),
             )
-            for a in range(count):
+            for a in range(2):
                 for s in passes:
-                    first[l, e0 + a, s] = tile[:, a, s - passes[0], :]
+                    first[l, 2 * pair + a, s] = tile[:, a, s - passes[0], :]
 
-        def entries(lst, start, count):
-            return lst[:, start // STRIPE : (start + count) // STRIPE]
-
-        xs = sb([P, 2 * T], U8, "xs")
-        first_scales = [sb([P, E * PASSES, H], U8, f"first_scales{l}") for l in range(2)]
-        w2s = sb([P, E, N], U8, "w2s")
-        moved = [sb([P, width], U8, f"moved{width}") for width in (3 * T, T)]
-        nc.gpsimd.memset(xs[:].bitcast(I32), 0)
-        nc.vector.memset(first_scales[0][:].bitcast(I32), 0)
-        nc.gpsimd.memset(first_scales[1][:].bitcast(I32), 0)
-        for g in range(2):
-            nc.vector.memset(moved[g][:].bitcast(I32), 0)
-        nc.vector.memset(w2s[:].bitcast(I32), 0)
-
-        slot_lists = [load_list(offs, "offs_sb")]
-        for q in range(4):
-            nc.sync.dma_start(xs[:, 0:T].bitcast(I32)[32 * q : 32 * q + 8], x_scales[:, 4 * q : 4 * q + 4, :].bitcast(I32))
         xw = [sb([P, T], I32, f"xw{s}") for s in range(PASSES)]
 
         def load_tokens(s):
             nc.sync.dma_start(xw[s][:], x_words[s].rearrange("p t d -> p (t d)").bitcast(I32))
 
+        xs = sb([P, 2 * T], U8, "xs")
+        first_scales = [sb([P, E * PASSES, H], U8, f"first_scales{l}") for l in range(2)]
+        w2s = sb([P, E, N], U8, "w2s")
+        moved_early = sb([P, 2 * PAIR], U8, "moved_early")
+        moved_late = [sb([P, PAIR], U8, f"moved_late{l}") for l in range(2)]
+        nc.gpsimd.memset(xs[:].bitcast(I32), 0)
+        nc.vector.memset(first_scales[0][:].bitcast(I32), 0)
+        nc.gpsimd.memset(first_scales[1][:].bitcast(I32), 0)
+        nc.vector.memset(moved_early[:].bitcast(I32), 0)
+        for l in range(2):
+            nc.vector.memset(moved_late[l][:].bitcast(I32), 0)
+        nc.vector.memset(w2s[:].bitcast(I32), 0)
+
+        slot_lists = {0: load_list(offs, "offs_sb")}
+        for q in range(4):
+            nc.sync.dma_start(xs[:, 0:T].bitcast(I32)[32 * q : 32 * q + 8], x_scales[:, 4 * q : 4 * q + 4, :].bitcast(I32))
         load_tokens(0)
-        slot_lists.append(load_list(offs2, "offs2_sb"))
-        load_words(0, 0, 2, (0,))
-        load_words(1, 0, 2, (0,))
+        load_words(0, 0, (0,))
+        slot_lists[1] = load_list(offs2, "offs2_sb")
         load_planes(first_scales[0], w1_scales)
+        load_tokens(1)
         load_planes(first_scales[1], wp_scales)
+        load_words(1, 0, (0,))
+        load_words(0, 0, (1,))
+        load_words(1, 0, (1,))
 
         ident = sb([P, P], F32, "ident")
         make_identity(nc, ident[:])
 
-        y = [sb([P, S], F32, f"y{t}") for t in range(4)]
-        direct = [sb([P, 3 * T], U8, "direct_first")]
+        direct_early = sb([P, 2 * PAIR], U8, "direct_early")
+        planes = {}
+        for l in range(2):
+            planes[l, 0, 0] = direct_early[:, l * PAIR : (l + 1) * PAIR]
+            planes[l, 0, 1] = moved_early[:, l * PAIR : (l + 1) * PAIR]
+            planes[l, 1, 1] = moved_late[l][:]
 
-        def plane(tiles, l, g):
-            if (l, g) == (1, 1):
-                return tiles[1][:]
-            return tiles[0][:, (2 * l + g) * T : (2 * l + g + 1) * T]
+        def gather_scales(l, pair):
+            nc.vector.tensor_copy(planes[l, pair, 0], xs[:].indirect(entries(slot_lists[l], pair * PAIR, PAIR)))
 
-        def gather_scales(l, g):
-            nc.vector.tensor_copy(plane(direct, l, g), xs[:].indirect(entries(slot_lists[l], g * T, T)))
-
-        def move_scales(batch):
-            src, dst = direct[batch][:].bitcast(I32), moved[batch][:].bitcast(I32)
+        def move_scales(dst, src):
             for p0, rows in ((0, 64), (64, 4), (96, 4)):
-                nc.sync.dma_start(dst[p0 : p0 + rows], src[p0 + 4 : p0 + 4 + rows])
-
-        def bank(name, which, shape):
-            return psum.tile(shape, F32, name=name, tag=f"bank{which}", bufs=1)
+                nc.sync.dma_start(dst.bitcast(I32)[p0 : p0 + rows], src.bitcast(I32)[p0 + 4 : p0 + 4 + rows])
 
         sums = {}
         gathered = {}
+        sum_banks = ((0, 1), (2, 3), (3, 4), (5, 6))
 
-        def room(units, tag=None, at=None):
-            tile = sb([P, len(units) * C], U32, f"gw{units[0][0]}_{units[0][1]}_{units[0][2]}", tag, at=at)
+        def room(units, tag=None):
+            tile = sb([P, len(units) * C], U32, "gw%d%d%d" % units[0], tag)
             for a, unit in enumerate(units):
                 gathered[unit] = tile[:, a * C : (a + 1) * C]
 
-        def gather_words(e, s, l, blocks=(0, 1)):
+        def first_layer(e, s, l, blocks=(0, 1)):
+            if (e, s, l) not in gathered:
+                room([(e, s, l)])
             cols = slice(blocks[0] * P, (blocks[-1] + 1) * P)
             nc.vector.tensor_copy(
                 gathered[e, s, l][:, cols],
                 xw[s][:].bitcast(U32).indirect(entries(slot_lists[l], e * C + cols.start, cols.stop - cols.start)),
             )
-
-        def first_layer(e, s, l, blocks=(0, 1)):
-            if (e, s, l) not in gathered:
-                room([(e, s, l)])
-            gather_words(e, s, l, blocks)
-            multiply(e, s, l, blocks)
-
-        def multiply(e, s, l, blocks=(0, 1)):
-            scales = plane((direct, moved)[s], l, e // 2)[:, (e % 2) * C : (e % 2 + 1) * C]
+            scales = planes[l, e // 2, s][:, (e % 2) * C : (e % 2 + 1) * C]
             for b in blocks:
                 if (e, b) not in sums:
-                    sums[e, b] = bank(f"sum{e}_{b}", (2 * e + b) % 4, [P, H])
+                    sums[e, b] = bank(f"sum{e}_{b}", sum_banks[e][b], [P, H])
                 nc.tensor.matmul_mx(
                     sums[e, b][:],
                     lhsT=gathered[e, s, l][:, b * P : (b + 1) * P].bitcast(FP8X4),
@@ -148,7 +145,7 @@ def tile_moe_duo_gelu_kernel(
                     rhs=first[l, e, s].bitcast(FP4X4),
                     rhs_scale=first_scales[l][:, e * PASSES + s, :],
                     start=(s == 0 and l == 0),
-                    stop=(s == 1 and l == 1),
+                    stop=(s == 1 and l == 1 - e // 2),
                 )
 
         def activate(e, b):
@@ -160,9 +157,8 @@ def tile_moe_duo_gelu_kernel(
             )
             return hb
 
-        def turn(tiles, hq, which, copier):
-            turned = bank(f"turned{len(turns)}", which, [P, len(tiles), 2, P])
-            turns.append(turned)
+        def turn(name, tiles, hq, which, copier):
+            turned = bank(f"turned{name}", which, [P, len(tiles), 2, P])
             for a, hb in reversed(list(enumerate(tiles))):
                 pairs = hb[:].bitcast(F32)
                 for u in range(2):
@@ -172,12 +168,11 @@ def tile_moe_duo_gelu_kernel(
                 turned[:].rearrange("p b u s -> p b s u"),
             )
 
-        turns = []
         second = {}
         second_scales = {}
 
-        def deal_words(e0, count, copier, tag=None):
-            words = sb([P, count, 1024], U8, f"w2w{e0}", tag)
+        def deal_words(e0, count, copier):
+            words = sb([P, count, 1024], U8, f"w2w{e0}", "hb1_1")
             copier(
                 words[:].bitcast(U16).rearrange("p e (t c i) -> p e c t i", t=4, i=8),
                 w2w[:, e0 : e0 + count, :].bitcast(U16).rearrange("p e (c i t) -> p e c t i", t=4, i=8),
@@ -185,112 +180,98 @@ def tile_moe_duo_gelu_kernel(
             for a in range(count):
                 second[e0 + a] = words[:, a, :]
 
-        def deal_scales(e0, count, copier, at=None):
-            scales = sb([P, count, N], U8, f"w2p{e0}", at=at)
-            copier(
-                scales[:].rearrange("p e (t c i) -> p e c t i", t=4, i=16),
-                w2s[:, e0 : e0 + count, :].rearrange("p e (c i t) -> p e c t i", t=4, i=16),
+        def deal_scales(e):
+            scales = sb([P, N], U8, f"w2p{e}")
+            nc.gpsimd.tensor_copy(
+                scales[:].rearrange("p (t c i) -> p c t i", t=4, i=16),
+                w2s[:, e, :].rearrange("p (c i t) -> p c t i", t=4, i=16),
             )
-            for a in range(count):
-                second_scales[e0 + a] = scales[:, a, :]
+            second_scales[e] = scales[:]
 
-        def quantise(hq, name, tag=None):
+        def quantise(hq, name):
             width = hq.shape[1] // 4
-            codes = sb([P, width], U32, f"hc{name}", tag)
+            codes = sb([P, width], U32, f"hc{name}")
             plane = sb([P, width], U8, f"hs{name}")
             nc.vector.quantize_mx(codes[:].bitcast(FP8X4), plane[:], hq)
             return codes[:], plane[:]
 
-        def second_product(bank_cols, e, t, operand):
-            words, scales = second[e], second_scales[e]
-            nc.tensor.matmul_mx(
-                bank_cols,
-                lhsT=words[:, 2 * P * t : 2 * P * (t + 1)].bitcast(FP4X4),
-                lhsT_scale=scales[:, P * t : P * (t + 1)],
-                rhs=operand[0].bitcast(FP8X4),
-                rhs_scale=operand[1],
-                start=True,
-                stop=True,
-            )
+        y = [sb([P, S], F32, f"y{t}") for t in range(4)]
 
-        def second_pair(e, pair, operand, which):
-            yp = bank(f"yp{e}_{pair}", which, [P, 2, C])
-            for a in range(2):
-                second_product(yp[:, a, :], e, 2 * pair + a, operand)
-            return yp
+        def second_layer(start, parts, banks, copiers):
+            for t in range(4):
+                yp = bank(f"yp{start}_{t}", banks[t], [P, PAIR])
+                done = 0
+                for e, (codes, plane) in parts:
+                    width = codes.shape[1]
+                    nc.tensor.matmul_mx(
+                        yp[:, done : done + width],
+                        lhsT=second[e][:, 2 * P * t : 2 * P * (t + 1)].bitcast(FP4X4),
+                        lhsT_scale=second_scales[e][:, P * t : P * (t + 1)],
+                        rhs=codes.bitcast(FP8X4),
+                        rhs_scale=plane,
+                        start=True,
+                        stop=True,
+                    )
+                    done = done + width
+                copiers[t](y[t][:, start : start + PAIR], yp[:])
 
-        def empty_pair(e, pair, yp, copier):
-            for a in range(2):
-                copier(y[2 * pair + a][:, e * C : (e + 1) * C], yp[:, a, :])
-
-        on_scalar, on_vector = nc.scalar.copy, nc.vector.tensor_copy
-        load_tokens(1)
-        load_words(0, 0, 2, (1,))
-        load_words(1, 0, 2, (1,))
         gather_scales(0, 0)
-        gather_scales(0, 1)
-        for e in range(2):
-            first_layer(e, 0, 0)
+        first_layer(0, 0, 0)
+        first_layer(1, 0, 0)
         gather_scales(1, 0)
-        move_scales(0)
-        load_words(0, 2, 2, (0, 1))
-        load_words(1, 2, 2, (0, 1))
+        move_scales(moved_early[:], direct_early[:])
+        load_words(0, 1, (0,))
         w2w = sb([P, E, 1024], U8, "w2raw")
         nc.sync.dma_start(w2w[:].bitcast(I32), w2_words.rearrange("e s p c -> p (e s) c").bitcast(I32))
-        hq01 = sb([P, 4 * H], BF16, "hq01")
-        hq = [hq01[:, 0 : 2 * H], hq01[:, 2 * H : 4 * H], sb([P, 2 * H], BF16, "hq2")[:]]
-        for e in range(2):
-            first_layer(e, 0, 1)
+        load_planes(w2s, w2_scales)
+        first_layer(0, 0, 1)
+        first_layer(1, 0, 1)
+        planes[0, 1, 0] = sb([P, PAIR], U8, "direct_late0", "gw000")[:]
+        gather_scales(0, 1)
+        gates = sb([P, 2, T], F32, "gates")
+        nc.sync.dma_start(gates[:], gate.rearrange("r p t -> p r t"))
+        load_words(1, 1, (0,))
+        load_words(1, 1, (1,))
+        load_words(0, 1, (1,))
+        token_lists = [load_list(pos1, "pos1_sb"), load_list(pos2, "pos2_sb")]
         hb = []
         for e in range(2):
             first_layer(e, 1, 0)
             first_layer(e, 1, 1)
             hb.extend([activate(e, 0), activate(e, 1)])
-        for e in range(2):
-            turn(hb[2 * e : 2 * e + 2], hq[e], 4 + e, on_scalar)
-        room([(2, 0, 0)], "gw0_0_1")
-        first_layer(2, 0, 0)
-        direct.append(sb([P, T], U8, "direct_last", "gw1_0_1"))
+        hq01 = sb([P, 4 * H], BF16, "hq01")
+        turn("0", hb[0:2], hq01[:, 0 : 2 * H], 4, on_scalar)
+        for b in range(2):
+            turn(f"1{b}", [hb[2 + b]], hq01[:, (2 + b) * H : (3 + b) * H], 5 + b, on_scalar)
+        deal_words(0, E, on_scalar)
+        planes[1, 1, 0] = sb([P, PAIR], U8, "direct_late1", "gw001")[:]
         gather_scales(1, 1)
-        move_scales(1)
-        load_planes(w2s, w2_scales)
+        for l in range(2):
+            move_scales(planes[l, 1, 1], planes[l, 1, 0])
+        room([(2, 0, 0), (2, 0, 1)], "gw101")
+        first_layer(2, 0, 0)
+        first_layer(2, 0, 1)
         for e in range(E):
-            deal_scales(e, 1, nc.gpsimd.tensor_copy)
-        deal_words(0, 2, on_scalar)
-        gates = sb([P, 2, T], F32, "gates")
-        nc.sync.dma_start(gates[:], gate.rearrange("r p t -> p r t"))
-        token_lists = [load_list(pos1, "pos1_sb"), load_list(pos2, "pos2_sb")]
-        order = [(2, 1, 0), (2, 0, 1), (3, 0, 0), (2, 1, 1), (3, 0, 1), (3, 1, 0), (3, 1, 1)]
-        room(order, "gw0_1_0")
+            deal_scales(e)
+        order = [(3, 0, 0), (3, 0, 1), (2, 1, 1), (2, 1, 0), (3, 1, 1), (3, 1, 0)]
+        room(order, "gw010")
         for unit in order[0:4]:
             first_layer(*unit)
         hb = [activate(2, 0), activate(2, 1)]
-        for unit in order[4:6]:
-            first_layer(*unit)
+        first_layer(3, 1, 1)
         for b in range(2):
-            first_layer(3, 1, 1, (b,))
+            first_layer(3, 1, 0, (b,))
             hb.append(activate(3, b))
         both = quantise(hq01[:], "01")
         early = [(e, (both[0][:, e * C : (e + 1) * C], both[1][:, e * C : (e + 1) * C])) for e in range(2)]
-        deal_words(2, 2, on_vector, "xw1")
-        turn(hb[0:2], hq[2], 6, on_vector)
-        hq3 = [sb([P, H], BF16, f"hq3_{b}")[:] for b in range(2)]
+        hq2 = sb([P, 2 * H], BF16, "hq2")
+        turn(2, hb[0:2], hq2[:], 0, on_vector)
+        hq3 = [sb([P, H], BF16, f"hq3_{b}") for b in range(2)]
         for b in range(2):
-            turn([hb[2 + b]], hq3[b], (7, 4)[b], on_scalar)
-        late = [(2, quantise(hq[2], "2")), (3, quantise(hq3[0], "3a")), (3, quantise(hq3[1], "3b"))]
-
-        def second_layer(start, parts, banks, copiers):
-            for t in range(4):
-                yp = bank(f"yp{start}_{t}", banks[t], [P, T])
-                done = 0
-                for e, operand in parts:
-                    width = operand[0].shape[1]
-                    second_product(yp[:, done : done + width], e, t, operand)
-                    done = done + width
-                copiers[t](y[t][:, start : start + T], yp[:])
-
-        second_layer(0, early, (0, 1, 5, 6), (on_vector, on_scalar, on_vector, on_scalar))
-        second_layer(T, late, (2, 3, 7, 4), (on_vector, on_scalar, on_vector, on_scalar))
+            turn(f"3{b}", [hb[2 + b]], hq3[b][:], 1 + b, on_scalar)
+        late = [(2, quantise(hq2[:], "2")), (3, quantise(hq3[0][:], "3a")), (3, quantise(hq3[1][:], "3b"))]
+        second_layer(0, early, (3, 4, 5, 6), (on_vector, on_vector, on_scalar, on_scalar))
+        second_layer(PAIR, late, (7, 0, 1, 2), (on_vector, on_scalar, on_vector, on_scalar))
 
         out_rows = out_0.rearrange("(p t) c -> p t c", t=4)
         out_codes = sb([P, T], U32, "out_codes")

@@ -171,8 +171,8 @@ def tile_moe_duo_gelu_kernel(
         second = {}
         second_scales = {}
 
-        def deal_words(e0, count, copier):
-            words = sb([P, count, 1024], U8, f"w2w{e0}", "hb1_1")
+        def deal_words(e0, count, copier, tag):
+            words = sb([P, count, 1024], U8, f"w2w{e0}", tag)
             copier(
                 words[:].bitcast(U16).rearrange("p e (t c i) -> p e c t i", t=4, i=8),
                 w2w[:, e0 : e0 + count, :].bitcast(U16).rearrange("p e (c i t) -> p e c t i", t=4, i=8),
@@ -220,7 +220,8 @@ def tile_moe_duo_gelu_kernel(
         first_layer(1, 0, 0)
         gather_scales(1, 0)
         move_scales(moved_early[:], direct_early[:])
-        load_words(0, 1, (0,))
+        load_words(0, 1, (0, 1))
+        load_words(1, 1, (0, 1))
         w2w = sb([P, E, 1024], U8, "w2raw")
         nc.sync.dma_start(w2w[:].bitcast(I32), w2_words.rearrange("e s p c -> p (e s) c").bitcast(I32))
         load_planes(w2s, w2_scales)
@@ -228,12 +229,6 @@ def tile_moe_duo_gelu_kernel(
         first_layer(1, 0, 1)
         planes[0, 1, 0] = sb([P, PAIR], U8, "direct_late0", "gw000")[:]
         gather_scales(0, 1)
-        gates = sb([P, 2, T], F32, "gates")
-        nc.sync.dma_start(gates[:], gate.rearrange("r p t -> p r t"))
-        load_words(1, 1, (0,))
-        load_words(1, 1, (1,))
-        load_words(0, 1, (1,))
-        token_lists = [load_list(pos1, "pos1_sb"), load_list(pos2, "pos2_sb")]
         hb = []
         for e in range(2):
             first_layer(e, 1, 0)
@@ -243,11 +238,14 @@ def tile_moe_duo_gelu_kernel(
         turn("0", hb[0:2], hq01[:, 0 : 2 * H], 4, on_scalar)
         for b in range(2):
             turn(f"1{b}", [hb[2 + b]], hq01[:, (2 + b) * H : (3 + b) * H], 5 + b, on_scalar)
-        deal_words(0, E, on_scalar)
+        deal_words(0, 2, on_scalar, "hb1_1")
         planes[1, 1, 0] = sb([P, PAIR], U8, "direct_late1", "gw001")[:]
         gather_scales(1, 1)
         for l in range(2):
             move_scales(planes[l, 1, 1], planes[l, 1, 0])
+        gates = sb([P, 2, T], F32, "gates")
+        nc.sync.dma_start(gates[:], gate.rearrange("r p t -> p r t"))
+        token_lists = [load_list(pos1, "pos1_sb"), load_list(pos2, "pos2_sb")]
         room([(2, 0, 0), (2, 0, 1)], "gw101")
         first_layer(2, 0, 0)
         first_layer(2, 0, 1)
@@ -264,6 +262,7 @@ def tile_moe_duo_gelu_kernel(
             hb.append(activate(3, b))
         both = quantise(hq01[:], "01")
         early = [(e, (both[0][:, e * C : (e + 1) * C], both[1][:, e * C : (e + 1) * C])) for e in range(2)]
+        deal_words(2, 2, on_vector, "xw1")
         hq2 = sb([P, 2 * H], BF16, "hq2")
         turn(2, hb[0:2], hq2[:], 0, on_vector)
         hq3 = [sb([P, H], BF16, f"hq3_{b}") for b in range(2)]

@@ -220,11 +220,11 @@ def tile_moe_duo_gelu_kernel(
         first_layer(1, 0, 0)
         gather_scales(1, 0)
         move_scales(moved_early[:], direct_early[:])
+        load_planes(w2s, w2_scales)
         load_words(0, 1, (0, 1))
         load_words(1, 1, (0, 1))
         w2w = sb([P, E, 1024], U8, "w2raw")
         nc.sync.dma_start(w2w[:].bitcast(I32), w2_words.rearrange("e s p c -> p (e s) c").bitcast(I32))
-        load_planes(w2s, w2_scales)
         first_layer(0, 0, 1)
         first_layer(1, 0, 1)
         planes[0, 1, 0] = sb([P, PAIR], U8, "direct_late0", "gw000")[:]

@@ -265,12 +265,12 @@ def tile_moe_duo_gelu_kernel(
         deal_words(2, 2, on_vector, "xw1")
         hq2 = sb([P, 2 * H], BF16, "hq2")
         turn(2, hb[0:2], hq2[:], 0, on_vector)
-        hq3 = [sb([P, H], BF16, f"hq3_{b}") for b in range(2)]
+        hq3 = sb([P, 2 * H], BF16, "hq3")
         for b in range(2):
-            turn(f"3{b}", [hb[2 + b]], hq3[b][:], 1 + b, on_scalar)
-        late = [(2, quantise(hq2[:], "2")), (3, quantise(hq3[0][:], "3a")), (3, quantise(hq3[1][:], "3b"))]
-        second_layer(0, early, (3, 4, 5, 6), (on_vector, on_vector, on_scalar, on_scalar))
-        second_layer(PAIR, late, (7, 0, 1, 2), (on_vector, on_scalar, on_vector, on_scalar))
+            turn(f"3{b}", [hb[2 + b]], hq3[:, b * H : (b + 1) * H], 1 + b, on_scalar)
+        late = [(2, quantise(hq2[:], "2")), (3, quantise(hq3[:], "3"))]
+        second_layer(0, early, (3, 4, 6, 1), (on_vector, on_vector, on_scalar, on_scalar))
+        second_layer(PAIR, late, (7, 0, 5, 2), (on_vector, on_scalar, on_vector, on_scalar))
 
         out_rows = out_0.rearrange("(p t) c -> p t c", t=4)
         out_codes = sb([P, T], U32, "out_codes")
@@ -313,30 +313,24 @@ def tile_moe_duo_gelu_kernel(
         rounded = sb([P, 4 * T], BF16, "rounded")
         starts = (0, HALF, HALF + P)
         totals = [sb([P, 4, width], F32, f"total{start}") for start, width in zip(starts, (HALF, P, P))]
-        for t in range(4):
-            pick(0, 1, t)
-        pick(0, 0, 3)
-        for t in range(4):
-            pick(1, 1, t)
-        pick_and_weigh(0, 0)
-        pick_and_weigh(0, 1)
-        weigh(0, 1, 0, 2)
-        pick_and_weigh(0, 2)
-        add_up(totals[0], 0, 0, 2)
-        pick_and_weigh(1, 0)
-        weigh(0, 1, 2, 4)
+        for h in range(2):
+            for t in range(4):
+                pick(h, 1, t)
+            pick(h, 0, 3)
+        for h in range(2):
+            for t in range(3):
+                pick_and_weigh(h, t)
+        weigh(0, 1, 0, 4)
         weigh(0, 0, 3, 4)
-        pick_and_weigh(1, 1)
-        add_up(totals[0], 0, 2, 4)
-        store_and_round(totals[0], 0, nc.scalar.copy)
-        pick_and_weigh(1, 2)
         weigh(1, 1, 0, 2)
-        pick_and_weigh(1, 3)
+        add_up(totals[0], 0, 0, 4)
+        store_and_round(totals[0], 0, nc.scalar.copy)
         weigh(1, 1, 2, 4)
-        hand_on(0, nc.sync)
+        weigh(1, 0, 3, 4)
         add_up(totals[1], starts[1], 0, 4)
         store_and_round(totals[1], starts[1], nc.scalar.copy)
         add_up(totals[2], starts[2], 0, 4)
+        hand_on(0, nc.sync)
         store_and_round(totals[2], starts[2], nc.vector.tensor_copy)
         hand_on(1, nc.scalar)
         scale_rows = out_2[0].bitcast(I32)

@@ -58,16 +58,16 @@ def tile_moe_duo_gelu_kernel(
 
         first = {}
 
-        def load_words(l, pair, passes):
-            tile = sb([P, 2, len(passes), 1024], U8, f"first{l}_{pair}_{passes[0]}")
-            rows = (w1_words, wp_words)[l][2 * pair : 2 * pair + 2, passes[0] : passes[-1] + 1]
+        def load_words(l, experts, passes):
+            count = len(experts) * len(passes)
+            tile = sb([P, count * 1024], U8, f"first{l}_{experts[0]}_{passes[0]}")
+            rows = (w1_words, wp_words)[l][experts[0] : experts[-1] + 1, passes[0] : passes[-1] + 1]
             nc.sync.dma_start(
-                tile[:].rearrange("p e s c -> p (e s) c").bitcast(I32),
-                rows.rearrange("e s p c -> p (e s) c").bitcast(I32),
+                tile[:].bitcast(I32).rearrange("p (a c) -> p a c", a=count),
+                rows.bitcast(I32).rearrange("e s p c -> p (e s) c"),
             )
-            for a in range(2):
-                for s in passes:
-                    first[l, 2 * pair + a, s] = tile[:, a, s - passes[0], :]
+            for a, (e, s) in enumerate((e, s) for e in experts for s in passes):
+                first[l, e, s] = tile[:, a * 1024 : (a + 1) * 1024]
 
         xw = [sb([P, T], I32, f"xw{s}") for s in range(PASSES)]
 
@@ -91,14 +91,14 @@ def tile_moe_duo_gelu_kernel(
         for q in range(4):
             nc.sync.dma_start(xs[:, 0:T].bitcast(I32)[32 * q : 32 * q + 8], x_scales[:, 4 * q : 4 * q + 4, :].bitcast(I32))
         load_tokens(0)
-        load_words(0, 0, (0,))
+        load_words(0, (0, 1), (0,))
         slot_lists[1] = load_list(offs2, "offs2_sb")
         load_planes(first_scales[0], w1_scales)
         load_tokens(1)
         load_planes(first_scales[1], wp_scales)
-        load_words(1, 0, (0,))
-        load_words(0, 0, (1,))
-        load_words(1, 0, (1,))
+        load_words(1, (0, 1), (0,))
+        load_words(0, (0, 1), (1,))
+        load_words(1, (0, 1), (1,))
 
         ident = sb([P, P], F32, "ident")
         make_identity(nc, ident[:])
@@ -119,7 +119,7 @@ def tile_moe_duo_gelu_kernel(
 
         sums = {}
         gathered = {}
-        sum_banks = ((0, 1), (2, 3), (3, 4), (5, 6))
+        sum_banks = ((0, 1), (2, 3), (6, 7), (3, 4))
 
         def room(units, tag=None):
             tile = sb([P, len(units) * C], U32, "gw%d%d%d" % units[0], tag)
@@ -145,7 +145,7 @@ def tile_moe_duo_gelu_kernel(
                     rhs=first[l, e, s].bitcast(FP4X4),
                     rhs_scale=first_scales[l][:, e * PASSES + s, :],
                     start=(s == 0 and l == 0),
-                    stop=(s == 1 and l == 1 - e // 2),
+                    stop=(s == 1 and l == 1),
                 )
 
         def activate(e, b):
@@ -220,45 +220,48 @@ def tile_moe_duo_gelu_kernel(
         first_layer(1, 0, 0)
         gather_scales(1, 0)
         move_scales(moved_early[:], direct_early[:])
+        load_words(0, (2, 3), (0, 1))
         load_planes(w2s, w2_scales)
-        load_words(0, 1, (0, 1))
-        load_words(1, 1, (0, 1))
-        w2w = sb([P, E, 1024], U8, "w2raw")
-        nc.sync.dma_start(w2w[:].bitcast(I32), w2_words.rearrange("e s p c -> p (e s) c").bitcast(I32))
         first_layer(0, 0, 1)
         first_layer(1, 0, 1)
         planes[0, 1, 0] = sb([P, PAIR], U8, "direct_late0", "gw000")[:]
         gather_scales(0, 1)
+        move_scales(planes[0, 1, 1], planes[0, 1, 0])
+        load_words(1, (2,), (0, 1))
+        w2w = sb([P, E, 1024], U8, "w2raw")
+        nc.sync.dma_start(w2w[:].bitcast(I32), w2_words.rearrange("e s p c -> p (e s) c").bitcast(I32))
         hb = []
         for e in range(2):
             first_layer(e, 1, 0)
             first_layer(e, 1, 1)
             hb.extend([activate(e, 0), activate(e, 1)])
         hq01 = sb([P, 4 * H], BF16, "hq01")
-        turn("0", hb[0:2], hq01[:, 0 : 2 * H], 4, on_scalar)
-        for b in range(2):
-            turn(f"1{b}", [hb[2 + b]], hq01[:, (2 + b) * H : (3 + b) * H], 5 + b, on_scalar)
+        room([(2, 0, 0), (2, 1, 0)], "gw001")
+        first_layer(2, 0, 0)
+        first_layer(2, 1, 0)
+        for e in range(2):
+            turn(e, hb[2 * e : 2 * e + 2], hq01[:, 2 * H * e : 2 * H * (e + 1)], 4 + e, on_scalar)
         deal_words(0, 2, on_scalar, "hb1_1")
-        planes[1, 1, 0] = sb([P, PAIR], U8, "direct_late1", "gw001")[:]
+        planes[1, 1, 0] = sb([P, PAIR], U8, "direct_late1", "gw101")[:]
         gather_scales(1, 1)
-        for l in range(2):
-            move_scales(planes[l, 1, 1], planes[l, 1, 0])
+        move_scales(planes[1, 1, 1], planes[1, 1, 0])
+        load_words(1, (3,), (0, 1))
         gates = sb([P, 2, T], F32, "gates")
         nc.sync.dma_start(gates[:], gate.rearrange("r p t -> p r t"))
         token_lists = [load_list(pos1, "pos1_sb"), load_list(pos2, "pos2_sb")]
-        room([(2, 0, 0), (2, 0, 1)], "gw101")
-        first_layer(2, 0, 0)
-        first_layer(2, 0, 1)
+        room([(3, 0, 0), (3, 1, 0)], "gw010")
+        for b in range(2):
+            for s in range(PASSES):
+                first_layer(3, s, 0, (b,))
         for e in range(E):
             deal_scales(e)
-        order = [(3, 0, 0), (3, 0, 1), (2, 1, 1), (2, 1, 0), (3, 1, 1), (3, 1, 0)]
-        room(order, "gw010")
-        for unit in order[0:4]:
-            first_layer(*unit)
+        room([(2, 0, 1), (2, 1, 1), (3, 0, 1), (3, 1, 1)], "hb1_0")
+        first_layer(2, 0, 1)
+        first_layer(2, 1, 1)
         hb = [activate(2, 0), activate(2, 1)]
-        first_layer(3, 1, 1)
+        first_layer(3, 0, 1)
         for b in range(2):
-            first_layer(3, 1, 0, (b,))
+            first_layer(3, 1, 1, (b,))
             hb.append(activate(3, b))
         both = quantise(hq01[:], "01")
         early = [(e, (both[0][:, e * C : (e + 1) * C], both[1][:, e * C : (e + 1) * C])) for e in range(2)]
@@ -269,8 +272,8 @@ def tile_moe_duo_gelu_kernel(
         for b in range(2):
             turn(f"3{b}", [hb[2 + b]], hq3[:, b * H : (b + 1) * H], 1 + b, on_scalar)
         late = [(2, quantise(hq2[:], "2")), (3, quantise(hq3[:], "3"))]
-        second_layer(0, early, (3, 4, 6, 1), (on_vector, on_vector, on_scalar, on_scalar))
-        second_layer(PAIR, late, (7, 0, 5, 2), (on_vector, on_scalar, on_vector, on_scalar))
+        second_layer(0, early, (6, 7, 4, 1), (on_vector, on_vector, on_scalar, on_scalar))
+        second_layer(PAIR, late, (5, 0, 3, 2), (on_vector, on_scalar, on_vector, on_scalar))
 
         out_rows = out_0.rearrange("(p t) c -> p t c", t=4)
         out_codes = sb([P, T], U32, "out_codes")

@@ -38,7 +38,7 @@ def tile_moe_duo_gelu_kernel(
         on_scalar, on_vector = nc.scalar.copy, nc.vector.tensor_copy
 
         def sb(shape, dtype, name, tag=None):
-            return keep.tile(shape, dtype, name=name, tag=tag or name, bufs=1, align_bytes=64)
+            return keep.tile(shape, dtype, name=name, tag=tag or name, bufs=1, align_bytes=256)
 
         def bank(name, which, shape):
             return psum.tile(shape, F32, name=name, tag=f"bank{which}", bufs=1)
@@ -280,32 +280,32 @@ def tile_moe_duo_gelu_kernel(
         out_plane = sb([P, T], U8, "out_plane")
         code_rows = out_1[0].rearrange("p t d -> p (t d)").bitcast(I32)
 
-        picked = [sb([P, 2, 4, HALF], F32, f"picked{h}") for h in range(2)]
-        products = [sb([P, 2, 4, HALF], F32, f"products{h}") for h in range(2)]
+        picked = sb([P, 5, T], F32, "picked")
+        products = sb([P, 2, 4, T], F32, "products")
 
-        def column(h, r, t):
-            return y[t][:].indirect(entries(token_lists[r], h * HALF, HALF))
+        def pick(row, r, t, start, count):
+            column = y[t][:].indirect(entries(token_lists[r], start, count))
+            nc.scalar.activation(picked[:, row, start : start + count], column, COPY)
 
-        def pick(h, r, t):
-            nc.scalar.activation(picked[h][:, r, t, :], column(h, r, t), COPY)
+        def pick_and_weigh(t):
+            nc.vector.tensor_tensor(products[:, 0, t, :], y[t][:].indirect(token_lists[0][:]), gates[:, 0, :], MULT)
 
-        def pick_and_weigh(h, t):
-            nc.vector.tensor_tensor(products[h][:, 0, t, :], column(h, 0, t), gates[:, 0, h * HALF : (h + 1) * HALF], MULT)
+        def weigh(h, t0, t1):
+            cols = slice(h * HALF, (h + 1) * HALF)
+            weights = gates[:, 1:2, cols].to_broadcast([P, t1 - t0, HALF])
+            nc.vector.tensor_tensor(products[:, 1, t0:t1, cols], picked[:, t0:t1, cols], weights, MULT)
 
-        def weigh(h, r, t0, t1):
-            weights = gates[:, r : r + 1, h * HALF : (h + 1) * HALF].to_broadcast([P, t1 - t0, HALF])
-            nc.vector.tensor_tensor(products[h][:, r, t0:t1, :], picked[h][:, r, t0:t1, :], weights, MULT)
+        def add_up(h, t0, t1):
+            cols = slice(h * HALF, (h + 1) * HALF)
+            nc.vector.tensor_tensor(totals[h][:, t0:t1, :], products[:, 0, t0:t1, cols], products[:, 1, t0:t1, cols], ADD)
 
-        def add_up(total, start, t0, t1):
-            h, cols = start // HALF, slice(start % HALF, start % HALF + total.shape[2])
-            nc.vector.tensor_tensor(total[:, t0:t1, :], products[h][:, 0, t0:t1, cols], products[h][:, 1, t0:t1, cols], ADD)
+        def store(h, t0, t1):
+            nc.sync.dma_start(out_rows[:, t0:t1, h * HALF : (h + 1) * HALF], totals[h][:, t0:t1, :])
 
-        def store_and_round(total, start, rounder):
-            width = total.shape[2]
-            nc.sync.dma_start(out_rows[:, :, start : start + width], total[:])
+        def round_off(start, width, rounder):
             rounder(
                 rounded[:, 4 * start : 4 * (start + width)].rearrange("p (c i t) -> p c t i", t=4, i=4),
-                total[:].rearrange("p t (c i) -> p c t i", i=4),
+                totals[start // HALF][:, :, start % HALF : start % HALF + width].rearrange("p t (c i) -> p c t i", i=4),
             )
 
         def hand_on(h, queue):
@@ -314,27 +314,29 @@ def tile_moe_duo_gelu_kernel(
             queue.dma_start(code_rows[:, cols], out_codes[:, cols].bitcast(I32))
 
         rounded = sb([P, 4 * T], BF16, "rounded")
-        starts = (0, HALF, HALF + P)
-        totals = [sb([P, 4, width], F32, f"total{start}") for start, width in zip(starts, (HALF, P, P))]
-        for h in range(2):
-            for t in range(4):
-                pick(h, 1, t)
-            pick(h, 0, 3)
-        for h in range(2):
-            for t in range(3):
-                pick_and_weigh(h, t)
-        weigh(0, 1, 0, 4)
-        weigh(0, 0, 3, 4)
-        weigh(1, 1, 0, 2)
-        add_up(totals[0], 0, 0, 4)
-        store_and_round(totals[0], 0, nc.scalar.copy)
-        weigh(1, 1, 2, 4)
-        weigh(1, 0, 3, 4)
-        add_up(totals[1], starts[1], 0, 4)
-        store_and_round(totals[1], starts[1], nc.scalar.copy)
-        add_up(totals[2], starts[2], 0, 4)
+        totals = [sb([P, 4, HALF], F32, f"total{h}") for h in range(2)]
+        for t in range(4):
+            pick(t, 1, t, 0, HALF)
+        pick(4, 0, 3, 0, T)
+        for t in range(4):
+            pick(t, 1, t, HALF, HALF)
+        for t in range(3):
+            pick_and_weigh(t)
+        weigh(0, 0, 4)
+        nc.vector.tensor_tensor(products[:, 0, 3, :], picked[:, 4, :], gates[:, 0, :], MULT)
+        weigh(1, 0, 1)
+        add_up(0, 0, 4)
+        store(0, 0, 4)
+        round_off(0, HALF, on_scalar)
+        weigh(1, 1, 3)
+        weigh(1, 3, 4)
+        add_up(1, 0, 3)
+        store(1, 0, 3)
+        add_up(1, 3, 4)
+        store(1, 3, 4)
         hand_on(0, nc.sync)
-        store_and_round(totals[2], starts[2], nc.vector.tensor_copy)
+        round_off(HALF, P, on_scalar)
+        round_off(HALF + P, P, on_vector)
         hand_on(1, nc.scalar)
         scale_rows = out_2[0].bitcast(I32)
         for r in range(4):

@@ -91,8 +91,8 @@ def tile_moe_duo_gelu_kernel(
         for q in range(4):
             nc.sync.dma_start(xs[:, 0:T].bitcast(I32)[32 * q : 32 * q + 8], x_scales[:, 4 * q : 4 * q + 4, :].bitcast(I32))
         load_tokens(0)
-        load_words(0, (0, 1), (0,))
         slot_lists[1] = load_list(offs2, "offs2_sb")
+        load_words(0, (0, 1), (0,))
         load_planes(first_scales[0], w1_scales)
         load_tokens(1)
         load_planes(first_scales[1], wp_scales)
@@ -134,6 +134,7 @@ def tile_moe_duo_gelu_kernel(
                 gathered[e, s, l][:, cols],
                 xw[s][:].bitcast(U32).indirect(entries(slot_lists[l], e * C + cols.start, cols.stop - cols.start)),
             )
+            opener = e // 2
             scales = planes[l, e // 2, s][:, (e % 2) * C : (e % 2 + 1) * C]
             for b in blocks:
                 if (e, b) not in sums:
@@ -144,8 +145,8 @@ def tile_moe_duo_gelu_kernel(
                     lhsT_scale=scales[:, b * P : (b + 1) * P],
                     rhs=first[l, e, s].bitcast(FP4X4),
                     rhs_scale=first_scales[l][:, e * PASSES + s, :],
-                    start=(s == 0 and l == 0),
-                    stop=(s == 1 and l == 1),
+                    start=(s == 0 and l == opener),
+                    stop=(s == 1 and l != opener),
                 )
 
         def activate(e, b):
@@ -217,17 +218,17 @@ def tile_moe_duo_gelu_kernel(
 
         gather_scales(0, 0)
         first_layer(0, 0, 0)
-        first_layer(1, 0, 0)
         gather_scales(1, 0)
         move_scales(moved_early[:], direct_early[:])
-        load_words(0, (2, 3), (0, 1))
+        first_layer(1, 0, 0)
+        load_words(1, (2, 3), (0, 1))
         load_planes(w2s, w2_scales)
         first_layer(0, 0, 1)
         first_layer(1, 0, 1)
-        planes[0, 1, 0] = sb([P, PAIR], U8, "direct_late0", "gw000")[:]
-        gather_scales(0, 1)
-        move_scales(planes[0, 1, 1], planes[0, 1, 0])
-        load_words(1, (2,), (0, 1))
+        planes[1, 1, 0] = sb([P, PAIR], U8, "direct_late1")[:]
+        gather_scales(1, 1)
+        move_scales(planes[1, 1, 1], planes[1, 1, 0])
+        load_words(0, (2,), (0, 1))
         w2w = sb([P, E, 1024], U8, "w2raw")
         nc.sync.dma_start(w2w[:].bitcast(I32), w2_words.rearrange("e s p c -> p (e s) c").bitcast(I32))
         hb = []
@@ -236,32 +237,32 @@ def tile_moe_duo_gelu_kernel(
             first_layer(e, 1, 1)
             hb.extend([activate(e, 0), activate(e, 1)])
         hq01 = sb([P, 4 * H], BF16, "hq01")
-        room([(2, 0, 0), (2, 1, 0)], "gw001")
-        first_layer(2, 0, 0)
-        first_layer(2, 1, 0)
+        room([(2, 0, 1), (2, 1, 1)], "gw001")
+        first_layer(2, 0, 1)
+        first_layer(2, 1, 1)
         for e in range(2):
             turn(e, hb[2 * e : 2 * e + 2], hq01[:, 2 * H * e : 2 * H * (e + 1)], 4 + e, on_scalar)
         deal_words(0, 2, on_scalar, "hb1_1")
-        planes[1, 1, 0] = sb([P, PAIR], U8, "direct_late1", "gw101")[:]
-        gather_scales(1, 1)
-        move_scales(planes[1, 1, 1], planes[1, 1, 0])
-        load_words(1, (3,), (0, 1))
+        planes[0, 1, 0] = sb([P, PAIR], U8, "direct_late0", "gw101")[:]
+        gather_scales(0, 1)
+        move_scales(planes[0, 1, 1], planes[0, 1, 0])
+        load_words(0, (3,), (0, 1))
         gates = sb([P, 2, T], F32, "gates")
         nc.sync.dma_start(gates[:], gate.rearrange("r p t -> p r t"))
         token_lists = [load_list(pos1, "pos1_sb"), load_list(pos2, "pos2_sb")]
-        room([(3, 0, 0), (3, 1, 0)], "gw010")
+        room([(3, 0, 1), (3, 1, 1)], "gw010")
         for b in range(2):
             for s in range(PASSES):
-                first_layer(3, s, 0, (b,))
+                first_layer(3, s, 1, (b,))
         for e in range(E):
             deal_scales(e)
-        room([(2, 0, 1), (2, 1, 1), (3, 0, 1), (3, 1, 1)], "hb1_0")
-        first_layer(2, 0, 1)
-        first_layer(2, 1, 1)
+        room([(2, 0, 0), (2, 1, 0), (3, 0, 0), (3, 1, 0)], "hb1_0")
+        first_layer(2, 0, 0)
+        first_layer(2, 1, 0)
         hb = [activate(2, 0), activate(2, 1)]
-        first_layer(3, 0, 1)
+        first_layer(3, 0, 0)
         for b in range(2):
-            first_layer(3, 1, 1, (b,))
+            first_layer(3, 1, 0, (b,))
             hb.append(activate(3, b))
         both = quantise(hq01[:], "01")
         early = [(e, (both[0][:, e * C : (e + 1) * C], both[1][:, e * C : (e + 1) * C])) for e in range(2)]

@@ -81,7 +81,7 @@ def tile_moe_duo_gelu_kernel(
         moved_late = [sb([P, PAIR], U8, f"moved_late{l}") for l in range(2)]
         nc.gpsimd.memset(xs[:].bitcast(I32), 0)
         nc.vector.memset(first_scales[0][:].bitcast(I32), 0)
-        nc.gpsimd.memset(first_scales[1][:].bitcast(I32), 0)
+        nc.vector.memset(first_scales[1][:].bitcast(I32), 0)
         nc.vector.memset(moved_early[:].bitcast(I32), 0)
         for l in range(2):
             nc.vector.memset(moved_late[l][:].bitcast(I32), 0)

@@ -79,7 +79,8 @@ def tile_moe_duo_gelu_kernel(
         w2s = sb([P, E, N], U8, "w2s")
         moved_early = sb([P, 2 * PAIR], U8, "moved_early")
         moved_late = [sb([P, PAIR], U8, f"moved_late{l}") for l in range(2)]
-        nc.gpsimd.memset(xs[:].bitcast(I32), 0)
+        for half in range(2):
+            nc.gpsimd.memset(xs[:, half * T : (half + 1) * T].bitcast(I32), 0)
         nc.vector.memset(first_scales[0][:].bitcast(I32), 0)
         nc.vector.memset(first_scales[1][:].bitcast(I32), 0)
         nc.vector.memset(moved_early[:].bitcast(I32), 0)
@@ -181,8 +182,8 @@ def tile_moe_duo_gelu_kernel(
             for a in range(count):
                 second[e0 + a] = words[:, a, :]
 
-        def deal_scales(e):
-            scales = sb([P, N], U8, f"w2p{e}")
+        def deal_scales(e, tag=None):
+            scales = sb([P, N], U8, f"w2p{e}", tag)
             nc.gpsimd.tensor_copy(
                 scales[:].rearrange("p (t c i) -> p c t i", t=4, i=16),
                 w2s[:, e, :].rearrange("p (c i t) -> p c t i", t=4, i=16),
@@ -254,7 +255,7 @@ def tile_moe_duo_gelu_kernel(
         for b in range(2):
             for s in range(PASSES):
                 first_layer(3, s, 1, (b,))
-        for e in range(E):
+        for e in range(2):
             deal_scales(e)
         room([(2, 0, 0), (2, 1, 0), (3, 0, 0), (3, 1, 0)], "hb1_0")
         first_layer(2, 0, 0)
@@ -266,6 +267,8 @@ def tile_moe_duo_gelu_kernel(
             hb.append(activate(3, b))
         both = quantise(hq01[:], "01")
         early = [(e, (both[0][:, e * C : (e + 1) * C], both[1][:, e * C : (e + 1) * C])) for e in range(2)]
+        deal_scales(2, "hq01")
+        deal_scales(3, "xw0")
         deal_words(2, 2, on_vector, "xw1")
         hq2 = sb([P, 2 * H], BF16, "hq2")
         turn(2, hb[0:2], hq2[:], 0, on_vector)

from contextlib import ExitStack

import concourse.mybir as mybir
from concourse.masks import make_identity

K, T, E, C, H, N = 1024, 512, 4, 256, 512, 512
S = E * C
FLOPS = 2 * S * (2 * K * H + H * N)

F32 = mybir.dt.float32
BF16 = mybir.dt.bfloat16
I32 = mybir.dt.int32
U32 = mybir.dt.uint32
U16 = mybir.dt.uint16
U8 = mybir.dt.uint8
FP8X4 = mybir.dt.float8_e4m3fn_x4
FP4X4 = mybir.dt.float4_e2m1fn_x4
GELU = mybir.ActivationFunctionType.Gelu_apprx_tanh
COPY = mybir.ActivationFunctionType.Copy
MULT = mybir.AluOpType.mult
ADD = mybir.AluOpType.add

P = 128
PASSES = K // 512
STRIPE = 16
HALF = T // 2
PAIR = 2 * C


def tile_moe_duo_gelu_kernel(
    tc, x_words, x_scales, w1_words, w1_scales, wp_words, wp_scales, w2_words, w2_scales,
    gate, offs, pos1, pos2, offs2, out_0, out_1, out_2,
):
    nc = tc.nc
    with ExitStack() as ctx:
        keep = ctx.enter_context(tc.tile_pool(name="keep", bufs=1))
        psum = ctx.enter_context(tc.psum_pool(name="psum", bufs=1))
        on_scalar, on_vector = nc.scalar.copy, nc.vector.tensor_copy

        def sb(shape, dtype, name, tag=None):
            return keep.tile(shape, dtype, name=name, tag=tag or name, bufs=1, align_bytes=256)

        def bank(name, which, shape):
            return psum.tile(shape, F32, name=name, tag=f"bank{which}", bufs=1)

        def load_list(src, name):
            tile = keep.tile(list(src.shape), U16, name=name)
            nc.sync.dma_start(tile[:], src)
            return tile

        def entries(lst, start, count):
            return lst[:, start // STRIPE : (start + count) // STRIPE]

        def load_planes(plane, scales):
            rows = scales.rearrange("e s b c -> b (e s) c").bitcast(I32)
            for r in range(4):
                nc.sync.dma_start(plane[r:P:32].bitcast(I32), rows[r:16:4])

        first = {}

        def load_words(l, experts, passes):
            count = len(experts) * len(passes)
            tile = sb([P, count * 1024], U8, f"first{l}_{experts[0]}_{passes[0]}")
            rows = (w1_words, wp_words)[l][experts[0] : experts[-1] + 1, passes[0] : passes[-1] + 1]
            nc.sync.dma_start(
                tile[:].bitcast(I32).rearrange("p (a c) -> p a c", a=count),
                rows.bitcast(I32).rearrange("e s p c -> p (e s) c"),
            )
            for a, (e, s) in enumerate((e, s) for e in experts for s in passes):
                first[l, e, s] = tile[:, a * 1024 : (a + 1) * 1024]

        xw = [sb([P, T], I32, f"xw{s}") for s in range(PASSES)]

        def load_tokens(s):
            nc.sync.dma_start(xw[s][:], x_words[s].rearrange("p t d -> p (t d)").bitcast(I32))

        xs = sb([P, 2 * T], U8, "xs")
        first_scales = [sb([P, E * PASSES, H], U8, f"first_scales{l}") for l in range(2)]
        w2s = sb([P, E, N], U8, "w2s")
        moved_early = sb([P, 2 * PAIR], U8, "moved_early")
        moved_late = [sb([P, PAIR], U8, f"moved_late{l}") for l in range(2)]
        for half in range(2):
            nc.gpsimd.memset(xs[:, half * T : (half + 1) * T].bitcast(I32), 0)
        nc.vector.memset(first_scales[0][:].bitcast(I32), 0)
        nc.vector.memset(first_scales[1][:].bitcast(I32), 0)
        nc.vector.memset(moved_early[:].bitcast(I32), 0)
        for l in range(2):
            nc.vector.memset(moved_late[l][:].bitcast(I32), 0)
        nc.vector.memset(w2s[:].bitcast(I32), 0)

        slot_lists = {0: load_list(offs, "offs_sb")}
        for q in range(4):
            nc.sync.dma_start(xs[:, 0:T].bitcast(I32)[32 * q : 32 * q + 8], x_scales[:, 4 * q : 4 * q + 4, :].bitcast(I32))
        load_tokens(0)
        slot_lists[1] = load_list(offs2, "offs2_sb")
        load_words(0, (0, 1), (0,))
        load_planes(first_scales[0], w1_scales)
        load_tokens(1)
        load_planes(first_scales[1], wp_scales)
        load_words(1, (0, 1), (0,))
        load_words(0, (0, 1), (1,))
        load_words(1, (0, 1), (1,))

        ident = sb([P, P], F32, "ident")
        make_identity(nc, ident[:])

        direct_early = sb([P, 2 * PAIR], U8, "direct_early")
        planes = {}
        for l in range(2):
            planes[l, 0, 0] = direct_early[:, l * PAIR : (l + 1) * PAIR]
            planes[l, 0, 1] = moved_early[:, l * PAIR : (l + 1) * PAIR]
            planes[l, 1, 1] = moved_late[l][:]

        def gather_scales(l, pair):
            nc.vector.tensor_copy(planes[l, pair, 0], xs[:].indirect(entries(slot_lists[l], pair * PAIR, PAIR)))

        def move_scales(dst, src):
            for p0, rows in ((0, 64), (64, 4), (96, 4)):
                nc.sync.dma_start(dst.bitcast(I32)[p0 : p0 + rows], src.bitcast(I32)[p0 + 4 : p0 + 4 + rows])

        sums = {}
        gathered = {}
        sum_banks = ((0, 1), (2, 3), (6, 7), (3, 4))

        def room(units, tag=None):
            tile = sb([P, len(units) * C], U32, "gw%d%d%d" % units[0], tag)
            for a, unit in enumerate(units):
                gathered[unit] = tile[:, a * C : (a + 1) * C]

        def first_layer(e, s, l, blocks=(0, 1)):
            if (e, s, l) not in gathered:
                room([(e, s, l)])
            cols = slice(blocks[0] * P, (blocks[-1] + 1) * P)
            nc.vector.tensor_copy(
                gathered[e, s, l][:, cols],
                xw[s][:].bitcast(U32).indirect(entries(slot_lists[l], e * C + cols.start, cols.stop - cols.start)),
            )
            opener = e // 2
            scales = planes[l, e // 2, s][:, (e % 2) * C : (e % 2 + 1) * C]
            for b in blocks:
                if (e, b) not in sums:
                    sums[e, b] = bank(f"sum{e}_{b}", sum_banks[e][b], [P, H])
                nc.tensor.matmul_mx(
                    sums[e, b][:],
                    lhsT=gathered[e, s, l][:, b * P : (b + 1) * P].bitcast(FP8X4),
                    lhsT_scale=scales[:, b * P : (b + 1) * P],
                    rhs=first[l, e, s].bitcast(FP4X4),
                    rhs_scale=first_scales[l][:, e * PASSES + s, :],
                    start=(s == 0 and l == opener),
                    stop=(s == 1 and l != opener),
                )

        def activate(e, b):
            hb = sb([P, H], BF16, f"hb{e}_{b}")
            nc.scalar.activation(
                hb[:].rearrange("s (u p d) -> s u p d", u=2, d=2),
                sums[e, b][:].rearrange("s (p u d) -> s u p d", u=2, d=2),
                GELU,
            )
            return hb

        def turn(name, tiles, hq, which, copier):
            turned = bank(f"turned{name}", which, [P, len(tiles), 2, P])
            for a, hb in reversed(list(enumerate(tiles))):
                pairs = hb[:].bitcast(F32)
                for u in range(2):
                    nc.tensor.transpose(turned[:, a, u, :], pairs[:, u * P : (u + 1) * P], ident[:])
            copier(
                hq.bitcast(F32).rearrange("p (b s u) -> p b s u", b=len(tiles), u=2),
                turned[:].rearrange("p b u s -> p b s u"),
            )

        second = {}
        second_scales = {}

        def deal_words(e0, count, copier, tag):
            words = sb([P, count, 1024], U8, f"w2w{e0}", tag)
            copier(
                words[:].bitcast(U16).rearrange("p e (t c i) -> p e c t i", t=4, i=8),
                w2w[:, e0 : e0 + count, :].bitcast(U16).rearrange("p e (c i t) -> p e c t i", t=4, i=8),
            )
            for a in range(count):
                second[e0 + a] = words[:, a, :]

        def deal_scales(e, tag=None):
            scales = sb([P, N], U8, f"w2p{e}", tag)
            nc.gpsimd.tensor_copy(
                scales[:].rearrange("p (t c i) -> p c t i", t=4, i=16),
                w2s[:, e, :].rearrange("p (c i t) -> p c t i", t=4, i=16),
            )
            second_scales[e] = scales[:]

        def quantise(hq, name):
            width = hq.shape[1] // 4
            codes = sb([P, width], U32, f"hc{name}")
            plane = sb([P, width], U8, f"hs{name}")
            nc.vector.quantize_mx(codes[:].bitcast(FP8X4), plane[:], hq)
            return codes[:], plane[:]

        y = [sb([P, S], F32, f"y{t}") for t in range(4)]

        def second_layer(start, parts, banks, copiers):
            for t in range(4):
                yp = bank(f"yp{start}_{t}", banks[t], [P, PAIR])
                done = 0
                for e, (codes, plane) in parts:
                    width = codes.shape[1]
                    nc.tensor.matmul_mx(
                        yp[:, done : done + width],
                        lhsT=second[e][:, 2 * P * t : 2 * P * (t + 1)].bitcast(FP4X4),
                        lhsT_scale=second_scales[e][:, P * t : P * (t + 1)],
                        rhs=codes.bitcast(FP8X4),
                        rhs_scale=plane,
                        start=True,
                        stop=True,
                    )
                    done = done + width
                copiers[t](y[t][:, start : start + PAIR], yp[:])

        gather_scales(0, 0)
        first_layer(0, 0, 0)
        gather_scales(1, 0)
        move_scales(moved_early[:], direct_early[:])
        first_layer(1, 0, 0)
        load_words(1, (2, 3), (0, 1))
        load_planes(w2s, w2_scales)
        first_layer(0, 0, 1)
        first_layer(1, 0, 1)
        planes[1, 1, 0] = sb([P, PAIR], U8, "direct_late1")[:]
        gather_scales(1, 1)
        move_scales(planes[1, 1, 1], planes[1, 1, 0])
        load_words(0, (2,), (0, 1))
        w2w = sb([P, E, 1024], U8, "w2raw")
        nc.sync.dma_start(w2w[:].bitcast(I32), w2_words.rearrange("e s p c -> p (e s) c").bitcast(I32))
        hb = []
        for e in range(2):
            first_layer(e, 1, 0)
            first_layer(e, 1, 1)
            hb.extend([activate(e, 0), activate(e, 1)])
        hq01 = sb([P, 4 * H], BF16, "hq01")
        room([(2, 0, 1), (2, 1, 1)], "gw001")
        first_layer(2, 0, 1)
        first_layer(2, 1, 1)
        for e in range(2):
            turn(e, hb[2 * e : 2 * e + 2], hq01[:, 2 * H * e : 2 * H * (e + 1)], 4 + e, on_scalar)
        deal_words(0, 2, on_scalar, "hb1_1")
        planes[0, 1, 0] = sb([P, PAIR], U8, "direct_late0", "gw101")[:]
        gather_scales(0, 1)
        move_scales(planes[0, 1, 1], planes[0, 1, 0])
        load_words(0, (3,), (0, 1))
        gates = sb([P, 2, T], F32, "gates")
        nc.sync.dma_start(gates[:], gate.rearrange("r p t -> p r t"))
        token_lists = [load_list(pos1, "pos1_sb"), load_list(pos2, "pos2_sb")]
        room([(3, 0, 1), (3, 1, 1)], "gw010")
        for b in range(2):
            for s in range(PASSES):
                first_layer(3, s, 1, (b,))
        for e in range(2):
            deal_scales(e)
        room([(2, 0, 0), (2, 1, 0), (3, 0, 0), (3, 1, 0)], "hb1_0")
        first_layer(2, 0, 0)
        first_layer(2, 1, 0)
        hb = [activate(2, 0), activate(2, 1)]
        first_layer(3, 0, 0)
        for b in range(2):
            first_layer(3, 1, 0, (b,))
            hb.append(activate(3, b))
        both = quantise(hq01[:], "01")
        early = [(e, (both[0][:, e * C : (e + 1) * C], both[1][:, e * C : (e + 1) * C])) for e in range(2)]
        deal_scales(2, "hq01")
        deal_scales(3, "xw0")
        deal_words(2, 2, on_vector, "xw1")
        hq2 = sb([P, 2 * H], BF16, "hq2")
        turn(2, hb[0:2], hq2[:], 0, on_vector)
        hq3 = sb([P, 2 * H], BF16, "hq3")
        for b in range(2):
            turn(f"3{b}", [hb[2 + b]], hq3[:, b * H : (b + 1) * H], 1 + b, on_scalar)
        late = [(2, quantise(hq2[:], "2")), (3, quantise(hq3[:], "3"))]
        second_layer(0, early, (6, 7, 4, 1), (on_vector, on_vector, on_scalar, on_scalar))
        second_layer(PAIR, late, (5, 0, 3, 2), (on_vector, on_scalar, on_vector, on_scalar))

        out_rows = out_0.rearrange("(p t) c -> p t c", t=4)
        out_codes = sb([P, T], U32, "out_codes")
        out_plane = sb([P, T], U8, "out_plane")
        code_rows = out_1[0].rearrange("p t d -> p (t d)").bitcast(I32)

        picked = sb([P, 5, T], F32, "picked")
        products = sb([P, 2, 4, T], F32, "products")

        def pick(row, r, t, start, count):
            column = y[t][:].indirect(entries(token_lists[r], start, count))
            nc.scalar.activation(picked[:, row, start : start + count], column, COPY)

        def pick_and_weigh(t):
            nc.vector.tensor_tensor(products[:, 0, t, :], y[t][:].indirect(token_lists[0][:]), gates[:, 0, :], MULT)

        def weigh(h, t0, t1):
            cols = slice(h * HALF, (h + 1) * HALF)
            weights = gates[:, 1:2, cols].to_broadcast([P, t1 - t0, HALF])
            nc.vector.tensor_tensor(products[:, 1, t0:t1, cols], picked[:, t0:t1, cols], weights, MULT)

        def add_up(h, t0, t1):
            cols = slice(h * HALF, (h + 1) * HALF)
            nc.vector.tensor_tensor(totals[h][:, t0:t1, :], products[:, 0, t0:t1, cols], products[:, 1, t0:t1, cols], ADD)

        def store(h, t0, t1):
            nc.sync.dma_start(out_rows[:, t0:t1, h * HALF : (h + 1) * HALF], totals[h][:, t0:t1, :])

        def round_off(start, width, rounder):
            rounder(
                rounded[:, 4 * start : 4 * (start + width)].rearrange("p (c i t) -> p c t i", t=4, i=4),
                totals[start // HALF][:, :, start % HALF : start % HALF + width].rearrange("p t (c i) -> p c t i", i=4),
            )

        def hand_on(h, queue):
            cols = slice(h * HALF, (h + 1) * HALF)
            nc.vector.quantize_mx(out_codes[:, cols].bitcast(FP8X4), out_plane[:, cols], rounded[:, 4 * cols.start : 4 * cols.stop])
            queue.dma_start(code_rows[:, cols], out_codes[:, cols].bitcast(I32))

        rounded = sb([P, 4 * T], BF16, "rounded")
        totals = [sb([P, 4, HALF], F32, f"total{h}") for h in range(2)]
        for t in range(4):
            pick(t, 1, t, 0, HALF)
        pick(4, 0, 3, 0, T)
        for t in range(4):
            pick(t, 1, t, HALF, HALF)
        for t in range(3):
            pick_and_weigh(t)
        weigh(0, 0, 4)
        nc.vector.tensor_tensor(products[:, 0, 3, :], picked[:, 4, :], gates[:, 0, :], MULT)
        weigh(1, 0, 1)
        add_up(0, 0, 4)
        store(0, 0, 4)
        round_off(0, HALF, on_scalar)
        weigh(1, 1, 3)
        weigh(1, 3, 4)
        add_up(1, 0, 3)
        store(1, 0, 3)
        add_up(1, 3, 4)
        store(1, 3, 4)
        hand_on(0, nc.sync)
        round_off(HALF, P, on_scalar)
        round_off(HALF + P, P, on_vector)
        hand_on(1, nc.scalar)
        scale_rows = out_2[0].bitcast(I32)
        for r in range(4):
            queue = nc.sync if r % 2 else nc.scalar
            queue.dma_start(scale_rows[r:16:4], out_plane[r:P:32].bitcast(I32))
